import numpy as np
import ml_dtypes


def mxq(x, axis, fmt="e4m3"):
    dtype, down = {"e4m3": (ml_dtypes.float8_e4m3fn, 7), "e5m2": (ml_dtypes.float8_e5m2, 14)}[fmt]
    v = np.moveaxis(np.asarray(x, np.float32).astype(ml_dtypes.bfloat16).astype(np.float64), axis, -1)
    blocks = v.reshape(v.shape[:-1] + (-1, 32))
    amax = np.abs(blocks).max(-1, keepdims=True)
    byte = np.maximum(np.where(amax > 0, np.frexp(amax)[1] - 1 + 127, 0) - down, 1)
    scale = np.exp2(byte - 127.0)
    codes = (blocks / scale).astype(np.float32).astype(dtype).astype(np.float64)
    return np.moveaxis((codes * scale).reshape(v.shape), -1, axis)


WIDE = False


def mx_kscale(k):
    if not WIDE:
        return np.ones(k)
    levels = np.array([10, -10, 5, -5, 0])
    if k % 512:
        return np.exp2(np.random.permutation(np.resize(levels, k // 32))).repeat(32)
    a = np.empty((k // 512, 16))
    for p in range(k // 512):
        a[p, :8] = np.random.permutation(np.resize(levels, 8))
        for g in range(8):
            far = levels[np.abs(levels - a[p, g]) >= 10]
            a[p, g + 8] = far[np.random.randint(len(far))]
    return np.exp2(a.ravel()).repeat(32)


def f64(x):
    return np.asarray(x).astype(np.float64)


def striped(idx):
    return np.tile(idx.reshape(-1, 16).T, (8, 1)).astype(np.uint16)


def unstriped(offs):
    return offs[:16].T.reshape(-1).astype(np.int64)


E2M1 = np.array([0.0, 0.5, 1.0, 1.5, 2.0, 3.0, 4.0, 6.0, -0.0, -0.5, -1.0, -1.5, -2.0, -3.0, -4.0, -6.0])


def pack_weight(w, fmt):
    k, n = w.shape
    w = f64(np.asarray(w, np.float32).astype(ml_dtypes.bfloat16)).reshape(k // 32, 32, n)
    amax = np.abs(w).max(1)
    if fmt == "e4m3":
        byte = np.frexp(amax)[1] - 1 + 127 - 7
    else:
        mant, ex = np.frexp(amax / 6.0)
        byte = np.where(mant > 0.5, ex, ex - 1) + 127
    byte = np.clip(np.where(amax > 0, byte, 1), 1, 254)
    scaled = (w * np.exp2(127.0 - byte)[:, None, :]).reshape(k, n).astype(np.float32)
    by_word = np.ascontiguousarray(scaled.reshape(k // 512, 128, 4, n).transpose(0, 1, 3, 2))
    if fmt == "e4m3":
        words = by_word.astype(ml_dtypes.float8_e4m3fn).view(np.uint8)
    else:
        c = by_word.astype(ml_dtypes.float4_e2m1fn).view(np.uint8) & 0xF
        words = (c[..., 0::2] | (c[..., 1::2] << 4)).reshape(k // 512, 128, 2 * n)
    return np.ascontiguousarray(words), np.ascontiguousarray(byte.astype(np.uint8).reshape(k // 512, 16, n))


def unpack_weight(words, scales, fmt):
    g, _, n = scales.shape
    words = np.ascontiguousarray(words).reshape(g, 128, n, -1)
    if fmt == "e4m3":
        vals = words.view(ml_dtypes.float8_e4m3fn).astype(np.float64)
    else:
        nib = np.empty((g, 128, n, 4), np.uint8)
        nib[..., 0::2] = words & 0xF
        nib[..., 1::2] = words >> 4
        vals = E2M1[nib]
    vals = vals * np.repeat(np.exp2(scales.astype(np.float64) - 127.0), 8, axis=1)[..., None]
    return vals.transpose(0, 1, 3, 2).reshape(g * 512, n)


def gelu(v):
    return 0.5 * v * (1.0 + np.tanh(np.sqrt(2.0 / np.pi) * (v + 0.044715 * v**3)))


K, H, N, T, S, P = 1024, 1024, 512, 4096, 1024, 512

def setup_inputs():
    n = np.random.standard_normal
    s = mx_kscale(K)[:, None]
    u = mx_kscale(H)[:, None]
    tab_words, tab_scales = pack_weight(n((K, T)) * s, "e4m3")
    w4_words, w4_scales = pack_weight(n((K, H)) / np.sqrt(K) / s, "e2m1")
    return {
        "tab_words": tab_words, "tab_scales": tab_scales,
        "offs": striped(np.random.permutation(T)[:S]),
        "w4_words": w4_words, "w4_scales": w4_scales,
        "pos1": striped(np.random.permutation(S)[:P]),
        "pos2": striped(np.random.permutation(S)[:P]),
        "pos3": striped(np.random.permutation(S)[:P]),
        "gain": (np.exp(0.3 * n(H)) * u[:, 0]).astype(np.float32),
        "wl": (n((H, N)) / np.sqrt(H) / u).astype(np.float32),
        "cut": (0.5 * n(N)).astype(np.float32),
    }

def reference(tab_words, tab_scales, offs, w4_words, w4_scales, pos1, pos2, pos3, gain, wl, cut):
    v = unpack_weight(tab_words, tab_scales, "e4m3")[:, unstriped(offs)]
    w4 = unpack_weight(w4_words, w4_scales, "e2m1")
    h = w4.T @ v
    hum = h[:, unstriped(pos1)]
    prime = h[:, unstriped(pos2)]
    tierce = h[:, unstriped(pos3)]
    d = np.square(hum) - prime * tierce
    z = f64(gain)[:, None] * d
    y = mxq(f64(wl), 0, "e4m3").T @ mxq(z, 0, "e4m3")
    return y + f64(cut)[:, None]

@@ -1,0 +1,277 @@
+from contextlib import ExitStack
+
+import concourse.mybir as mybir
+from concourse.masks import make_identity
+
+K, H, N, T, S, M = 1024, 1024, 512, 4096, 1024, 512
+FLOPS = 2 * K * H * S + 2 * H * N * M
+
+F32 = mybir.dt.float32
+BF16 = mybir.dt.bfloat16
+I32 = mybir.dt.int32
+U32 = mybir.dt.uint32
+U16 = mybir.dt.uint16
+U8 = mybir.dt.uint8
+FP8X4 = mybir.dt.float8_e4m3fn_x4
+FP4X4 = mybir.dt.float4_e2m1fn_x4
+ACT = mybir.ActivationFunctionType
+ALU = mybir.AluOpType
+
+P = 128
+PACK = 4
+BANK = 512
+LAST_CHUNKS = ((0, 256), (256, 128), (384, 128))
+
+
+def tile_list_bell_discriminant_kernel(
+    tc, tab_words, tab_scales, offs, w4_words, w4_scales, pos1, pos2, pos3, gain, wl, cut, out
+):
+    nc = tc.nc
+    with ExitStack() as ctx:
+        lists = ctx.enter_context(tc.tile_pool(name="lists", bufs=1))
+        keep = ctx.enter_context(tc.tile_pool(name="keep", bufs=1))
+        work = ctx.enter_context(tc.tile_pool(name="work", bufs=3))
+        psum = ctx.enter_context(tc.psum_pool(name="psum", bufs=8))
+
+        def held(shape, dtype, name):
+            return keep.tile(shape, dtype, name=name, align_bytes=64)
+
+        offs_sb = lists.tile([P, S // 16], U16, name="offs_sb")
+        pos_sb = [lists.tile([P, M // 16], U16, name="pos_sb%d" % i) for i in range(3)]
+
+        tab_sc = held([P, T], U8, "tab_sc")
+        picked_sc = held([P, S], U8, "picked_sc")
+        w4_sc_raw = held([32, H // 4], I32, "w4_sc_raw")
+        planes = [held([P, S + H], U8, "planes%d" % a) for a in range(2)]
+        w4_raw = {}
+        w4_wd = [held([P, 2, 1024], U8, "w4_wd%d" % b) for b in range(2)]
+        tab_wd = [held([P, T], I32, "big%d" % a) for a in range(2)]
+        v_wd = [[held([P, BANK], U32, "v_wd%d%d" % (a, u)) for u in range(2)] for a in range(2)]
+        vec_rows = held([P, P], F32, "vec_rows")
+        ident = held([P, P], F32, "ident")
+        vec_cols = held([P, 12], F32, "vec_cols")
+        gain_sb = vec_cols[:, 0:8]
+        cut_sb = vec_cols[:, 8:12]
+        wl_bf = [held([P, N, PACK], BF16, "wl_bf%d" % b) for b in range(2)]
+        wl_wd = [held([P, N], U32, "wl_wd%d" % b) for b in range(2)]
+        wl_sc = [held([P, N], U8, "wl_sc%d" % b) for b in range(2)]
+        h_sb = [held([P, S], F32, "h_sb%d" % s) for s in range(8)]
+
+        nc.vector.memset(tab_sc[32:64, :].bitcast(I32), 0)
+        nc.vector.memset(tab_sc[64:128, :].bitcast(I32), 0)
+        for a in range(2):
+            nc.vector.memset(planes[a][:].bitcast(I32), 0)
+        sc_rows = planes[0][0:32, :].bitcast(I32)
+        nc.gpsimd.memset(vec_rows[:], 0.0)
+        make_identity(nc, ident[:])
+
+        def load_w4(b):
+            w4_raw[b] = held([P, 2, 256], I32, "big0" if b else "w4_raw")
+            nc.sync.dma_start(
+                out=w4_raw[b][:],
+                in_=w4_words[:, :, 1024 * b : 1024 * (b + 1)].bitcast(I32).rearrange("a p c -> p a c"),
+            )
+
+        def load_tab(a):
+            nc.sync.dma_start(out=tab_wd[a][:], in_=tab_words[a].rearrange("p t i -> p (t i)").bitcast(I32))
+
+        nc.sync.dma_start(offs_sb[:], offs)
+        nc.sync.dma_start(out=tab_sc[0:32, :].bitcast(I32), in_=tab_scales.rearrange("a q t -> (a q) t").bitcast(I32))
+        nc.sync.dma_start(out=w4_sc_raw[:], in_=w4_scales.rearrange("a q c -> (a q) c").bitcast(I32))
+        load_w4(0)
+        load_tab(0)
+        for tile_, src in zip(pos_sb, (pos1, pos2, pos3)):
+            nc.sync.dma_start(tile_[:], src)
+        load_tab(1)
+        for b in range(2):
+            nc.gpsimd.dma_start(
+                out=vec_rows[PACK * b : PACK * (b + 1), :],
+                in_=gain[512 * b : 512 * (b + 1)].rearrange("(g t i) -> t g i", t=PACK, i=8),
+            )
+        nc.gpsimd.dma_start(out=vec_rows[8:12, :], in_=cut.rearrange("(c p) -> c p", p=P))
+
+        def order_w4(b):
+            nc.vector.tensor_copy(
+                out=w4_wd[b][:].bitcast(I32).rearrange("p a (t g w) -> p a t g w", t=PACK, w=4),
+                in_=w4_raw[b][:].rearrange("p a (g t w) -> p a t g w", t=PACK, w=4),
+            )
+
+        def gather_words(a):
+            for u in range(2):
+                nc.vector.tensor_copy(
+                    v_wd[a][u][:], tab_wd[a][:].bitcast(U32).indirect(offs_sb[:, 32 * u : 32 * (u + 1)])
+                )
+
+        order_w4(0)
+        nc.vector.tensor_copy(
+            out=sc_rows[:, S // 4 :].rearrange("p (b t g w) -> p b t g w", b=2, t=PACK, w=2),
+            in_=w4_sc_raw[:].rearrange("p (b g t w) -> p b t g w", b=2, t=PACK, w=2),
+        )
+        nc.vector.tensor_copy(picked_sc[:], tab_sc[:].indirect(offs_sb[:]))
+        nc.vector.tensor_copy(out=sc_rows[:, : S // 4], in_=picked_sc[0:32, :].bitcast(I32))
+        for j in range(1, 8):
+            a, q = divmod(j, 4)
+            nc.scalar.dma_start(out=planes[a][32 * q : 32 * q + 4, :].bitcast(I32), in_=sc_rows[4 * j : 4 * j + 4, :])
+        gather_words(0)
+        load_w4(1)
+
+        acc = {}
+
+        def first_product(s, u, a):
+            b, t = divmod(s, PACK)
+            if a == 0:
+                acc[s, u] = psum.tile([P, BANK], F32, name="bank", tag="bank")
+            nc.tensor.matmul_mx(
+                out=acc[s, u][:],
+                lhsT=w4_wd[b][:, a, 256 * t : 256 * (t + 1)].bitcast(FP4X4),
+                lhsT_scale=planes[a][:, S + P * s : S + P * (s + 1)],
+                rhs=v_wd[a][u][:].bitcast(FP8X4),
+                rhs_scale=planes[a][:, BANK * u : BANK * (u + 1)],
+                start=(a == 0),
+                stop=(a == 1),
+            )
+
+        def finish_h(s):
+            for u in range(2):
+                if s >= 2:
+                    first_product(s, u, 0)
+                first_product(s, u, 1)
+                copy = nc.vector.tensor_copy if (s, u) == (0, 1) else nc.scalar.copy
+                copy(out=h_sb[s][:, BANK * u : BANK * (u + 1)], in_=acc[s, u][:])
+
+        for s in range(2):
+            for u in range(2):
+                first_product(s, u, 0)
+        gather_words(1)
+        wl_raw = held([P, 2, PACK, N], F32, "big1")
+        for b in range(2):
+            rows = wl[512 * b : 512 * (b + 1), :].rearrange("(g t i) n -> t g i n", t=PACK, i=8)
+            for t in range(PACK):
+                nc.sync.dma_start(out=wl_raw[:, b, t, :], in_=rows[t])
+        order_w4(1)
+        finish_h(0)
+        finish_h(1)
+        turned = psum.tile([P, P], F32, name="bank", tag="bank")
+        nc.tensor.transpose(turned[:], vec_rows[:], ident[:])
+        nc.scalar.copy(out=vec_cols[:], in_=turned[:, 0:12])
+
+        def interleave(copy, dst, src):
+            copy(
+                out=dst.rearrange("p (c i) t -> p c t i", i=4),
+                in_=src.rearrange("p t (c i) -> p c t i", i=4),
+            )
+
+        def quantize(codes, scales, grouped):
+            nc.vector.quantize_mx(
+                out=codes.bitcast(FP8X4), scales=scales, in_=grouped.rearrange("p m t -> p (m t)")
+            )
+
+        def pick(s, m0, w):
+            cols = slice(m0 // 16, (m0 + w) // 16)
+            hum = work.tile([P, w], F32, name="hum", tag="hum")
+            prime = work.tile([P, w], F32, name="prime", tag="prime")
+            cross = work.tile([P, w], F32, name="cross", tag="cross")
+            square = work.tile([P, w], F32, name="square", tag="square")
+            nc.vector.tensor_copy(prime[:], h_sb[s][:].indirect(pos_sb[1][:, cols]))
+            nc.vector.tensor_copy(hum[:], h_sb[s][:].indirect(pos_sb[0][:, cols]))
+            nc.vector.tensor_tensor(cross[:], h_sb[s][:].indirect(pos_sb[2][:, cols]), prime[:], ALU.mult)
+            nc.scalar.activation(out=square[:], in_=hum[:], func=ACT.Square)
+            return square, cross
+
+        def combine(s, picked, z_rows, w):
+            t = s % PACK
+            square, cross = picked
+            diff = work.tile([P, w], F32, name="diff", tag="diff")
+            nc.vector.tensor_tensor(diff[:], square[:], cross[:], ALU.subtract)
+            nc.scalar.activation(out=z_rows[:, t, :], in_=diff[:], func=ACT.Copy, scale=gain_sb[:, s : s + 1])
+
+        def pack_z(z_rows, w, name, copy):
+            z_bf = held([P, w, PACK], BF16, name + "_bf")
+            z_wd = held([P, w], U32, name + "_wd")
+            z_sc = held([P, w], U8, name + "_sc")
+            interleave(copy, z_bf[:], z_rows[:])
+            return z_bf, z_wd, z_sc
+
+        def second_product(bank, c, b, z_wd, z_sc):
+            nc.tensor.matmul_mx(
+                out=bank[:],
+                lhsT=wl_wd[b][:, P * c : P * (c + 1)].bitcast(FP8X4),
+                lhsT_scale=wl_sc[b][:, P * c : P * (c + 1)],
+                rhs=z_wd.bitcast(FP8X4),
+                rhs_scale=z_sc,
+                start=(b == 0),
+                stop=(b == 1),
+            )
+
+        def cast_wl(b, c):
+            cols = slice(P * c, P * (c + 1))
+            interleave(nc.scalar.copy, wl_bf[b][:, cols, :], wl_raw[:, b, :, cols])
+
+        z0_rows = held([P, PACK, M], BF16, "z0_rows")
+        waiting = None
+        for t in range(PACK):
+            picked = pick(t, 0, M)
+            finish_h(t + 2)
+            if waiting is not None:
+                combine(*waiting)
+            waiting = (t, picked, z0_rows, M)
+            if t >= 2:
+                cast_wl(0, 2 * (t - 2))
+                cast_wl(0, 2 * (t - 2) + 1)
+
+        z0 = None
+        banks = {}
+        steps = [(j, t) for j in range(len(LAST_CHUNKS)) for t in range(PACK)]
+        z1_rows = [held([P, PACK, w], BF16, "z1_rows%d" % j) for j, (m0, w) in enumerate(LAST_CHUNKS)]
+
+        def open_chunk(j):
+            m0, w = LAST_CHUNKS[j]
+            for c in range(N // P):
+                banks[j, c] = psum.tile([P, w], F32, name="bank", tag="bank")
+                second_product(banks[j, c], c, 0, z0[1][:, m0 : m0 + w], z0[2][:, m0 : m0 + w])
+
+        def close_chunk(j, z1):
+            m0, w = LAST_CHUNKS[j]
+            last = j == len(LAST_CHUNKS) - 1
+            quantize(z1[1][:], z1[2][:], z1[0][:])
+            result = held([P, N // P, w], F32, "result%d" % j)
+            for c in range(N // P):
+                second_product(banks[j, c], c, 1, z1[1][:], z1[2][:])
+                if last and c % 2:
+                    nc.vector.tensor_scalar(result[:, c, :], banks[j, c][:], cut_sb[:, c : c + 1], None, ALU.add)
+                else:
+                    nc.scalar.activation(
+                        out=result[:, c, :], in_=banks[j, c][:], func=ACT.Identity, bias=cut_sb[:, c : c + 1]
+                    )
+            nc.sync.dma_start(out=out[:, m0 : m0 + w].rearrange("(c p) m -> p c m", p=P), in_=result[:])
+
+        z1 = None
+        for j, t in steps:
+            m0, w = LAST_CHUNKS[j]
+            picked = pick(PACK + t, m0, w)
+            if j == 0 and t < 2:
+                finish_h(PACK + t + 2)
+            combine(*waiting)
+            waiting = (PACK + t, picked, z1_rows[j], w)
+            if j == 0:
+                cast_wl(1, t)
+                if t == 0:
+                    quantize(wl_wd[0][:], wl_sc[0][:], wl_bf[0][:])
+                    z0 = pack_z(z0_rows, M, "z0", nc.scalar.copy)
+                if t == 3:
+                    quantize(z0[1][:], z0[2][:], z0[0][:])
+                    open_chunk(0)
+                    open_chunk(1)
+            else:
+                if t == 0:
+                    if j == 1:
+                        quantize(wl_wd[1][:], wl_sc[1][:], wl_bf[1][:])
+                    z1 = pack_z(z1_rows[j - 1], LAST_CHUNKS[j - 1][1], "z1_%d" % (j - 1), nc.scalar.copy)
+                if t == 2:
+                    close_chunk(j - 1, z1)
+                    if j == 1:
+                        open_chunk(2)
+        combine(*waiting)
+        j = len(LAST_CHUNKS) - 1
+        z1 = pack_z(z1_rows[j], LAST_CHUNKS[j][1], "z1_%d" % j, nc.vector.tensor_copy)
+        close_chunk(j, z1)

@@ -178,11 +178,11 @@ def tile_list_bell_discriminant_kernel(
             nc.scalar.activation(out=square[:], in_=hum[:], func=ACT.Square)
             return square, cross
 
-        def combine(s, picked, z_rows, w):
+        def combine(s, picked, z_rows, w, engine=nc.gpsimd):
             t = s % PACK
             square, cross = picked
             diff = work.tile([P, w], F32, name="diff", tag="diff")
-            nc.vector.tensor_tensor(diff[:], square[:], cross[:], ALU.subtract)
+            engine.tensor_tensor(diff[:], square[:], cross[:], ALU.subtract)
             nc.scalar.activation(out=z_rows[:, t, :], in_=diff[:], func=ACT.Copy, scale=gain_sb[:, s : s + 1])
 
         def pack_z(z_rows, w, name, copy):
@@ -271,7 +271,7 @@ def tile_list_bell_discriminant_kernel(
                     close_chunk(j - 1, z1)
                     if j == 1:
                         open_chunk(2)
-        combine(*waiting)
+        combine(*waiting, nc.vector)
         j = len(LAST_CHUNKS) - 1
         z1 = pack_z(z1_rows[j], LAST_CHUNKS[j][1], "z1_%d" % j, nc.vector.tensor_copy)
         close_chunk(j, z1)

@@ -30,7 +30,7 @@ def tile_list_bell_discriminant_kernel(
     with ExitStack() as ctx:
         lists = ctx.enter_context(tc.tile_pool(name="lists", bufs=1))
         keep = ctx.enter_context(tc.tile_pool(name="keep", bufs=1))
-        work = ctx.enter_context(tc.tile_pool(name="work", bufs=3))
+        work = ctx.enter_context(tc.tile_pool(name="work", bufs=5))
         psum = ctx.enter_context(tc.psum_pool(name="psum", bufs=8))
 
         def held(shape, dtype, name):
@@ -80,8 +80,6 @@ def tile_list_bell_discriminant_kernel(
         nc.sync.dma_start(out=w4_sc_raw[:], in_=w4_scales.rearrange("a q c -> (a q) c").bitcast(I32))
         load_w4(0)
         load_tab(0)
-        for tile_, src in zip(pos_sb, (pos1, pos2, pos3)):
-            nc.sync.dma_start(tile_[:], src)
         load_tab(1)
         for b in range(2):
             nc.gpsimd.dma_start(
@@ -111,7 +109,10 @@ def tile_list_bell_discriminant_kernel(
         nc.vector.tensor_copy(out=sc_rows[:, : S // 4], in_=picked_sc[0:32, :].bitcast(I32))
         for j in range(1, 8):
             a, q = divmod(j, 4)
-            nc.scalar.dma_start(out=planes[a][32 * q : 32 * q + 4, :].bitcast(I32), in_=sc_rows[4 * j : 4 * j + 4, :])
+            queue = nc.sync if j == 7 else nc.scalar
+            queue.dma_start(out=planes[a][32 * q : 32 * q + 4, :].bitcast(I32), in_=sc_rows[4 * j : 4 * j + 4, :])
+        for tile_, src in zip(pos_sb, (pos1, pos2, pos3)):
+            nc.sync.dma_start(tile_[:], src)
         gather_words(0)
         load_w4(1)
 
@@ -183,7 +184,10 @@ def tile_list_bell_discriminant_kernel(
             square, cross = picked
             diff = work.tile([P, w], F32, name="diff", tag="diff")
             engine.tensor_tensor(diff[:], square[:], cross[:], ALU.subtract)
-            nc.scalar.activation(out=z_rows[:, t, :], in_=diff[:], func=ACT.Copy, scale=gain_sb[:, s : s + 1])
+            if z_rows is z1_rows[-1] and engine is nc.gpsimd:
+                nc.scalar.activation(out=z_rows[:, t, :], in_=diff[:], func=ACT.Copy, scale=gain_sb[:, s : s + 1])
+            else:
+                engine.tensor_scalar(z_rows[:, t, :], diff[:], gain_sb[:, s : s + 1], 0.0, ALU.mult, ALU.add)
 
         def pack_z(z_rows, w, name, copy):
             z_bf = held([P, w, PACK], BF16, name + "_bf")
@@ -208,21 +212,23 @@ def tile_list_bell_discriminant_kernel(
             interleave(nc.scalar.copy, wl_bf[b][:, cols, :], wl_raw[:, b, :, cols])
 
         z0_rows = held([P, PACK, M], BF16, "z0_rows")
+        z1_rows = [held([P, PACK, w], BF16, "z1_rows%d" % j) for j, (m0, w) in enumerate(LAST_CHUNKS)]
         waiting = None
         for t in range(PACK):
             picked = pick(t, 0, M)
-            finish_h(t + 2)
+            if t < 3:
+                finish_h(2 * t + 2)
+                finish_h(2 * t + 3)
             if waiting is not None:
                 combine(*waiting)
             waiting = (t, picked, z0_rows, M)
             if t >= 2:
-                cast_wl(0, 2 * (t - 2))
-                cast_wl(0, 2 * (t - 2) + 1)
+                for c in range(N // P):
+                    cast_wl(t - 2, c)
 
         z0 = None
         banks = {}
         steps = [(j, t) for j in range(len(LAST_CHUNKS)) for t in range(PACK)]
-        z1_rows = [held([P, PACK, w], BF16, "z1_rows%d" % j) for j, (m0, w) in enumerate(LAST_CHUNKS)]
 
         def open_chunk(j):
             m0, w = LAST_CHUNKS[j]
@@ -243,29 +249,31 @@ def tile_list_bell_discriminant_kernel(
                     nc.scalar.activation(
                         out=result[:, c, :], in_=banks[j, c][:], func=ACT.Identity, bias=cut_sb[:, c : c + 1]
                     )
-            nc.sync.dma_start(out=out[:, m0 : m0 + w].rearrange("(c p) m -> p c m", p=P), in_=result[:])
+                if c % 2 and (last or c == 3):
+                    c0 = c - 1 if last else 0
+                    nc.sync.dma_start(
+                        out=out[P * c0 : P * (c + 1), m0 : m0 + w].rearrange("(c p) m -> p c m", p=P),
+                        in_=result[:, c0 : c + 1, :],
+                    )
 
         z1 = None
         for j, t in steps:
             m0, w = LAST_CHUNKS[j]
             picked = pick(PACK + t, m0, w)
-            if j == 0 and t < 2:
-                finish_h(PACK + t + 2)
             combine(*waiting)
             waiting = (PACK + t, picked, z1_rows[j], w)
             if j == 0:
-                cast_wl(1, t)
                 if t == 0:
                     quantize(wl_wd[0][:], wl_sc[0][:], wl_bf[0][:])
                     z0 = pack_z(z0_rows, M, "z0", nc.scalar.copy)
+                if t == 1:
+                    quantize(wl_wd[1][:], wl_sc[1][:], wl_bf[1][:])
                 if t == 3:
                     quantize(z0[1][:], z0[2][:], z0[0][:])
                     open_chunk(0)
                     open_chunk(1)
             else:
                 if t == 0:
-                    if j == 1:
-                        quantize(wl_wd[1][:], wl_sc[1][:], wl_bf[1][:])
                     z1 = pack_z(z1_rows[j - 1], LAST_CHUNKS[j - 1][1], "z1_%d" % (j - 1), nc.scalar.copy)
                 if t == 2:
                     close_chunk(j - 1, z1)

@@ -155,6 +155,7 @@ def tile_list_bell_discriminant_kernel(
         turned = psum.tile([P, P], F32, name="bank", tag="bank")
         nc.tensor.transpose(turned[:], vec_rows[:], ident[:])
         nc.scalar.copy(out=vec_cols[:], in_=turned[:, 0:12])
+        finish_h(2)
 
         def interleave(copy, dst, src):
             copy(
@@ -184,7 +185,7 @@ def tile_list_bell_discriminant_kernel(
             square, cross = picked
             diff = work.tile([P, w], F32, name="diff", tag="diff")
             engine.tensor_tensor(diff[:], square[:], cross[:], ALU.subtract)
-            if z_rows is z1_rows[-1] and engine is nc.gpsimd:
+            if engine is nc.gpsimd:
                 nc.scalar.activation(out=z_rows[:, t, :], in_=diff[:], func=ACT.Copy, scale=gain_sb[:, s : s + 1])
             else:
                 engine.tensor_scalar(z_rows[:, t, :], diff[:], gain_sb[:, s : s + 1], 0.0, ALU.mult, ALU.add)
@@ -213,18 +214,16 @@ def tile_list_bell_discriminant_kernel(
 
         z0_rows = held([P, PACK, M], BF16, "z0_rows")
         z1_rows = [held([P, PACK, w], BF16, "z1_rows%d" % j) for j, (m0, w) in enumerate(LAST_CHUNKS)]
-        waiting = None
+        casts = [(b, c) for b in range(2) for c in range(N // P)]
         for t in range(PACK):
             picked = pick(t, 0, M)
-            if t < 3:
-                finish_h(2 * t + 2)
-                finish_h(2 * t + 3)
-            if waiting is not None:
-                combine(*waiting)
-            waiting = (t, picked, z0_rows, M)
-            if t >= 2:
-                for c in range(N // P):
-                    cast_wl(t - 2, c)
+            if t == 0:
+                finish_h(3)
+            finish_h(PACK + t)
+            if t in (1, 2):
+                cast_wl(*casts.pop(0))
+                cast_wl(*casts.pop(0))
+            combine(t, picked, z0_rows, M)
 
         z0 = None
         banks = {}
@@ -260,26 +259,26 @@ def tile_list_bell_discriminant_kernel(
         for j, t in steps:
             m0, w = LAST_CHUNKS[j]
             picked = pick(PACK + t, m0, w)
-            combine(*waiting)
-            waiting = (PACK + t, picked, z1_rows[j], w)
             if j == 0:
+                cast_wl(*casts.pop(0))
                 if t == 0:
                     quantize(wl_wd[0][:], wl_sc[0][:], wl_bf[0][:])
-                    z0 = pack_z(z0_rows, M, "z0", nc.scalar.copy)
                 if t == 1:
-                    quantize(wl_wd[1][:], wl_sc[1][:], wl_bf[1][:])
-                if t == 3:
+                    z0 = pack_z(z0_rows, M, "z0", nc.vector.tensor_copy)
+                if t == 2:
                     quantize(z0[1][:], z0[2][:], z0[0][:])
                     open_chunk(0)
                     open_chunk(1)
             else:
                 if t == 0:
+                    if j == 1:
+                        quantize(wl_wd[1][:], wl_sc[1][:], wl_bf[1][:])
                     z1 = pack_z(z1_rows[j - 1], LAST_CHUNKS[j - 1][1], "z1_%d" % (j - 1), nc.scalar.copy)
                 if t == 2:
                     close_chunk(j - 1, z1)
                     if j == 1:
                         open_chunk(2)
-        combine(*waiting, nc.vector)
+            combine(PACK + t, picked, z1_rows[j], w, nc.vector if (j, t) == steps[-1] else nc.gpsimd)
         j = len(LAST_CHUNKS) - 1
         z1 = pack_z(z1_rows[j], LAST_CHUNKS[j][1], "z1_%d" % j, nc.vector.tensor_copy)
         close_chunk(j, z1)

@@ -19,8 +19,17 @@ ALU = mybir.AluOpType
 
 P = 128
 PACK = 4
+PASS = P * PACK
 BANK = 512
-LAST_CHUNKS = ((0, 256), (256, 128), (384, 128))
+RUN = 8
+PER_COLUMN = 16
+SCALE_ROWS = 32
+SLICES = H // P
+N_TILES = N // P
+HALF = M // 2
+CHUNKS = ((0, HALF), (HALF, P), (HALF + P, P))
+EARLY_SLICES = 2
+WORK_BUFS = 5
 
 
 def tile_list_bell_discriminant_kernel(
@@ -30,63 +39,65 @@ def tile_list_bell_discriminant_kernel(
     with ExitStack() as ctx:
         lists = ctx.enter_context(tc.tile_pool(name="lists", bufs=1))
         keep = ctx.enter_context(tc.tile_pool(name="keep", bufs=1))
-        work = ctx.enter_context(tc.tile_pool(name="work", bufs=5))
+        work = ctx.enter_context(tc.tile_pool(name="work", bufs=WORK_BUFS))
         psum = ctx.enter_context(tc.psum_pool(name="psum", bufs=8))
 
         def held(shape, dtype, name):
             return keep.tile(shape, dtype, name=name, align_bytes=64)
 
-        offs_sb = lists.tile([P, S // 16], U16, name="offs_sb")
-        pos_sb = [lists.tile([P, M // 16], U16, name="pos_sb%d" % i) for i in range(3)]
+        def bank(width):
+            return psum.tile([P, width], F32, name="bank", tag="bank")
+
+        offs_sb = lists.tile([P, S // PER_COLUMN], U16, name="offs_sb")
+        pos_sb = [lists.tile([P, M // PER_COLUMN], U16, name="pos_sb%d" % i) for i in range(3)]
+        hum_list, prime_list, tierce_list = pos_sb
 
         tab_sc = held([P, T], U8, "tab_sc")
         picked_sc = held([P, S], U8, "picked_sc")
-        w4_sc_raw = held([32, H // 4], I32, "w4_sc_raw")
+        w4_sc_raw = held([SCALE_ROWS, H // 4], I32, "w4_sc_raw")
         planes = [held([P, S + H], U8, "planes%d" % a) for a in range(2)]
         w4_raw = {}
-        w4_wd = [held([P, 2, 1024], U8, "w4_wd%d" % b) for b in range(2)]
-        tab_wd = [held([P, T], I32, "big%d" % a) for a in range(2)]
+        w4_wd = [held([P, 2, 2 * PASS], U8, "w4_wd%d" % b) for b in range(2)]
+        tab_wd = [held([P, T], I32, "window%d" % a) for a in range(2)]
         v_wd = [[held([P, BANK], U32, "v_wd%d%d" % (a, u)) for u in range(2)] for a in range(2)]
         vec_rows = held([P, P], F32, "vec_rows")
         ident = held([P, P], F32, "ident")
-        vec_cols = held([P, 12], F32, "vec_cols")
-        gain_sb = vec_cols[:, 0:8]
-        cut_sb = vec_cols[:, 8:12]
+        vec_cols = held([P, SLICES + N_TILES], F32, "vec_cols")
+        gain_sb = vec_cols[:, :SLICES]
+        cut_sb = vec_cols[:, SLICES:]
         wl_bf = [held([P, N, PACK], BF16, "wl_bf%d" % b) for b in range(2)]
         wl_wd = [held([P, N], U32, "wl_wd%d" % b) for b in range(2)]
         wl_sc = [held([P, N], U8, "wl_sc%d" % b) for b in range(2)]
-        h_sb = [held([P, S], F32, "h_sb%d" % s) for s in range(8)]
+        h_sb = [held([P, S], F32, "h_sb%d" % s) for s in range(SLICES)]
 
-        nc.vector.memset(tab_sc[32:64, :].bitcast(I32), 0)
-        nc.vector.memset(tab_sc[64:128, :].bitcast(I32), 0)
+        nc.vector.memset(tab_sc[SCALE_ROWS:64, :].bitcast(I32), 0)
+        nc.vector.memset(tab_sc[64:, :].bitcast(I32), 0)
         for a in range(2):
             nc.vector.memset(planes[a][:].bitcast(I32), 0)
-        sc_rows = planes[0][0:32, :].bitcast(I32)
         nc.gpsimd.memset(vec_rows[:], 0.0)
         make_identity(nc, ident[:])
 
-        def load_w4(b):
-            w4_raw[b] = held([P, 2, 256], I32, "big0" if b else "w4_raw")
+        def load_w4(b, name):
+            w4_raw[b] = held([P, 2, PASS // 2], I32, name)
             nc.sync.dma_start(
                 out=w4_raw[b][:],
-                in_=w4_words[:, :, 1024 * b : 1024 * (b + 1)].bitcast(I32).rearrange("a p c -> p a c"),
+                in_=w4_words[:, :, 2 * PASS * b : 2 * PASS * (b + 1)].bitcast(I32).rearrange("a p c -> p a c"),
             )
 
-        def load_tab(a):
-            nc.sync.dma_start(out=tab_wd[a][:], in_=tab_words[a].rearrange("p t i -> p (t i)").bitcast(I32))
-
         nc.sync.dma_start(offs_sb[:], offs)
-        nc.sync.dma_start(out=tab_sc[0:32, :].bitcast(I32), in_=tab_scales.rearrange("a q t -> (a q) t").bitcast(I32))
+        nc.sync.dma_start(
+            out=tab_sc[:SCALE_ROWS, :].bitcast(I32), in_=tab_scales.rearrange("a q t -> (a q) t").bitcast(I32)
+        )
         nc.sync.dma_start(out=w4_sc_raw[:], in_=w4_scales.rearrange("a q c -> (a q) c").bitcast(I32))
-        load_w4(0)
-        load_tab(0)
-        load_tab(1)
+        load_w4(0, "w4_raw")
+        for a in range(2):
+            nc.sync.dma_start(out=tab_wd[a][:], in_=tab_words[a].rearrange("p t i -> p (t i)").bitcast(I32))
         for b in range(2):
             nc.gpsimd.dma_start(
                 out=vec_rows[PACK * b : PACK * (b + 1), :],
-                in_=gain[512 * b : 512 * (b + 1)].rearrange("(g t i) -> t g i", t=PACK, i=8),
+                in_=gain[PASS * b : PASS * (b + 1)].rearrange("(g t i) -> t g i", t=PACK, i=RUN),
             )
-        nc.gpsimd.dma_start(out=vec_rows[8:12, :], in_=cut.rearrange("(c p) -> c p", p=P))
+        nc.gpsimd.dma_start(out=vec_rows[SLICES : SLICES + N_TILES, :], in_=cut.rearrange("(c p) -> c p", p=P))
 
         def order_w4(b):
             nc.vector.tensor_copy(
@@ -95,36 +106,38 @@ def tile_list_bell_discriminant_kernel(
             )
 
         def gather_words(a):
+            columns = BANK // PER_COLUMN
             for u in range(2):
                 nc.vector.tensor_copy(
-                    v_wd[a][u][:], tab_wd[a][:].bitcast(U32).indirect(offs_sb[:, 32 * u : 32 * (u + 1)])
+                    v_wd[a][u][:], tab_wd[a][:].bitcast(U32).indirect(offs_sb[:, columns * u : columns * (u + 1)])
                 )
 
-        order_w4(0)
+        staged = planes[0][:SCALE_ROWS, :].bitcast(I32)
         nc.vector.tensor_copy(
-            out=sc_rows[:, S // 4 :].rearrange("p (b t g w) -> p b t g w", b=2, t=PACK, w=2),
+            out=staged[:, S // 4 :].rearrange("p (b t g w) -> p b t g w", b=2, t=PACK, w=2),
             in_=w4_sc_raw[:].rearrange("p (b g t w) -> p b t g w", b=2, t=PACK, w=2),
         )
         nc.vector.tensor_copy(picked_sc[:], tab_sc[:].indirect(offs_sb[:]))
-        nc.vector.tensor_copy(out=sc_rows[:, : S // 4], in_=picked_sc[0:32, :].bitcast(I32))
-        for j in range(1, 8):
-            a, q = divmod(j, 4)
-            queue = nc.sync if j == 7 else nc.scalar
-            queue.dma_start(out=planes[a][32 * q : 32 * q + 4, :].bitcast(I32), in_=sc_rows[4 * j : 4 * j + 4, :])
-        for tile_, src in zip(pos_sb, (pos1, pos2, pos3)):
-            nc.sync.dma_start(tile_[:], src)
+        nc.vector.tensor_copy(out=staged[:, : S // 4], in_=picked_sc[:SCALE_ROWS, :].bitcast(I32))
+        order_w4(0)
+        for e in range(1, 8):
+            a, q = divmod(e, 4)
+            queue = nc.sync if e == 7 else nc.scalar
+            queue.dma_start(out=planes[a][32 * q : 32 * q + 4, :].bitcast(I32), in_=staged[4 * e : 4 * e + 4, :])
+        for list_sb, src in zip(pos_sb, (pos1, pos2, pos3)):
+            nc.sync.dma_start(list_sb[:], src)
         gather_words(0)
-        load_w4(1)
+        load_w4(1, "window0")
 
         acc = {}
 
         def first_product(s, u, a):
             b, t = divmod(s, PACK)
             if a == 0:
-                acc[s, u] = psum.tile([P, BANK], F32, name="bank", tag="bank")
+                acc[s, u] = bank(BANK)
             nc.tensor.matmul_mx(
                 out=acc[s, u][:],
-                lhsT=w4_wd[b][:, a, 256 * t : 256 * (t + 1)].bitcast(FP4X4),
+                lhsT=w4_wd[b][:, a, 2 * P * t : 2 * P * (t + 1)].bitcast(FP4X4),
                 lhsT_scale=planes[a][:, S + P * s : S + P * (s + 1)],
                 rhs=v_wd[a][u][:].bitcast(FP8X4),
                 rhs_scale=planes[a][:, BANK * u : BANK * (u + 1)],
@@ -134,27 +147,29 @@ def tile_list_bell_discriminant_kernel(
 
         def finish_h(s):
             for u in range(2):
-                if s >= 2:
+                if s >= EARLY_SLICES:
                     first_product(s, u, 0)
                 first_product(s, u, 1)
                 copy = nc.vector.tensor_copy if (s, u) == (0, 1) else nc.scalar.copy
                 copy(out=h_sb[s][:, BANK * u : BANK * (u + 1)], in_=acc[s, u][:])
 
-        for s in range(2):
+        for s in range(EARLY_SLICES):
             for u in range(2):
                 first_product(s, u, 0)
         gather_words(1)
-        wl_raw = held([P, 2, PACK, N], F32, "big1")
+        wl_raw = held([P, 2, PACK, N], F32, "window1")
         for b in range(2):
-            rows = wl[512 * b : 512 * (b + 1), :].rearrange("(g t i) n -> t g i n", t=PACK, i=8)
+            rows = wl[PASS * b : PASS * (b + 1), :].rearrange("(g t i) n -> t g i n", t=PACK, i=RUN)
             for t in range(PACK):
                 nc.sync.dma_start(out=wl_raw[:, b, t, :], in_=rows[t])
         order_w4(1)
         finish_h(0)
         finish_h(1)
-        turned = psum.tile([P, P], F32, name="bank", tag="bank")
+        turned = bank(P)
         nc.tensor.transpose(turned[:], vec_rows[:], ident[:])
-        nc.scalar.copy(out=vec_cols[:], in_=turned[:, 0:12])
+        nc.scalar.copy(out=vec_cols[:], in_=turned[:, : SLICES + N_TILES])
+        gain_wide = held([P, PACK, P], F32, "gain_wide")
+        nc.scalar.copy(out=gain_wide[:], in_=gain_sb[:, PACK:].unsqueeze(2).to_broadcast([P, PACK, P]))
         finish_h(2)
 
         def interleave(copy, dst, src):
@@ -163,43 +178,50 @@ def tile_list_bell_discriminant_kernel(
                 in_=src.rearrange("p t (c i) -> p c t i", i=4),
             )
 
-        def quantize(codes, scales, grouped):
+        def quantize(grouped, codes, scales):
             nc.vector.quantize_mx(
-                out=codes.bitcast(FP8X4), scales=scales, in_=grouped.rearrange("p m t -> p (m t)")
+                out=codes[:].bitcast(FP8X4), scales=scales[:], in_=grouped[:].rearrange("p m t -> p (m t)")
             )
 
         def pick(s, m0, w):
-            cols = slice(m0 // 16, (m0 + w) // 16)
+            cols = slice(m0 // PER_COLUMN, (m0 + w) // PER_COLUMN)
             hum = work.tile([P, w], F32, name="hum", tag="hum")
             prime = work.tile([P, w], F32, name="prime", tag="prime")
             cross = work.tile([P, w], F32, name="cross", tag="cross")
             square = work.tile([P, w], F32, name="square", tag="square")
-            nc.vector.tensor_copy(prime[:], h_sb[s][:].indirect(pos_sb[1][:, cols]))
-            nc.vector.tensor_copy(hum[:], h_sb[s][:].indirect(pos_sb[0][:, cols]))
-            nc.vector.tensor_tensor(cross[:], h_sb[s][:].indirect(pos_sb[2][:, cols]), prime[:], ALU.mult)
+            if w == P:
+                nc.vector.tensor_tensor(
+                    prime[:], h_sb[s][:].indirect(prime_list[:, cols]), gain_wide[:, s - PACK, :], ALU.mult
+                )
+            else:
+                nc.vector.tensor_copy(prime[:], h_sb[s][:].indirect(prime_list[:, cols]))
+            nc.vector.tensor_copy(hum[:], h_sb[s][:].indirect(hum_list[:, cols]))
+            nc.vector.tensor_tensor(cross[:], h_sb[s][:].indirect(tierce_list[:, cols]), prime[:], ALU.mult)
             nc.scalar.activation(out=square[:], in_=hum[:], func=ACT.Square)
             return square, cross
 
-        def combine(s, picked, z_rows, w, engine=nc.gpsimd):
+        def combine(s, picked, z_rows, w):
             t = s % PACK
             square, cross = picked
-            diff = work.tile([P, w], F32, name="diff", tag="diff")
-            engine.tensor_tensor(diff[:], square[:], cross[:], ALU.subtract)
-            if engine is nc.gpsimd:
-                nc.scalar.activation(out=z_rows[:, t, :], in_=diff[:], func=ACT.Copy, scale=gain_sb[:, s : s + 1])
+            if w == P:
+                nc.vector.scalar_tensor_tensor(
+                    z_rows[:, t, :], square[:], gain_sb[:, s : s + 1], cross[:], ALU.mult, ALU.subtract
+                )
             else:
-                engine.tensor_scalar(z_rows[:, t, :], diff[:], gain_sb[:, s : s + 1], 0.0, ALU.mult, ALU.add)
+                diff = work.tile([P, w], F32, name="diff", tag="diff")
+                nc.gpsimd.tensor_tensor(diff[:], square[:], cross[:], ALU.subtract)
+                nc.scalar.activation(out=z_rows[:, t, :], in_=diff[:], func=ACT.Copy, scale=gain_sb[:, s : s + 1])
 
-        def pack_z(z_rows, w, name, copy):
+        def group_z(z_rows, w, name, copy):
             z_bf = held([P, w, PACK], BF16, name + "_bf")
             z_wd = held([P, w], U32, name + "_wd")
             z_sc = held([P, w], U8, name + "_sc")
-            interleave(copy, z_bf[:], z_rows[:])
+            interleave(copy, z_bf[:], z_rows)
             return z_bf, z_wd, z_sc
 
-        def second_product(bank, c, b, z_wd, z_sc):
+        def second_product(sums, c, b, z_wd, z_sc):
             nc.tensor.matmul_mx(
-                out=bank[:],
+                out=sums[:],
                 lhsT=wl_wd[b][:, P * c : P * (c + 1)].bitcast(FP8X4),
                 lhsT_scale=wl_sc[b][:, P * c : P * (c + 1)],
                 rhs=z_wd.bitcast(FP8X4),
@@ -208,77 +230,87 @@ def tile_list_bell_discriminant_kernel(
                 stop=(b == 1),
             )
 
-        def cast_wl(b, c):
-            cols = slice(P * c, P * (c + 1))
-            interleave(nc.scalar.copy, wl_bf[b][:, cols, :], wl_raw[:, b, :, cols])
+        wl_pieces = [(b, c) for b in range(2) for c in range(N_TILES)]
+
+        def cast_wl(pieces):
+            for turn in range(pieces):
+                b, c = wl_pieces.pop(0)
+                cols = slice(P * c, P * (c + 1))
+                interleave(nc.scalar.copy, wl_bf[b][:, cols, :], wl_raw[:, b, :, cols])
 
         z0_rows = held([P, PACK, M], BF16, "z0_rows")
-        z1_rows = [held([P, PACK, w], BF16, "z1_rows%d" % j) for j, (m0, w) in enumerate(LAST_CHUNKS)]
-        casts = [(b, c) for b in range(2) for c in range(N // P)]
-        for t in range(PACK):
+        z1_rows = [held([P, PACK, w], BF16, "z1_rows%d" % j) for j, (m0, w) in enumerate(CHUNKS)]
+        for t, pieces in enumerate((0, 2, 2, 1)):
             picked = pick(t, 0, M)
             if t == 0:
                 finish_h(3)
             finish_h(PACK + t)
-            if t in (1, 2):
-                cast_wl(*casts.pop(0))
-                cast_wl(*casts.pop(0))
+            cast_wl(pieces)
             combine(t, picked, z0_rows, M)
 
-        z0 = None
-        banks = {}
-        steps = [(j, t) for j in range(len(LAST_CHUNKS)) for t in range(PACK)]
+        z0 = {}
+        sums = {}
 
         def open_chunk(j):
-            m0, w = LAST_CHUNKS[j]
-            for c in range(N // P):
-                banks[j, c] = psum.tile([P, w], F32, name="bank", tag="bank")
-                second_product(banks[j, c], c, 0, z0[1][:, m0 : m0 + w], z0[2][:, m0 : m0 + w])
+            m0, w = CHUNKS[j]
+            half, lo = divmod(m0, HALF)
+            for c in range(N_TILES):
+                sums[j, c] = bank(w)
+                second_product(sums[j, c], c, 0, z0[half][1][:, lo : lo + w], z0[half][2][:, lo : lo + w])
 
         def close_chunk(j, z1):
-            m0, w = LAST_CHUNKS[j]
-            last = j == len(LAST_CHUNKS) - 1
-            quantize(z1[1][:], z1[2][:], z1[0][:])
-            result = held([P, N // P, w], F32, "result%d" % j)
-            for c in range(N // P):
-                second_product(banks[j, c], c, 1, z1[1][:], z1[2][:])
-                if last and c % 2:
-                    nc.vector.tensor_scalar(result[:, c, :], banks[j, c][:], cut_sb[:, c : c + 1], None, ALU.add)
+            m0, w = CHUNKS[j]
+            last = j == len(CHUNKS) - 1
+            tiles_a_store = 2 if last else N_TILES
+            quantize(*z1)
+            result = held([P, N_TILES, w], F32, "result%d" % j)
+            for c in range(N_TILES):
+                second_product(sums[j, c], c, 1, z1[1][:], z1[2][:])
+                if last:
+                    nc.vector.tensor_scalar(result[:, c, :], sums[j, c][:], cut_sb[:, c : c + 1], None, ALU.add)
                 else:
                     nc.scalar.activation(
-                        out=result[:, c, :], in_=banks[j, c][:], func=ACT.Identity, bias=cut_sb[:, c : c + 1]
+                        out=result[:, c, :], in_=sums[j, c][:], func=ACT.Identity, bias=cut_sb[:, c : c + 1]
                     )
-                if c % 2 and (last or c == 3):
-                    c0 = c - 1 if last else 0
+                if (c + 1) % tiles_a_store == 0:
+                    c0 = c + 1 - tiles_a_store
                     nc.sync.dma_start(
                         out=out[P * c0 : P * (c + 1), m0 : m0 + w].rearrange("(c p) m -> p c m", p=P),
                         in_=result[:, c0 : c + 1, :],
                     )
 
         z1 = None
-        for j, t in steps:
-            m0, w = LAST_CHUNKS[j]
-            picked = pick(PACK + t, m0, w)
-            if j == 0:
-                cast_wl(*casts.pop(0))
-                if t == 0:
-                    quantize(wl_wd[0][:], wl_sc[0][:], wl_bf[0][:])
-                if t == 1:
-                    z0 = pack_z(z0_rows, M, "z0", nc.vector.tensor_copy)
-                if t == 2:
-                    quantize(z0[1][:], z0[2][:], z0[0][:])
-                    open_chunk(0)
-                    open_chunk(1)
-            else:
-                if t == 0:
-                    if j == 1:
-                        quantize(wl_wd[1][:], wl_sc[1][:], wl_bf[1][:])
-                    z1 = pack_z(z1_rows[j - 1], LAST_CHUNKS[j - 1][1], "z1_%d" % (j - 1), nc.scalar.copy)
-                if t == 2:
-                    close_chunk(j - 1, z1)
-                    if j == 1:
+        waiting = []
+        for j, (m0, w) in enumerate(CHUNKS):
+            for t in range(PACK):
+                picked = pick(PACK + t, m0, w)
+                if waiting:
+                    combine(*waiting.pop())
+                if j == 0:
+                    if t == 0:
+                        quantize(wl_bf[0], wl_wd[0], wl_sc[0])
+                    if t == 1:
+                        z0[0] = group_z(z0_rows[:, :, :HALF], HALF, "z0a", nc.scalar.copy)
+                    else:
+                        cast_wl(1)
+                    if t == PACK - 1:
+                        quantize(*z0[0])
+                        open_chunk(0)
+                    combine(PACK + t, picked, z1_rows[j], w)
+                else:
+                    if t == 0:
+                        if j == 1:
+                            quantize(wl_bf[1], wl_wd[1], wl_sc[1])
+                        z1 = group_z(z1_rows[j - 1][:], CHUNKS[j - 1][1], "z1_%d" % (j - 1), nc.scalar.copy)
+                    if (j, t) == (1, 1):
+                        z0[1] = group_z(z0_rows[:, :, HALF:], HALF, "z0b", nc.scalar.copy)
+                    if t == 2:
+                        close_chunk(j - 1, z1)
+                    if (j, t) == (1, PACK - 1):
+                        quantize(*z0[1])
+                        open_chunk(1)
                         open_chunk(2)
-            combine(PACK + t, picked, z1_rows[j], w, nc.vector if (j, t) == steps[-1] else nc.gpsimd)
-        j = len(LAST_CHUNKS) - 1
-        z1 = pack_z(z1_rows[j], LAST_CHUNKS[j][1], "z1_%d" % j, nc.vector.tensor_copy)
-        close_chunk(j, z1)
+                    waiting.append((PACK + t, picked, z1_rows[j], w))
+        combine(*waiting.pop())
+        j = len(CHUNKS) - 1
+        close_chunk(j, group_z(z1_rows[j][:], CHUNKS[j][1], "z1_%d" % j, nc.vector.tensor_copy))

@@ -27,7 +27,7 @@ SCALE_ROWS = 32
 SLICES = H // P
 N_TILES = N // P
 HALF = M // 2
-CHUNKS = ((0, HALF), (HALF, P), (HALF + P, P))
+WIDE = M - P
 EARLY_SLICES = 2
 WORK_BUFS = 5
 
@@ -179,9 +179,7 @@ def tile_list_bell_discriminant_kernel(
             )
 
         def quantize(grouped, codes, scales):
-            nc.vector.quantize_mx(
-                out=codes[:].bitcast(FP8X4), scales=scales[:], in_=grouped[:].rearrange("p m t -> p (m t)")
-            )
+            nc.vector.quantize_mx(out=codes.bitcast(FP8X4), scales=scales, in_=grouped.rearrange("p m t -> p (m t)"))
 
         def pick(s, m0, w):
             cols = slice(m0 // PER_COLUMN, (m0 + w) // PER_COLUMN)
@@ -189,45 +187,49 @@ def tile_list_bell_discriminant_kernel(
             prime = work.tile([P, w], F32, name="prime", tag="prime")
             cross = work.tile([P, w], F32, name="cross", tag="cross")
             square = work.tile([P, w], F32, name="square", tag="square")
-            if w == P:
-                nc.vector.tensor_tensor(
-                    prime[:], h_sb[s][:].indirect(prime_list[:, cols]), gain_wide[:, s - PACK, :], ALU.mult
-                )
-            else:
-                nc.vector.tensor_copy(prime[:], h_sb[s][:].indirect(prime_list[:, cols]))
+            nc.vector.tensor_copy(prime[:], h_sb[s][:].indirect(prime_list[:, cols]))
             nc.vector.tensor_copy(hum[:], h_sb[s][:].indirect(hum_list[:, cols]))
             nc.vector.tensor_tensor(cross[:], h_sb[s][:].indirect(tierce_list[:, cols]), prime[:], ALU.mult)
             nc.scalar.activation(out=square[:], in_=hum[:], func=ACT.Square)
             return square, cross
 
-        def combine(s, picked, z_rows, w):
-            t = s % PACK
+        def combine(engine, s, picked, z_row):
             square, cross = picked
-            if w == P:
-                nc.vector.scalar_tensor_tensor(
-                    z_rows[:, t, :], square[:], gain_sb[:, s : s + 1], cross[:], ALU.mult, ALU.subtract
-                )
-            else:
-                diff = work.tile([P, w], F32, name="diff", tag="diff")
-                nc.gpsimd.tensor_tensor(diff[:], square[:], cross[:], ALU.subtract)
-                nc.scalar.activation(out=z_rows[:, t, :], in_=diff[:], func=ACT.Copy, scale=gain_sb[:, s : s + 1])
+            diff = work.tile(list(square.shape), F32, name="diff", tag="diff")
+            engine.tensor_tensor(diff[:], square[:], cross[:], ALU.subtract)
+            nc.scalar.activation(out=z_row, in_=diff[:], func=ACT.Copy, scale=gain_sb[:, s : s + 1])
 
-        def group_z(z_rows, w, name, copy):
-            z_bf = held([P, w, PACK], BF16, name + "_bf")
-            z_wd = held([P, w], U32, name + "_wd")
-            z_sc = held([P, w], U8, name + "_sc")
-            interleave(copy, z_bf[:], z_rows)
-            return z_bf, z_wd, z_sc
+        def pick_last(t, prime):
+            s = PACK + t
+            cols = slice(WIDE // PER_COLUMN, M // PER_COLUMN)
+            hum = work.tile([P, P], F32, name="hum", tag="hum")
+            cross = work.tile([P, P], F32, name="cross", tag="cross")
+            square = work.tile([P, P], F32, name="square", tag="square")
+            nc.vector.tensor_copy(hum[:], h_sb[s][:].indirect(hum_list[:, cols]))
+            nc.vector.tensor_tensor(prime[:], h_sb[s][:].indirect(prime_list[:, cols]), gain_wide[:, t, :], ALU.mult)
+            nc.vector.tensor_tensor(cross[:], h_sb[s][:].indirect(tierce_list[:, cols]), prime[:], ALU.mult)
+            nc.scalar.activation(out=square[:], in_=hum[:], func=ACT.Square)
+            return square, cross
 
-        def second_product(sums, c, b, z_wd, z_sc):
+        def combine_last(t, picked, z_row):
+            square, cross = picked
+            s = PACK + t
+            nc.vector.scalar_tensor_tensor(z_row, square[:], gain_sb[:, s : s + 1], cross[:], ALU.mult, ALU.subtract)
+
+        def second_product(sums, c, b, z_wd, z_sc, start, stop):
             nc.tensor.matmul_mx(
-                out=sums[:],
+                out=sums,
                 lhsT=wl_wd[b][:, P * c : P * (c + 1)].bitcast(FP8X4),
                 lhsT_scale=wl_sc[b][:, P * c : P * (c + 1)],
                 rhs=z_wd.bitcast(FP8X4),
                 rhs_scale=z_sc,
-                start=(b == 0),
-                stop=(b == 1),
+                start=start,
+                stop=stop,
+            )
+
+        def store(result, c0, tiles, m0, w):
+            nc.sync.dma_start(
+                out=out[P * c0 : P * (c0 + tiles), m0 : m0 + w].rearrange("(c p) m -> p c m", p=P), in_=result
             )
 
         wl_pieces = [(b, c) for b in range(2) for c in range(N_TILES)]
@@ -239,78 +241,83 @@ def tile_list_bell_discriminant_kernel(
                 interleave(nc.scalar.copy, wl_bf[b][:, cols, :], wl_raw[:, b, :, cols])
 
         z0_rows = held([P, PACK, M], BF16, "z0_rows")
-        z1_rows = [held([P, PACK, w], BF16, "z1_rows%d" % j) for j, (m0, w) in enumerate(CHUNKS)]
-        for t, pieces in enumerate((0, 2, 2, 1)):
+        for t, pieces in enumerate((1, 2, 2, 1)):
             picked = pick(t, 0, M)
-            if t == 0:
-                finish_h(3)
-            finish_h(PACK + t)
+            finish_h(PACK - 1 + t)
             cast_wl(pieces)
-            combine(t, picked, z0_rows, M)
+            combine(nc.gpsimd, t, picked, z0_rows[:, t, :])
 
-        z0 = {}
-        sums = {}
+        z0_bf = held([P, M, PACK], BF16, "z0_bf")
+        z0_wd = held([P, M], U32, "z0_wd")
+        z0_sc = held([P, M], U8, "z0_sc")
+        z1_rows = held([P, PACK, WIDE], BF16, "z1_rows")
+        for t in range(PACK):
+            picked = pick(PACK + t, 0, WIDE)
+            if t == 0:
+                finish_h(SLICES - 1)
+                quantize(wl_bf[0][:], wl_wd[0][:], wl_sc[0][:])
+            elif t < PACK - 1:
+                cols = slice(HALF * (t - 1), HALF * t)
+                interleave(nc.scalar.copy, z0_bf[:, cols, :], z0_rows[:, :, cols])
+                cast_wl(1)
+            else:
+                quantize(wl_bf[1][:], wl_wd[1][:], wl_sc[1][:])
+                quantize(z0_bf[:], z0_wd[:], z0_sc[:])
+            combine(nc.gpsimd if t < PACK - 1 else nc.vector, PACK + t, picked, z1_rows[:, t, :])
 
-        def open_chunk(j):
-            m0, w = CHUNKS[j]
-            half, lo = divmod(m0, HALF)
-            for c in range(N_TILES):
-                sums[j, c] = bank(w)
-                second_product(sums[j, c], c, 0, z0[half][1][:, lo : lo + w], z0[half][2][:, lo : lo + w])
+        parts = (slice(0, HALF), slice(HALF, WIDE))
+        wide_sums = [bank(WIDE) for c in range(N_TILES)]
+        last_sums = [bank(P) for c in range(N_TILES)]
+        for c in range(N_TILES):
+            for cols in parts:
+                second_product(wide_sums[c][:, cols], c, 0, z0_wd[:, cols], z0_sc[:, cols], cols.start == 0, False)
+        for c in range(N_TILES):
+            second_product(last_sums[c][:], c, 0, z0_wd[:, WIDE:], z0_sc[:, WIDE:], True, False)
 
-        def close_chunk(j, z1):
-            m0, w = CHUNKS[j]
-            last = j == len(CHUNKS) - 1
-            tiles_a_store = 2 if last else N_TILES
-            quantize(*z1)
-            result = held([P, N_TILES, w], F32, "result%d" % j)
-            for c in range(N_TILES):
-                second_product(sums[j, c], c, 1, z1[1][:], z1[2][:])
-                if last:
-                    nc.vector.tensor_scalar(result[:, c, :], sums[j, c][:], cut_sb[:, c : c + 1], None, ALU.add)
-                else:
-                    nc.scalar.activation(
-                        out=result[:, c, :], in_=sums[j, c][:], func=ACT.Identity, bias=cut_sb[:, c : c + 1]
-                    )
-                if (c + 1) % tiles_a_store == 0:
-                    c0 = c + 1 - tiles_a_store
-                    nc.sync.dma_start(
-                        out=out[P * c0 : P * (c + 1), m0 : m0 + w].rearrange("(c p) m -> p c m", p=P),
-                        in_=result[:, c0 : c + 1, :],
-                    )
+        z1_wd = held([P, M], U32, "z1_wd")
+        z1_sc = held([P, M], U8, "z1_sc")
+        last_rows = held([P, PACK, P], BF16, "last_rows")
+        picks = []
+        for t in range(PACK):
+            if t < 2:
+                prime = work.tile([P, P], F32, name="prime", tag="prime")
+            else:
+                cols = parts[t - 2]
+                quantize(z1_bf[t - 2][:], z1_wd[:, cols], z1_sc[:, cols])
+                for c in range(N_TILES):
+                    second_product(wide_sums[c][:, cols], c, 1, z1_wd[:, cols], z1_sc[:, cols], False, t == 3)
+                prime = held([P, P], F32, "z1_bf%d" % (t - 2))
+            picks.append(pick_last(t, prime))
+            if t == 0:
+                z1_bf = []
+                for j, cols in enumerate(parts):
+                    z1_bf.append(held([P, cols.stop - cols.start, PACK], BF16, "z1_bf%d" % j))
+                    interleave(nc.scalar.copy, z1_bf[j][:], z1_rows[:, :, cols])
+            else:
+                combine_last(t - 1, picks[t - 1], last_rows[:, t - 1, :])
+        combine_last(PACK - 1, picks[PACK - 1], last_rows[:, PACK - 1, :])
 
-        z1 = None
-        waiting = []
-        for j, (m0, w) in enumerate(CHUNKS):
-            for t in range(PACK):
-                picked = pick(PACK + t, m0, w)
-                if waiting:
-                    combine(*waiting.pop())
-                if j == 0:
-                    if t == 0:
-                        quantize(wl_bf[0], wl_wd[0], wl_sc[0])
-                    if t == 1:
-                        z0[0] = group_z(z0_rows[:, :, :HALF], HALF, "z0a", nc.scalar.copy)
-                    else:
-                        cast_wl(1)
-                    if t == PACK - 1:
-                        quantize(*z0[0])
-                        open_chunk(0)
-                    combine(PACK + t, picked, z1_rows[j], w)
-                else:
-                    if t == 0:
-                        if j == 1:
-                            quantize(wl_bf[1], wl_wd[1], wl_sc[1])
-                        z1 = group_z(z1_rows[j - 1][:], CHUNKS[j - 1][1], "z1_%d" % (j - 1), nc.scalar.copy)
-                    if (j, t) == (1, 1):
-                        z0[1] = group_z(z0_rows[:, :, HALF:], HALF, "z0b", nc.scalar.copy)
-                    if t == 2:
-                        close_chunk(j - 1, z1)
-                    if (j, t) == (1, PACK - 1):
-                        quantize(*z0[1])
-                        open_chunk(1)
-                        open_chunk(2)
-                    waiting.append((PACK + t, picked, z1_rows[j], w))
-        combine(*waiting.pop())
-        j = len(CHUNKS) - 1
-        close_chunk(j, group_z(z1_rows[j][:], CHUNKS[j][1], "z1_%d" % j, nc.vector.tensor_copy))
+        wide_result = held([P, N_TILES, WIDE], F32, "wide_result")
+        for c in range(N_TILES):
+            nc.scalar.activation(
+                out=wide_result[:, c, :], in_=wide_sums[c][:], func=ACT.Identity, bias=cut_sb[:, c : c + 1]
+            )
+            if c % 2 == 1:
+                store(wide_result[:, c - 1 : c + 1, :], c - 1, 2, 0, WIDE)
+
+        last_bf = held([P, P, PACK], BF16, "last_bf")
+        interleave(nc.vector.tensor_copy, last_bf[:], last_rows[:])
+        quantize(last_bf[:], z1_wd[:, WIDE:], z1_sc[:, WIDE:])
+        last_result = [held([P, 2, P], F32, "last_result%d" % j) for j in range(2)]
+        for c in range(N_TILES):
+            second_product(last_sums[c][:], c, 1, z1_wd[:, WIDE:], z1_sc[:, WIDE:], False, True)
+        for c in range(N_TILES):
+            j, lo = divmod(c, 2)
+            if j == 0:
+                nc.vector.tensor_scalar(last_result[j][:, lo, :], last_sums[c][:], cut_sb[:, c : c + 1], None, ALU.add)
+            else:
+                nc.scalar.activation(
+                    out=last_result[j][:, lo, :], in_=last_sums[c][:], func=ACT.Identity, bias=cut_sb[:, c : c + 1]
+                )
+            if lo == 1:
+                store(last_result[j][:], 2 * j, 2, WIDE, P)

@@ -27,9 +27,8 @@ SCALE_ROWS = 32
 SLICES = H // P
 N_TILES = N // P
 HALF = M // 2
-WIDE = M - P
-EARLY_SLICES = 2
-WORK_BUFS = 5
+EARLY_SLICES = 4
+WORK_BUFS = 3
 
 
 def tile_list_bell_discriminant_kernel(
@@ -129,6 +128,12 @@ def tile_list_bell_discriminant_kernel(
         gather_words(0)
         load_w4(1, "window0")
 
+        turned = bank(P)
+        nc.tensor.transpose(turned[:], vec_rows[:], ident[:])
+        nc.scalar.copy(out=vec_cols[:], in_=turned[:, : SLICES + N_TILES])
+        minus_gain = held([P, SLICES], F32, "minus_gain")
+        nc.scalar.activation(out=minus_gain[:], in_=gain_sb, func=ACT.Copy, scale=-1.0)
+
         acc = {}
 
         def first_product(s, u, a):
@@ -165,12 +170,6 @@ def tile_list_bell_discriminant_kernel(
         order_w4(1)
         finish_h(0)
         finish_h(1)
-        turned = bank(P)
-        nc.tensor.transpose(turned[:], vec_rows[:], ident[:])
-        nc.scalar.copy(out=vec_cols[:], in_=turned[:, : SLICES + N_TILES])
-        gain_wide = held([P, PACK, P], F32, "gain_wide")
-        nc.scalar.copy(out=gain_wide[:], in_=gain_sb[:, PACK:].unsqueeze(2).to_broadcast([P, PACK, P]))
-        finish_h(2)
 
         def interleave(copy, dst, src):
             copy(
@@ -181,40 +180,40 @@ def tile_list_bell_discriminant_kernel(
         def quantize(grouped, codes, scales):
             nc.vector.quantize_mx(out=codes.bitcast(FP8X4), scales=scales, in_=grouped.rearrange("p m t -> p (m t)"))
 
-        def pick(s, m0, w):
-            cols = slice(m0 // PER_COLUMN, (m0 + w) // PER_COLUMN)
-            hum = work.tile([P, w], F32, name="hum", tag="hum")
-            prime = work.tile([P, w], F32, name="prime", tag="prime")
-            cross = work.tile([P, w], F32, name="cross", tag="cross")
-            square = work.tile([P, w], F32, name="square", tag="square")
-            nc.vector.tensor_copy(prime[:], h_sb[s][:].indirect(prime_list[:, cols]))
-            nc.vector.tensor_copy(hum[:], h_sb[s][:].indirect(hum_list[:, cols]))
-            nc.vector.tensor_tensor(cross[:], h_sb[s][:].indirect(tierce_list[:, cols]), prime[:], ALU.mult)
-            nc.scalar.activation(out=square[:], in_=hum[:], func=ACT.Square)
-            return square, cross
+        halves = (slice(0, HALF), slice(HALF, M))
+        hum, prime, square, cross, diff = {}, {}, {}, {}, {}
 
-        def combine(engine, s, picked, z_row):
-            square, cross = picked
-            diff = work.tile(list(square.shape), F32, name="diff", tag="diff")
-            engine.tensor_tensor(diff[:], square[:], cross[:], ALU.subtract)
-            nc.scalar.activation(out=z_row, in_=diff[:], func=ACT.Copy, scale=gain_sb[:, s : s + 1])
+        def entries(cols):
+            return slice(cols.start // PER_COLUMN, cols.stop // PER_COLUMN)
 
-        def pick_last(t, prime):
-            s = PACK + t
-            cols = slice(WIDE // PER_COLUMN, M // PER_COLUMN)
-            hum = work.tile([P, P], F32, name="hum", tag="hum")
-            cross = work.tile([P, P], F32, name="cross", tag="cross")
-            square = work.tile([P, P], F32, name="square", tag="square")
-            nc.vector.tensor_copy(hum[:], h_sb[s][:].indirect(hum_list[:, cols]))
-            nc.vector.tensor_tensor(prime[:], h_sb[s][:].indirect(prime_list[:, cols]), gain_wide[:, t, :], ALU.mult)
-            nc.vector.tensor_tensor(cross[:], h_sb[s][:].indirect(tierce_list[:, cols]), prime[:], ALU.mult)
-            nc.scalar.activation(out=square[:], in_=hum[:], func=ACT.Square)
-            return square, cross
+        def pick_hum(s):
+            hum[s] = held([P, M], F32, "picks%d" % s)
+            nc.vector.tensor_copy(hum[s][:], h_sb[s][:].indirect(hum_list[:]))
 
-        def combine_last(t, picked, z_row):
-            square, cross = picked
-            s = PACK + t
-            nc.vector.scalar_tensor_tensor(z_row, square[:], gain_sb[:, s : s + 1], cross[:], ALU.mult, ALU.subtract)
+        def pick_prime(s):
+            nc.vector.tensor_copy(prime[s], h_sb[s][:].indirect(prime_list[:]))
+
+        def pick_cross(s, j):
+            nc.vector.tensor_tensor(
+                cross[s, j], h_sb[s][:].indirect(tierce_list[:, entries(halves[j])]), prime[s][:, halves[j]], ALU.mult
+            )
+
+        def square_hum(s):
+            square[s] = work.tile([P, M], F32, name="square", tag="square")
+            nc.scalar.activation(out=square[s][:], in_=hum[s][:], func=ACT.Square)
+
+        def subtract(s, j):
+            if j == 0:
+                diff[s] = work.tile([P, M], F32, name="diff", tag="diff")
+            nc.gpsimd.tensor_tensor(diff[s][:, halves[j]], square[s][:, halves[j]], cross[s, j], ALU.subtract)
+
+        def scale(dst, src, s):
+            nc.scalar.activation(out=dst, in_=src, func=ACT.Copy, scale=gain_sb[:, s : s + 1])
+
+        def combine(s, j, scaled):
+            nc.vector.scalar_tensor_tensor(
+                z_rows[1][:, s - PACK, halves[j]], cross[s, j], minus_gain[:, s : s + 1], scaled, ALU.mult, ALU.add
+            )
 
         def second_product(sums, c, b, z_wd, z_sc, start, stop):
             nc.tensor.matmul_mx(
@@ -232,92 +231,92 @@ def tile_list_bell_discriminant_kernel(
                 out=out[P * c0 : P * (c0 + tiles), m0 : m0 + w].rearrange("(c p) m -> p c m", p=P), in_=result
             )
 
-        wl_pieces = [(b, c) for b in range(2) for c in range(N_TILES)]
+        def cast_wl(b, c):
+            cols = slice(P * c, P * (c + 1))
+            interleave(nc.scalar.copy, wl_bf[b][:, cols, :], wl_raw[:, b, :, cols])
 
-        def cast_wl(pieces):
-            for turn in range(pieces):
-                b, c = wl_pieces.pop(0)
-                cols = slice(P * c, P * (c + 1))
-                interleave(nc.scalar.copy, wl_bf[b][:, cols, :], wl_raw[:, b, :, cols])
+        z_rows = [held([P, PACK, M], BF16, "z_rows%d" % b) for b in range(2)]
+        z_bf = [held([P, M, PACK], BF16, "z_bf%d" % b) for b in range(2)]
+        z_wd = [held([P, M], U32, "z_wd%d" % b) for b in range(2)]
+        z_sc = [held([P, M], U8, "z_sc%d" % b) for b in range(2)]
 
-        z0_rows = held([P, PACK, M], BF16, "z0_rows")
-        for t, pieces in enumerate((1, 2, 2, 1)):
-            picked = pick(t, 0, M)
-            finish_h(PACK - 1 + t)
-            cast_wl(pieces)
-            combine(nc.gpsimd, t, picked, z0_rows[:, t, :])
+        def group_z(copy, b, cols):
+            interleave(copy, z_bf[b][:, cols, :], z_rows[b][:, :, cols])
 
-        z0_bf = held([P, M, PACK], BF16, "z0_bf")
-        z0_wd = held([P, M], U32, "z0_wd")
-        z0_sc = held([P, M], U8, "z0_sc")
-        z1_rows = held([P, PACK, WIDE], BF16, "z1_rows")
-        for t in range(PACK):
-            picked = pick(PACK + t, 0, WIDE)
-            if t == 0:
-                finish_h(SLICES - 1)
-                quantize(wl_bf[0][:], wl_wd[0][:], wl_sc[0][:])
-            elif t < PACK - 1:
-                cols = slice(HALF * (t - 1), HALF * t)
-                interleave(nc.scalar.copy, z0_bf[:, cols, :], z0_rows[:, :, cols])
-                cast_wl(1)
+        def spare(s, turn):
+            if s <= PACK:
+                cast_wl((s - 1) % 2, 2 * ((s - 1) // 2) + turn)
             else:
-                quantize(wl_bf[1][:], wl_wd[1][:], wl_sc[1][:])
-                quantize(z0_bf[:], z0_wd[:], z0_sc[:])
-            combine(nc.gpsimd if t < PACK - 1 else nc.vector, PACK + t, picked, z1_rows[:, t, :])
+                c = 2 * (s - PACK - 1) + turn
+                group_z(nc.scalar.copy, 0, slice(P * c, P * (c + 1)))
 
-        parts = (slice(0, HALF), slice(HALF, WIDE))
-        wide_sums = [bank(WIDE) for c in range(N_TILES)]
-        last_sums = [bank(P) for c in range(N_TILES)]
-        for c in range(N_TILES):
-            for cols in parts:
-                second_product(wide_sums[c][:, cols], c, 0, z0_wd[:, cols], z0_sc[:, cols], cols.start == 0, False)
-        for c in range(N_TILES):
-            second_product(last_sums[c][:], c, 0, z0_wd[:, WIDE:], z0_sc[:, WIDE:], True, False)
+        first_prime = held([P, M], F32, "first_prime")
+        prime[0] = first_prime[:]
+        pick_hum(0)
+        pick_prime(0)
+        square_hum(0)
+        finish_h(2)
+        last = SLICES - 1
+        for s in range(1, SLICES):
+            pick_hum(s)
+            if s in (PACK + 1, PACK + 2):
+                b = s - PACK - 1
+                quantize(wl_bf[b][:], wl_wd[b][:], wl_sc[b][:])
+            picks = held([P, 2 * M], F32, "picks%d" % (s - 1))
+            cross[s - 1, 0], prime[s], cross[s - 1, 1] = picks[:, :HALF], picks[:, HALF : HALF + M], picks[:, HALF + M :]
+            pick_cross(s - 1, 0)
+            subtract(s - 1, 0)
+            pick_prime(s)
+            if s == last:
+                break
+            pick_cross(s - 1, 1)
+            subtract(s - 1, 1)
+            square_hum(s)
+            if s >= 2:
+                scale(z_rows[(s - 2) // PACK][:, (s - 2) % PACK, :], diff[s - 2][:], s - 2)
+            spare(s, 0)
+            if s + 2 < SLICES:
+                finish_h(s + 2)
+            spare(s, 1)
 
-        z1_wd = held([P, M], U32, "z1_wd")
-        z1_sc = held([P, M], U8, "z1_sc")
-        last_rows = held([P, PACK, P], BF16, "last_rows")
-        picks = []
-        for t in range(PACK):
-            if t < 2:
-                prime = work.tile([P, P], F32, name="prime", tag="prime")
-            else:
-                cols = parts[t - 2]
-                quantize(z1_bf[t - 2][:], z1_wd[:, cols], z1_sc[:, cols])
-                for c in range(N_TILES):
-                    second_product(wide_sums[c][:, cols], c, 1, z1_wd[:, cols], z1_sc[:, cols], False, t == 3)
-                prime = held([P, P], F32, "z1_bf%d" % (t - 2))
-            picks.append(pick_last(t, prime))
-            if t == 0:
-                z1_bf = []
-                for j, cols in enumerate(parts):
-                    z1_bf.append(held([P, cols.stop - cols.start, PACK], BF16, "z1_bf%d" % j))
-                    interleave(nc.scalar.copy, z1_bf[j][:], z1_rows[:, :, cols])
-            else:
-                combine_last(t - 1, picks[t - 1], last_rows[:, t - 1, :])
-        combine_last(PACK - 1, picks[PACK - 1], last_rows[:, PACK - 1, :])
-
-        wide_result = held([P, N_TILES, WIDE], F32, "wide_result")
-        for c in range(N_TILES):
-            nc.scalar.activation(
-                out=wide_result[:, c, :], in_=wide_sums[c][:], func=ACT.Identity, bias=cut_sb[:, c : c + 1]
-            )
-            if c % 2 == 1:
-                store(wide_result[:, c - 1 : c + 1, :], c - 1, 2, 0, WIDE)
-
-        last_bf = held([P, P, PACK], BF16, "last_bf")
-        interleave(nc.vector.tensor_copy, last_bf[:], last_rows[:])
-        quantize(last_bf[:], z1_wd[:, WIDE:], z1_sc[:, WIDE:])
-        last_result = [held([P, 2, P], F32, "last_result%d" % j) for j in range(2)]
-        for c in range(N_TILES):
-            second_product(last_sums[c][:], c, 1, z1_wd[:, WIDE:], z1_sc[:, WIDE:], False, True)
-        for c in range(N_TILES):
-            j, lo = divmod(c, 2)
-            if j == 0:
-                nc.vector.tensor_scalar(last_result[j][:, lo, :], last_sums[c][:], cut_sb[:, c : c + 1], None, ALU.add)
-            else:
-                nc.scalar.activation(
-                    out=last_result[j][:, lo, :], in_=last_sums[c][:], func=ACT.Identity, bias=cut_sb[:, c : c + 1]
-                )
-            if lo == 1:
-                store(last_result[j][:], 2 * j, 2, WIDE, P)
+        quantize(z_bf[0][:], z_wd[0][:], z_sc[0][:])
+        sums = [[bank(HALF) for c in range(N_TILES)] for j in range(2)]
+        for j in range(2):
+            for c in range(N_TILES):
+                second_product(sums[j][c][:], c, 0, z_wd[0][:, halves[j]], z_sc[0][:, halves[j]], True, False)
+        square_hum(last)
+        scale(z_rows[1][:, last - 2 - PACK, :], diff[last - 2][:], last - 2)
+        scaled_last = held([P, M], F32, "scaled_last")
+        scale(scaled_last[:], square[last][:], last)
+        scale(z_rows[1][:, last - 1 - PACK, halves[0]], diff[last - 1][:, halves[0]], last - 1)
+        scaled_half = held([P, HALF], F32, "scaled_half")
+        scale(scaled_half[:], square[last - 1][:, halves[1]], last - 1)
+        picks = held([P, M], F32, "picks%d" % last)
+        cross[last, 0], cross[last - 1, 1] = picks[:, halves[0]], picks[:, halves[1]]
+        pick_cross(last, 0)
+        pick_cross(last - 1, 1)
+        combine(last, 0, scaled_last[:, halves[0]])
+        group_z(nc.scalar.copy, 1, halves[0])
+        last_cross = work.tile([P, HALF], F32, name="square", tag="square")
+        cross[last, 1] = last_cross[:]
+        pick_cross(last, 1)
+        combine(last - 1, 1, scaled_half[:])
+        combine(last, 1, scaled_last[:, halves[1]])
+        group_z(nc.scalar.copy, 1, slice(HALF, HALF + P))
+        group_z(nc.vector.tensor_copy, 1, slice(HALF + P, M))
+        for j in range(2):
+            cols = halves[j]
+            quantize(z_bf[1][:, cols, :], z_wd[1][:, cols], z_sc[1][:, cols])
+            for c in range(N_TILES):
+                second_product(sums[j][c][:], c, 1, z_wd[1][:, cols], z_sc[1][:, cols], False, True)
+            for pair in range(2):
+                result = held([P, 2, HALF], F32, "result%d%d" % (j, pair))
+                for lo in range(2):
+                    c = 2 * pair + lo
+                    if (j, pair) == (1, 0):
+                        nc.vector.tensor_scalar(result[:, lo, :], sums[j][c][:], cut_sb[:, c : c + 1], None, ALU.add)
+                    else:
+                        nc.scalar.activation(
+                            out=result[:, lo, :], in_=sums[j][c][:], func=ACT.Identity, bias=cut_sb[:, c : c + 1]
+                        )
+                store(result[:], 2 * pair, 2, cols.start, HALF)

@@ -28,7 +28,7 @@ SLICES = H // P
 N_TILES = N // P
 HALF = M // 2
 EARLY_SLICES = 4
-WORK_BUFS = 3
+WORK_BUFS = 4
 
 
 def tile_list_bell_discriminant_kernel(
@@ -181,38 +181,38 @@ def tile_list_bell_discriminant_kernel(
             nc.vector.quantize_mx(out=codes.bitcast(FP8X4), scales=scales, in_=grouped.rearrange("p m t -> p (m t)"))
 
         halves = (slice(0, HALF), slice(HALF, M))
-        hum, prime, square, cross, diff = {}, {}, {}, {}, {}
+        hum, prime, square, diff = {}, {}, {}, {}
 
         def entries(cols):
             return slice(cols.start // PER_COLUMN, cols.stop // PER_COLUMN)
 
         def pick_hum(s):
-            hum[s] = held([P, M], F32, "picks%d" % s)
+            hum[s] = work.tile([P, M], F32, name="hum", tag="hum")
             nc.vector.tensor_copy(hum[s][:], h_sb[s][:].indirect(hum_list[:]))
 
         def pick_prime(s):
-            nc.vector.tensor_copy(prime[s], h_sb[s][:].indirect(prime_list[:]))
+            prime[s] = work.tile([P, M], F32, name="prime", tag="prime")
+            nc.vector.tensor_copy(prime[s][:], h_sb[s][:].indirect(prime_list[:]))
 
-        def pick_cross(s, j):
-            nc.vector.tensor_tensor(
-                cross[s, j], h_sb[s][:].indirect(tierce_list[:, entries(halves[j])]), prime[s][:, halves[j]], ALU.mult
-            )
+        def pick_cross(s, cols, dst):
+            nc.vector.tensor_tensor(dst, h_sb[s][:].indirect(tierce_list[:, entries(cols)]), prime[s][:, cols], ALU.mult)
 
         def square_hum(s):
             square[s] = work.tile([P, M], F32, name="square", tag="square")
             nc.scalar.activation(out=square[s][:], in_=hum[s][:], func=ACT.Square)
 
-        def subtract(s, j):
-            if j == 0:
-                diff[s] = work.tile([P, M], F32, name="diff", tag="diff")
-            nc.gpsimd.tensor_tensor(diff[s][:, halves[j]], square[s][:, halves[j]], cross[s, j], ALU.subtract)
+        def cross_and_subtract(s, cols):
+            cross = work.tile([P, cols.stop], F32, name="cross", tag="cross")
+            diff[s] = work.tile([P, cols.stop], F32, name="diff", tag="diff")
+            pick_cross(s, cols, cross[:])
+            nc.gpsimd.tensor_tensor(diff[s][:], square[s][:, cols], cross[:], ALU.subtract)
 
         def scale(dst, src, s):
             nc.scalar.activation(out=dst, in_=src, func=ACT.Copy, scale=gain_sb[:, s : s + 1])
 
-        def combine(s, j, scaled):
+        def combine(s, cols, cross, scaled):
             nc.vector.scalar_tensor_tensor(
-                z_rows[1][:, s - PACK, halves[j]], cross[s, j], minus_gain[:, s : s + 1], scaled, ALU.mult, ALU.add
+                z_rows[1][:, s - PACK, cols], cross, minus_gain[:, s : s + 1], scaled, ALU.mult, ALU.add
             )
 
         def second_product(sums, c, b, z_wd, z_sc, start, stop):
@@ -245,78 +245,79 @@ def tile_list_bell_discriminant_kernel(
 
         def spare(s, turn):
             if s <= PACK:
-                cast_wl((s - 1) % 2, 2 * ((s - 1) // 2) + turn)
+                cast_wl((s - 1) // 2, 2 * ((s - 1) % 2) + turn)
             else:
                 c = 2 * (s - PACK - 1) + turn
                 group_z(nc.scalar.copy, 0, slice(P * c, P * (c + 1)))
 
-        first_prime = held([P, M], F32, "first_prime")
-        prime[0] = first_prime[:]
-        pick_hum(0)
-        pick_prime(0)
-        square_hum(0)
-        finish_h(2)
         last = SLICES - 1
-        for s in range(1, SLICES):
-            pick_hum(s)
-            if s in (PACK + 1, PACK + 2):
-                b = s - PACK - 1
-                quantize(wl_bf[b][:], wl_wd[b][:], wl_sc[b][:])
-            picks = held([P, 2 * M], F32, "picks%d" % (s - 1))
-            cross[s - 1, 0], prime[s], cross[s - 1, 1] = picks[:, :HALF], picks[:, HALF : HALF + M], picks[:, HALF + M :]
-            pick_cross(s - 1, 0)
-            subtract(s - 1, 0)
+        for s in range(last):
             pick_prime(s)
-            if s == last:
-                break
-            pick_cross(s - 1, 1)
-            subtract(s - 1, 1)
+            pick_hum(s)
             square_hum(s)
-            if s >= 2:
-                scale(z_rows[(s - 2) // PACK][:, (s - 2) % PACK, :], diff[s - 2][:], s - 2)
-            spare(s, 0)
+            cross_and_subtract(s, slice(0, M if s < last - 1 else HALF))
             if s + 2 < SLICES:
                 finish_h(s + 2)
-            spare(s, 1)
+            if s >= 1:
+                scale(z_rows[(s - 1) // PACK][:, (s - 1) % PACK, :], diff[s - 1][:], s - 1)
+                spare(s, 0)
+                spare(s, 1)
+            if s in (2, PACK):
+                b = s // 2 - 1
+                quantize(wl_bf[b][:], wl_wd[b][:], wl_sc[b][:])
 
+        pick_hum(last)
+        pick_prime(last)
         quantize(z_bf[0][:], z_wd[0][:], z_sc[0][:])
-        sums = [[bank(HALF) for c in range(N_TILES)] for j in range(2)]
-        for j in range(2):
-            for c in range(N_TILES):
-                second_product(sums[j][c][:], c, 0, z_wd[0][:, halves[j]], z_sc[0][:, halves[j]], True, False)
+        chunks = (halves[0], slice(HALF, HALF + P), slice(HALF + P, M))
+        sums = {}
+        for j, cols in enumerate(chunks):
+            width = cols.stop - cols.start
+            shared = HALF // width
+            for c0 in range(0, N_TILES, shared):
+                group = bank(HALF)
+                for lo in range(shared):
+                    sums[j, c0 + lo] = group[:, width * lo : width * (lo + 1)]
+                    second_product(sums[j, c0 + lo], c0 + lo, 0, z_wd[0][:, cols], z_sc[0][:, cols], lo == 0, False)
         square_hum(last)
-        scale(z_rows[1][:, last - 2 - PACK, :], diff[last - 2][:], last - 2)
         scaled_last = held([P, M], F32, "scaled_last")
         scale(scaled_last[:], square[last][:], last)
-        scale(z_rows[1][:, last - 1 - PACK, halves[0]], diff[last - 1][:, halves[0]], last - 1)
+        scale(z_rows[1][:, last - 1 - PACK, halves[0]], diff[last - 1][:], last - 1)
         scaled_half = held([P, HALF], F32, "scaled_half")
         scale(scaled_half[:], square[last - 1][:, halves[1]], last - 1)
-        picks = held([P, M], F32, "picks%d" % last)
-        cross[last, 0], cross[last - 1, 1] = picks[:, halves[0]], picks[:, halves[1]]
-        pick_cross(last, 0)
-        pick_cross(last - 1, 1)
-        combine(last, 0, scaled_last[:, halves[0]])
-        group_z(nc.scalar.copy, 1, halves[0])
-        last_cross = work.tile([P, HALF], F32, name="square", tag="square")
-        cross[last, 1] = last_cross[:]
-        pick_cross(last, 1)
-        combine(last - 1, 1, scaled_half[:])
-        combine(last, 1, scaled_last[:, halves[1]])
-        group_z(nc.scalar.copy, 1, slice(HALF, HALF + P))
-        group_z(nc.vector.tensor_copy, 1, slice(HALF + P, M))
-        for j in range(2):
-            cols = halves[j]
+
+        def close(j, on_vector):
+            cols = chunks[j]
+            width = cols.stop - cols.start
+            shared = HALF // width
             quantize(z_bf[1][:, cols, :], z_wd[1][:, cols], z_sc[1][:, cols])
             for c in range(N_TILES):
-                second_product(sums[j][c][:], c, 1, z_wd[1][:, cols], z_sc[1][:, cols], False, True)
-            for pair in range(2):
-                result = held([P, 2, HALF], F32, "result%d%d" % (j, pair))
+                second_product(sums[j, c], c, 1, z_wd[1][:, cols], z_sc[1][:, cols], False, c % shared == shared - 1)
+            for c0 in range(0, N_TILES, 2):
+                result = held([P, 2, width], F32, "result%d%d" % (j, c0))
                 for lo in range(2):
-                    c = 2 * pair + lo
-                    if (j, pair) == (1, 0):
-                        nc.vector.tensor_scalar(result[:, lo, :], sums[j][c][:], cut_sb[:, c : c + 1], None, ALU.add)
+                    c = c0 + lo
+                    if on_vector:
+                        nc.vector.tensor_scalar(result[:, lo, :], sums[j, c], cut_sb[:, c : c + 1], None, ALU.add)
                     else:
                         nc.scalar.activation(
-                            out=result[:, lo, :], in_=sums[j][c][:], func=ACT.Identity, bias=cut_sb[:, c : c + 1]
+                            out=result[:, lo, :], in_=sums[j, c], func=ACT.Identity, bias=cut_sb[:, c : c + 1]
                         )
-                store(result[:], 2 * pair, 2, cols.start, HALF)
+                store(result[:], c0, 2, cols.start, width)
+
+        end_cross = [held([P, HALF], F32, "end_cross%d" % i) for i in range(2)]
+        pick_cross(last, halves[0], end_cross[0][:])
+        pick_cross(last - 1, halves[1], end_cross[1][:])
+        combine(last, halves[0], end_cross[0][:], scaled_last[:, halves[0]])
+        group_z(nc.scalar.copy, 1, halves[0])
+        combine(last - 1, halves[1], end_cross[1][:], scaled_half[:])
+        last_cross = held([P, HALF], F32, "end_cross0")
+        for j in (1, 2):
+            pick_cross(last, chunks[j], last_cross[:, P * (j - 1) : P * j])
+        for j in (1, 2):
+            combine(last, chunks[j], last_cross[:, P * (j - 1) : P * j], scaled_last[:, chunks[j]])
+        group_z(nc.scalar.copy, 1, chunks[1])
+        close(0, False)
+        group_z(nc.vector.tensor_copy, 1, chunks[2])
+        close(2, True)
+        close(1, False)

@@ -27,7 +27,6 @@ SCALE_ROWS = 32
 SLICES = H // P
 N_TILES = N // P
 HALF = M // 2
-EARLY_SLICES = 4
 WORK_BUFS = 4
 
 
@@ -39,13 +38,13 @@ def tile_list_bell_discriminant_kernel(
         lists = ctx.enter_context(tc.tile_pool(name="lists", bufs=1))
         keep = ctx.enter_context(tc.tile_pool(name="keep", bufs=1))
         work = ctx.enter_context(tc.tile_pool(name="work", bufs=WORK_BUFS))
-        psum = ctx.enter_context(tc.psum_pool(name="psum", bufs=8))
+        psum = [ctx.enter_context(tc.psum_pool(name="psum%d" % i, bufs=4)) for i in range(2)]
 
         def held(shape, dtype, name):
             return keep.tile(shape, dtype, name=name, align_bytes=64)
 
-        def bank(width):
-            return psum.tile([P, width], F32, name="bank", tag="bank")
+        def bank(width, pool):
+            return psum[pool].tile([P, width], F32, name="bank", tag="bank")
 
         offs_sb = lists.tile([P, S // PER_COLUMN], U16, name="offs_sb")
         pos_sb = [lists.tile([P, M // PER_COLUMN], U16, name="pos_sb%d" % i) for i in range(3)]
@@ -128,7 +127,7 @@ def tile_list_bell_discriminant_kernel(
         gather_words(0)
         load_w4(1, "window0")
 
-        turned = bank(P)
+        turned = bank(P, 1)
         nc.tensor.transpose(turned[:], vec_rows[:], ident[:])
         nc.scalar.copy(out=vec_cols[:], in_=turned[:, : SLICES + N_TILES])
         minus_gain = held([P, SLICES], F32, "minus_gain")
@@ -136,39 +135,57 @@ def tile_list_bell_discriminant_kernel(
 
         acc = {}
 
-        def first_product(s, u, a):
+        def first_product(part, a):
+            s, j0, width = part
             b, t = divmod(s, PACK)
+            u, lo = divmod(j0, BANK)
             if a == 0:
-                acc[s, u] = bank(BANK)
-            nc.tensor.matmul_mx(
-                out=acc[s, u][:],
-                lhsT=w4_wd[b][:, a, 2 * P * t : 2 * P * (t + 1)].bitcast(FP4X4),
-                lhsT_scale=planes[a][:, S + P * s : S + P * (s + 1)],
-                rhs=v_wd[a][u][:].bitcast(FP8X4),
-                rhs_scale=planes[a][:, BANK * u : BANK * (u + 1)],
-                start=(a == 0),
-                stop=(a == 1),
-            )
+                acc[part] = bank(width, 0)
+            n = BANK if width == BANK else P
+            for j in range(0, width, n):
+                nc.tensor.matmul_mx(
+                    out=acc[part][:, j : j + n],
+                    lhsT=w4_wd[b][:, a, 2 * P * t : 2 * P * (t + 1)].bitcast(FP4X4),
+                    lhsT_scale=planes[a][:, S + P * s : S + P * (s + 1)],
+                    rhs=v_wd[a][u][:, lo + j : lo + j + n].bitcast(FP8X4),
+                    rhs_scale=planes[a][:, j0 + j : j0 + j + n],
+                    start=(a == 0 and j == 0),
+                    stop=(a == 1 and j + n == width),
+                )
+
+        def empty(part, copy):
+            s, j0, width = part
+            copy(out=h_sb[s][:, j0 : j0 + width], in_=acc[part][:])
 
         def finish_h(s):
-            for u in range(2):
-                if s >= EARLY_SLICES:
-                    first_product(s, u, 0)
-                first_product(s, u, 1)
-                copy = nc.vector.tensor_copy if (s, u) == (0, 1) else nc.scalar.copy
-                copy(out=h_sb[s][:, BANK * u : BANK * (u + 1)], in_=acc[s, u][:])
+            for j0 in (0, BANK):
+                part = (s, j0, BANK)
+                if part not in done:
+                    if part not in acc:
+                        first_product(part, 0)
+                    first_product(part, 1)
+                if part not in emptied:
+                    empty(part, nc.scalar.copy)
 
-        for s in range(EARLY_SLICES):
-            for u in range(2):
-                first_product(s, u, 0)
+        firsts = [(s, 0, BANK) for s in range(2)]
+        seconds = [(0, BANK, HALF), (0, BANK + HALF, HALF)]
+        for part in firsts + seconds:
+            first_product(part, 0)
         gather_words(1)
         wl_raw = held([P, 2, PACK, N], F32, "window1")
         for b in range(2):
             rows = wl[PASS * b : PASS * (b + 1), :].rearrange("(g t i) n -> t g i n", t=PACK, i=RUN)
             for t in range(PACK):
                 nc.sync.dma_start(out=wl_raw[:, b, t, :], in_=rows[t])
+        for part in firsts + seconds:
+            first_product(part, 1)
+        done = firsts + seconds
+        emptied = done
+        empty(firsts[0], nc.scalar.copy)
+        empty(firsts[1], nc.scalar.copy)
+        empty(seconds[0], nc.scalar.copy)
+        empty(seconds[1], nc.vector.tensor_copy)
         order_w4(1)
-        finish_h(0)
         finish_h(1)
 
         def interleave(copy, dst, src):
@@ -275,7 +292,7 @@ def tile_list_bell_discriminant_kernel(
             width = cols.stop - cols.start
             shared = HALF // width
             for c0 in range(0, N_TILES, shared):
-                group = bank(HALF)
+                group = bank(HALF, min(j, 1))
                 for lo in range(shared):
                     sums[j, c0 + lo] = group[:, width * lo : width * (lo + 1)]
                     second_product(sums[j, c0 + lo], c0 + lo, 0, z_wd[0][:, cols], z_sc[0][:, cols], lo == 0, False)
@@ -286,13 +303,16 @@ def tile_list_bell_discriminant_kernel(
         scaled_half = held([P, HALF], F32, "scaled_half")
         scale(scaled_half[:], square[last - 1][:, halves[1]], last - 1)
 
-        def close(j, on_vector):
+        def multiply(j):
             cols = chunks[j]
-            width = cols.stop - cols.start
-            shared = HALF // width
+            shared = HALF // (cols.stop - cols.start)
             quantize(z_bf[1][:, cols, :], z_wd[1][:, cols], z_sc[1][:, cols])
             for c in range(N_TILES):
                 second_product(sums[j, c], c, 1, z_wd[1][:, cols], z_sc[1][:, cols], False, c % shared == shared - 1)
+
+        def leave(j, on_vector):
+            cols = chunks[j]
+            width = cols.stop - cols.start
             for c0 in range(0, N_TILES, 2):
                 result = held([P, 2, width], F32, "result%d%d" % (j, c0))
                 for lo in range(2):
@@ -316,8 +336,11 @@ def tile_list_bell_discriminant_kernel(
             pick_cross(last, chunks[j], last_cross[:, P * (j - 1) : P * j])
         for j in (1, 2):
             combine(last, chunks[j], last_cross[:, P * (j - 1) : P * j], scaled_last[:, chunks[j]])
-        group_z(nc.scalar.copy, 1, chunks[1])
-        close(0, False)
-        group_z(nc.vector.tensor_copy, 1, chunks[2])
-        close(2, True)
-        close(1, False)
+        multiply(0)
+        leave(0, False)
+        for j in (1, 2):
+            group_z(nc.vector.tensor_copy, 1, chunks[j])
+        for j in (1, 2):
+            multiply(j)
+        leave(1, False)
+        leave(2, True)

@@ -27,7 +27,7 @@ SCALE_ROWS = 32
 SLICES = H // P
 N_TILES = N // P
 HALF = M // 2
-WORK_BUFS = 4
+WORK_BUFS = 2
 
 
 def tile_list_bell_discriminant_kernel(
@@ -64,7 +64,7 @@ def tile_list_bell_discriminant_kernel(
         gain_sb = vec_cols[:, :SLICES]
         cut_sb = vec_cols[:, SLICES:]
         wl_bf = [held([P, N, PACK], BF16, "wl_bf%d" % b) for b in range(2)]
-        wl_wd = [held([P, N], U32, "wl_wd%d" % b) for b in range(2)]
+        wl_wd = {0: held([P, N], U32, "wl_wd0")}
         wl_sc = [held([P, N], U8, "wl_sc%d" % b) for b in range(2)]
         h_sb = [held([P, S], F32, "h_sb%d" % s) for s in range(SLICES)]
 
@@ -187,7 +187,6 @@ def tile_list_bell_discriminant_kernel(
         empty(seconds[1], nc.vector.tensor_copy)
         order_w4(1)
         finish_h(1)
-
         def interleave(copy, dst, src):
             copy(
                 out=dst.rearrange("p (c i) t -> p c t i", i=4),
@@ -198,38 +197,28 @@ def tile_list_bell_discriminant_kernel(
             nc.vector.quantize_mx(out=codes.bitcast(FP8X4), scales=scales, in_=grouped.rearrange("p m t -> p (m t)"))
 
         halves = (slice(0, HALF), slice(HALF, M))
-        hum, prime, square, diff = {}, {}, {}, {}
 
         def entries(cols):
             return slice(cols.start // PER_COLUMN, cols.stop // PER_COLUMN)
 
-        def pick_hum(s):
-            hum[s] = work.tile([P, M], F32, name="hum", tag="hum")
-            nc.vector.tensor_copy(hum[s][:], h_sb[s][:].indirect(hum_list[:]))
+        def pair_tile(name):
+            return work.tile([P, 2, M], F32, name=name, tag=name)
 
-        def pick_prime(s):
-            prime[s] = work.tile([P, M], F32, name="prime", tag="prime")
-            nc.vector.tensor_copy(prime[s][:], h_sb[s][:].indirect(prime_list[:]))
+        def pick(dst, s, picks):
+            nc.vector.tensor_copy(dst, h_sb[s][:].indirect(picks[:]))
 
-        def pick_cross(s, cols, dst):
-            nc.vector.tensor_tensor(dst, h_sb[s][:].indirect(tierce_list[:, entries(cols)]), prime[s][:, cols], ALU.mult)
+        def pick_cross(dst, s, cols, prime):
+            nc.vector.tensor_tensor(dst, h_sb[s][:].indirect(tierce_list[:, entries(cols)]), prime, ALU.mult)
 
-        def square_hum(s):
-            square[s] = work.tile([P, M], F32, name="square", tag="square")
-            nc.scalar.activation(out=square[s][:], in_=hum[s][:], func=ACT.Square)
-
-        def cross_and_subtract(s, cols):
-            cross = work.tile([P, cols.stop], F32, name="cross", tag="cross")
-            diff[s] = work.tile([P, cols.stop], F32, name="diff", tag="diff")
-            pick_cross(s, cols, cross[:])
-            nc.gpsimd.tensor_tensor(diff[s][:], square[s][:, cols], cross[:], ALU.subtract)
+        def square_of(dst, src):
+            nc.scalar.activation(out=dst, in_=src, func=ACT.Square)
 
         def scale(dst, src, s):
             nc.scalar.activation(out=dst, in_=src, func=ACT.Copy, scale=gain_sb[:, s : s + 1])
 
         def combine(s, cols, cross, scaled):
             nc.vector.scalar_tensor_tensor(
-                z_rows[1][:, s - PACK, cols], cross, minus_gain[:, s : s + 1], scaled, ALU.mult, ALU.add
+                z1_part(cols)[:, s - PACK, :], cross, minus_gain[:, s : s + 1], scaled, ALU.mult, ALU.add
             )
 
         def second_product(sums, c, b, z_wd, z_sc, start, stop):
@@ -252,57 +241,73 @@ def tile_list_bell_discriminant_kernel(
             cols = slice(P * c, P * (c + 1))
             interleave(nc.scalar.copy, wl_bf[b][:, cols, :], wl_raw[:, b, :, cols])
 
-        z_rows = [held([P, PACK, M], BF16, "z_rows%d" % b) for b in range(2)]
+        z0_rows = held([P, PACK, M], BF16, "z0_rows")
+        z1_rows = [held([P, PACK, HALF], BF16, "z1_rows%d" % j) for j in range(2)]
         z_bf = [held([P, M, PACK], BF16, "z_bf%d" % b) for b in range(2)]
-        z_wd = [held([P, M], U32, "z_wd%d" % b) for b in range(2)]
+        z_wd = {1: held([P, M], U32, "z_wd1")}
         z_sc = [held([P, M], U8, "z_sc%d" % b) for b in range(2)]
 
-        def group_z(copy, b, cols):
-            interleave(copy, z_bf[b][:, cols, :], z_rows[b][:, :, cols])
+        def z1_part(cols):
+            j = cols.start // HALF
+            return z1_rows[j][:, :, cols.start - HALF * j : cols.stop - HALF * j]
 
-        def spare(s, turn):
-            if s <= PACK:
-                cast_wl((s - 1) // 2, 2 * ((s - 1) % 2) + turn)
+        whole = slice(0, M)
+        diff = {}
+
+        def apply_gain(s):
+            if s < PACK:
+                scale(z0_rows[:, s, :], diff[s][:], s)
             else:
-                c = 2 * (s - PACK - 1) + turn
-                group_z(nc.scalar.copy, 0, slice(P * c, P * (c + 1)))
+                for cols in halves:
+                    scale(z1_part(cols)[:, s - PACK, :], diff[s][:, cols], s)
 
-        last = SLICES - 1
-        for s in range(last):
-            pick_prime(s)
-            pick_hum(s)
-            square_hum(s)
-            cross_and_subtract(s, slice(0, M if s < last - 1 else HALF))
-            if s + 2 < SLICES:
-                finish_h(s + 2)
-            if s >= 1:
-                scale(z_rows[(s - 1) // PACK][:, (s - 1) % PACK, :], diff[s - 1][:], s - 1)
-                spare(s, 0)
-                spare(s, 1)
-            if s in (2, PACK):
-                b = s // 2 - 1
-                quantize(wl_bf[b][:], wl_wd[b][:], wl_sc[b][:])
+        def picks_of(s0):
+            picks = held([P, 2, 2, M], F32, "after_diff%d" % (s0 - 3))
+            return picks[:, 0], picks[:, 1]
 
-        pick_hum(last)
-        pick_prime(last)
-        quantize(z_bf[0][:], z_wd[0][:], z_sc[0][:])
-        chunks = (halves[0], slice(HALF, HALF + P), slice(HALF + P, M))
-        sums = {}
-        for j, cols in enumerate(chunks):
-            width = cols.stop - cols.start
-            shared = HALF // width
-            for c0 in range(0, N_TILES, shared):
-                group = bank(HALF, min(j, 1))
-                for lo in range(shared):
-                    sums[j, c0 + lo] = group[:, width * lo : width * (lo + 1)]
-                    second_product(sums[j, c0 + lo], c0 + lo, 0, z_wd[0][:, cols], z_sc[0][:, cols], lo == 0, False)
-        square_hum(last)
-        scaled_last = held([P, M], F32, "scaled_last")
-        scale(scaled_last[:], square[last][:], last)
-        scale(z_rows[1][:, last - 1 - PACK, halves[0]], diff[last - 1][:], last - 1)
-        scaled_half = held([P, HALF], F32, "scaled_half")
-        scale(scaled_half[:], square[last - 1][:, halves[1]], last - 1)
+        finish_h(2)
+        for s0 in range(0, SLICES - 2, 2):
+            hum, prime = picks_of(s0)
+            square = pair_tile("square")
+            for i in range(2):
+                pick(prime[:, i, :], s0 + i, prime_list)
+                pick(hum[:, i, :], s0 + i, hum_list)
+            square_of(square[:, 0, :], hum[:, 0, :])
+            if s0 > 0:
+                apply_gain(s0 - 2)
+                apply_gain(s0 - 1)
+            finish_h(s0 + 3)
+            square_of(square[:, 1, :], hum[:, 1, :])
+            if s0 + 4 < SLICES:
+                finish_h(s0 + 4)
+            cross = held([P, 2, M], F32, "after_diff%d" % (s0 - 2))
+            for i in range(2):
+                pick_cross(cross[:, i, :], s0 + i, whole, prime[:, i, :])
+            for i in range(2):
+                diff[s0 + i] = held([P, M], F32, "after_diff%d" % (s0 + i))
+                nc.gpsimd.tensor_tensor(diff[s0 + i][:], square[:, i, :], cross[:, i, :], ALU.subtract)
+            if s0 < PACK:
+                b = s0 // 2
+                for c in range(N_TILES):
+                    cast_wl(b, c)
+                if b == 0:
+                    quantize(wl_bf[0][:], wl_wd[0][:], wl_sc[0][:])
+            else:
+                for c in range(M // P):
+                    cols = slice(P * c, P * (c + 1))
+                    interleave(nc.scalar.copy, z_bf[0][:, cols, :], z0_rows[:, :, cols])
 
+        s0 = SLICES - 2
+        hum, prime = picks_of(s0)
+        square, scaled = held([P, 2, M], F32, "last_square"), pair_tile("scaled")
+        for dst, picks in ((hum, hum_list), (prime, prime_list)):
+            for i in range(2):
+                pick(dst[:, i, :], s0 + i, picks)
+        for i in range(2):
+            square_of(square[:, i, :], hum[:, i, :])
+            scale(scaled[:, i, :], square[:, i, :], s0 + i)
+        apply_gain(s0 - 2)
+        apply_gain(s0 - 1)
         def multiply(j):
             cols = chunks[j]
             shared = HALF // (cols.stop - cols.start)
@@ -325,21 +330,38 @@ def tile_list_bell_discriminant_kernel(
                         )
                 store(result[:], c0, 2, cols.start, width)
 
-        end_cross = [held([P, HALF], F32, "end_cross%d" % i) for i in range(2)]
-        pick_cross(last, halves[0], end_cross[0][:])
-        pick_cross(last - 1, halves[1], end_cross[1][:])
-        combine(last, halves[0], end_cross[0][:], scaled_last[:, halves[0]])
-        group_z(nc.scalar.copy, 1, halves[0])
-        combine(last - 1, halves[1], end_cross[1][:], scaled_half[:])
-        last_cross = held([P, HALF], F32, "end_cross0")
-        for j in (1, 2):
-            pick_cross(last, chunks[j], last_cross[:, P * (j - 1) : P * j])
-        for j in (1, 2):
-            combine(last, chunks[j], last_cross[:, P * (j - 1) : P * j], scaled_last[:, chunks[j]])
+        cross = held([P, 2, HALF], F32, "end_cross")
+        for i in range(2):
+            pick_cross(cross[:, i, :], s0 + i, halves[0], prime[:, i, halves[0]])
+        for i in range(2):
+            combine(s0 + i, halves[0], cross[:, i, :], scaled[:, i, halves[0]])
+        interleave(nc.scalar.copy, z_bf[1][:, halves[0], :], z1_rows[0][:])
+        late_words = held([P, 2, M], U32, "last_square")
+        z_wd[0], wl_wd[1] = late_words[:, 0, :], late_words[:, 1, :]
+        quantize(z_bf[0][:], z_wd[0], z_sc[0][:])
+        quantize(wl_bf[1][:], wl_wd[1], wl_sc[1][:])
+        chunks = (halves[0], slice(HALF, HALF + P), slice(HALF + P, M))
+        sums = {}
+        for j, cols in enumerate(chunks):
+            width = cols.stop - cols.start
+            shared = HALF // width
+            for c0 in range(0, N_TILES, shared):
+                group = bank(HALF, min(j, 1))
+                for lo in range(shared):
+                    sums[j, c0 + lo] = group[:, width * lo : width * (lo + 1)]
+                    second_product(sums[j, c0 + lo], c0 + lo, 0, z_wd[0][:, cols], z_sc[0][:, cols], lo == 0, False)
+
         multiply(0)
         leave(0, False)
+        cross = held([P, 2, HALF], F32, "z1_rows0")
+        pick_cross(cross[:, 0, :], s0, halves[1], prime[:, 0, halves[1]])
+        pick_cross(cross[:, 1, :P], s0 + 1, chunks[1], prime[:, 1, chunks[1]])
+        combine(s0, halves[1], cross[:, 0, :], scaled[:, 0, halves[1]])
+        pick_cross(cross[:, 1, P:], s0 + 1, chunks[2], prime[:, 1, chunks[2]])
+        combine(s0 + 1, chunks[1], cross[:, 1, :P], scaled[:, 1, chunks[1]])
+        combine(s0 + 1, chunks[2], cross[:, 1, P:], scaled[:, 1, chunks[2]])
         for j in (1, 2):
-            group_z(nc.vector.tensor_copy, 1, chunks[j])
+            interleave(nc.vector.tensor_copy, z_bf[1][:, chunks[j], :], z1_part(chunks[j]))
         for j in (1, 2):
             multiply(j)
         leave(1, False)

@@ -27,6 +27,7 @@ SCALE_ROWS = 32
 SLICES = H // P
 N_TILES = N // P
 HALF = M // 2
+CUT0 = 32 - N_TILES
 WORK_BUFS = 2
 
 
@@ -58,11 +59,10 @@ def tile_list_bell_discriminant_kernel(
         w4_wd = [held([P, 2, 2 * PASS], U8, "w4_wd%d" % b) for b in range(2)]
         tab_wd = [held([P, T], I32, "window%d" % a) for a in range(2)]
         v_wd = [[held([P, BANK], U32, "v_wd%d%d" % (a, u)) for u in range(2)] for a in range(2)]
-        vec_rows = held([P, P], F32, "vec_rows")
+        vec_rows = [held([P, P], F32, name) for name in ("gain_rows", "cut_rows")]
         ident = held([P, P], F32, "ident")
-        vec_cols = held([P, SLICES + N_TILES], F32, "vec_cols")
-        gain_sb = vec_cols[:, :SLICES]
-        cut_sb = vec_cols[:, SLICES:]
+        gain_sb = held([P, SLICES], F32, "gain_sb")
+        cut_sb = held([P, N_TILES], F32, "cut_sb")
         wl_bf = [held([P, N, PACK], BF16, "wl_bf%d" % b) for b in range(2)]
         wl_wd = {0: held([P, N], U32, "wl_wd0")}
         wl_sc = [held([P, N], U8, "wl_sc%d" % b) for b in range(2)]
@@ -72,7 +72,9 @@ def tile_list_bell_discriminant_kernel(
         nc.vector.memset(tab_sc[64:, :].bitcast(I32), 0)
         for a in range(2):
             nc.vector.memset(planes[a][:].bitcast(I32), 0)
-        nc.gpsimd.memset(vec_rows[:], 0.0)
+        nc.gpsimd.memset(vec_rows[0][:], 0.0)
+        for rows in (slice(0, CUT0), slice(32, 64), slice(64, P)):
+            nc.gpsimd.memset(vec_rows[1][rows, :], 0.0)
         make_identity(nc, ident[:])
 
         def load_w4(b, name):
@@ -82,6 +84,7 @@ def tile_list_bell_discriminant_kernel(
                 in_=w4_words[:, :, 2 * PASS * b : 2 * PASS * (b + 1)].bitcast(I32).rearrange("a p c -> p a c"),
             )
 
+        nc.scalar.dma_start(out=vec_rows[1][CUT0:32, :], in_=cut.rearrange("(c p) -> c p", p=P))
         nc.sync.dma_start(offs_sb[:], offs)
         nc.sync.dma_start(
             out=tab_sc[:SCALE_ROWS, :].bitcast(I32), in_=tab_scales.rearrange("a q t -> (a q) t").bitcast(I32)
@@ -90,12 +93,13 @@ def tile_list_bell_discriminant_kernel(
         load_w4(0, "w4_raw")
         for a in range(2):
             nc.sync.dma_start(out=tab_wd[a][:], in_=tab_words[a].rearrange("p t i -> p (t i)").bitcast(I32))
-        for b in range(2):
-            nc.gpsimd.dma_start(
-                out=vec_rows[PACK * b : PACK * (b + 1), :],
-                in_=gain[PASS * b : PASS * (b + 1)].rearrange("(g t i) -> t g i", t=PACK, i=RUN),
-            )
-        nc.gpsimd.dma_start(out=vec_rows[SLICES : SLICES + N_TILES, :], in_=cut.rearrange("(c p) -> c p", p=P))
+
+        def turn(rows, row0, cols):
+            turned = bank(P, 1)
+            nc.tensor.transpose(turned[:], rows[:], ident[:])
+            nc.scalar.copy(out=cols[:], in_=turned[:, row0 : row0 + cols.shape[1]])
+
+        turn(vec_rows[1], CUT0, cut_sb)
 
         def order_w4(b):
             nc.vector.tensor_copy(
@@ -120,18 +124,18 @@ def tile_list_bell_discriminant_kernel(
         order_w4(0)
         for e in range(1, 8):
             a, q = divmod(e, 4)
-            queue = nc.sync if e == 7 else nc.scalar
+            queue = nc.sync if a == 1 else nc.scalar
             queue.dma_start(out=planes[a][32 * q : 32 * q + 4, :].bitcast(I32), in_=staged[4 * e : 4 * e + 4, :])
         for list_sb, src in zip(pos_sb, (pos1, pos2, pos3)):
             nc.sync.dma_start(list_sb[:], src)
         gather_words(0)
         load_w4(1, "window0")
 
-        turned = bank(P, 1)
-        nc.tensor.transpose(turned[:], vec_rows[:], ident[:])
-        nc.scalar.copy(out=vec_cols[:], in_=turned[:, : SLICES + N_TILES])
-        minus_gain = held([P, SLICES], F32, "minus_gain")
-        nc.scalar.activation(out=minus_gain[:], in_=gain_sb, func=ACT.Copy, scale=-1.0)
+        for b in range(2):
+            nc.sync.dma_start(
+                out=vec_rows[0][PACK * b : PACK * (b + 1), :],
+                in_=gain[PASS * b : PASS * (b + 1)].rearrange("(g t i) -> t g i", t=PACK, i=RUN),
+            )
 
         acc = {}
 
@@ -266,6 +270,9 @@ def tile_list_bell_discriminant_kernel(
             return picks[:, 0], picks[:, 1]
 
         finish_h(2)
+        turn(vec_rows[0], 0, gain_sb)
+        minus_gain = held([P, SLICES], F32, "minus_gain")
+        nc.scalar.activation(out=minus_gain[:], in_=gain_sb[:], func=ACT.Copy, scale=-1.0)
         for s0 in range(0, SLICES - 2, 2):
             hum, prime = picks_of(s0)
             square = pair_tile("square")

@@ -23,7 +23,8 @@ PASS = P * PACK
 BANK = 512
 RUN = 8
 PER_COLUMN = 16
-SCALE_ROWS = 32
+BLOCKS = 16
+ROW0 = (48, 112)
 SLICES = H // P
 N_TILES = N // P
 HALF = M // 2
@@ -53,7 +54,8 @@ def tile_list_bell_discriminant_kernel(
 
         tab_sc = held([P, T], U8, "tab_sc")
         picked_sc = held([P, S], U8, "picked_sc")
-        w4_sc_raw = held([SCALE_ROWS, H // 4], I32, "w4_sc_raw")
+        w4_sc_raw = held([P, H // 4], I32, "w4_sc_raw")
+        staged = held([P, (S + H) // 4], I32, "staged")
         planes = [held([P, S + H], U8, "planes%d" % a) for a in range(2)]
         w4_raw = {}
         w4_wd = [held([P, 2, 2 * PASS], U8, "w4_wd%d" % b) for b in range(2)]
@@ -68,8 +70,9 @@ def tile_list_bell_discriminant_kernel(
         wl_sc = [held([P, N], U8, "wl_sc%d" % b) for b in range(2)]
         h_sb = [held([P, S], F32, "h_sb%d" % s) for s in range(SLICES)]
 
-        nc.vector.memset(tab_sc[SCALE_ROWS:64, :].bitcast(I32), 0)
-        nc.vector.memset(tab_sc[64:, :].bitcast(I32), 0)
+        for a in range(2):
+            nc.vector.memset(tab_sc[64 * a : ROW0[a], :].bitcast(I32), 0)
+            nc.vector.memset(w4_sc_raw[64 * a : ROW0[a], :], 0)
         for a in range(2):
             nc.vector.memset(planes[a][:].bitcast(I32), 0)
         nc.gpsimd.memset(vec_rows[0][:], 0.0)
@@ -86,10 +89,9 @@ def tile_list_bell_discriminant_kernel(
 
         nc.scalar.dma_start(out=vec_rows[1][CUT0:32, :], in_=cut.rearrange("(c p) -> c p", p=P))
         nc.sync.dma_start(offs_sb[:], offs)
-        nc.sync.dma_start(
-            out=tab_sc[:SCALE_ROWS, :].bitcast(I32), in_=tab_scales.rearrange("a q t -> (a q) t").bitcast(I32)
-        )
-        nc.sync.dma_start(out=w4_sc_raw[:], in_=w4_scales.rearrange("a q c -> (a q) c").bitcast(I32))
+        for dst, src in ((tab_sc[:].bitcast(I32), tab_scales), (w4_sc_raw[:], w4_scales)):
+            for a in range(2):
+                nc.sync.dma_start(out=dst[ROW0[a] : ROW0[a] + BLOCKS, :], in_=src[a].bitcast(I32))
         load_w4(0, "w4_raw")
         for a in range(2):
             nc.sync.dma_start(out=tab_wd[a][:], in_=tab_words[a].rearrange("p t i -> p (t i)").bitcast(I32))
@@ -114,18 +116,18 @@ def tile_list_bell_discriminant_kernel(
                     v_wd[a][u][:], tab_wd[a][:].bitcast(U32).indirect(offs_sb[:, columns * u : columns * (u + 1)])
                 )
 
-        staged = planes[0][:SCALE_ROWS, :].bitcast(I32)
         nc.vector.tensor_copy(
             out=staged[:, S // 4 :].rearrange("p (b t g w) -> p b t g w", b=2, t=PACK, w=2),
             in_=w4_sc_raw[:].rearrange("p (b g t w) -> p b t g w", b=2, t=PACK, w=2),
         )
         nc.vector.tensor_copy(picked_sc[:], tab_sc[:].indirect(offs_sb[:]))
-        nc.vector.tensor_copy(out=staged[:, : S // 4], in_=picked_sc[:SCALE_ROWS, :].bitcast(I32))
+        nc.vector.tensor_copy(out=staged[:, : S // 4], in_=picked_sc[:].bitcast(I32))
         order_w4(0)
-        for e in range(1, 8):
-            a, q = divmod(e, 4)
-            queue = nc.sync if a == 1 else nc.scalar
-            queue.dma_start(out=planes[a][32 * q : 32 * q + 4, :].bitcast(I32), in_=staged[4 * e : 4 * e + 4, :])
+        for a in range(2):
+            for q in range(4):
+                row = ROW0[a] + 4 * q
+                queue = nc.sync if a == 1 and q % 2 == 1 else nc.scalar
+                queue.dma_start(out=planes[a][32 * q : 32 * q + 4, :].bitcast(I32), in_=staged[row : row + 4, :])
         for list_sb, src in zip(pos_sb, (pos1, pos2, pos3)):
             nc.sync.dma_start(list_sb[:], src)
         gather_words(0)
@@ -164,16 +166,12 @@ def tile_list_bell_discriminant_kernel(
         def finish_h(s):
             for j0 in (0, BANK):
                 part = (s, j0, BANK)
-                if part not in done:
-                    if part not in acc:
-                        first_product(part, 0)
-                    first_product(part, 1)
-                if part not in emptied:
-                    empty(part, nc.scalar.copy)
+                first_product(part, 0)
+                first_product(part, 1)
+                empty(part, nc.scalar.copy)
 
-        firsts = [(s, 0, BANK) for s in range(2)]
-        seconds = [(0, BANK, HALF), (0, BANK + HALF, HALF)]
-        for part in firsts + seconds:
+        parts = [(0, 0, BANK), (0, BANK, HALF), (0, BANK + HALF, HALF)]
+        for part in parts:
             first_product(part, 0)
         gather_words(1)
         wl_raw = held([P, 2, PACK, N], F32, "window1")
@@ -181,14 +179,9 @@ def tile_list_bell_discriminant_kernel(
             rows = wl[PASS * b : PASS * (b + 1), :].rearrange("(g t i) n -> t g i n", t=PACK, i=RUN)
             for t in range(PACK):
                 nc.sync.dma_start(out=wl_raw[:, b, t, :], in_=rows[t])
-        for part in firsts + seconds:
+        for part, copy in zip(parts, (nc.scalar.copy, nc.scalar.copy, nc.vector.tensor_copy)):
             first_product(part, 1)
-        done = firsts + seconds
-        emptied = done
-        empty(firsts[0], nc.scalar.copy)
-        empty(firsts[1], nc.scalar.copy)
-        empty(seconds[0], nc.scalar.copy)
-        empty(seconds[1], nc.vector.tensor_copy)
+            empty(part, copy)
         order_w4(1)
         finish_h(1)
         def interleave(copy, dst, src):

@@ -40,13 +40,14 @@ def tile_list_bell_discriminant_kernel(
         lists = ctx.enter_context(tc.tile_pool(name="lists", bufs=1))
         keep = ctx.enter_context(tc.tile_pool(name="keep", bufs=1))
         work = ctx.enter_context(tc.tile_pool(name="work", bufs=WORK_BUFS))
-        psum = [ctx.enter_context(tc.psum_pool(name="psum%d" % i, bufs=4)) for i in range(2)]
+        psum = ctx.enter_context(tc.psum_pool(name="psum", bufs=4))
+        psum_turn = ctx.enter_context(tc.psum_pool(name="psum_turn", bufs=1))
 
         def held(shape, dtype, name):
             return keep.tile(shape, dtype, name=name, align_bytes=64)
 
-        def bank(width, pool):
-            return psum[pool].tile([P, width], F32, name="bank", tag="bank")
+        def bank(width):
+            return psum.tile([P, width], F32, name="bank", tag="bank")
 
         offs_sb = lists.tile([P, S // PER_COLUMN], U16, name="offs_sb")
         pos_sb = [lists.tile([P, M // PER_COLUMN], U16, name="pos_sb%d" % i) for i in range(3)]
@@ -97,7 +98,7 @@ def tile_list_bell_discriminant_kernel(
             nc.sync.dma_start(out=tab_wd[a][:], in_=tab_words[a].rearrange("p t i -> p (t i)").bitcast(I32))
 
         def turn(rows, row0, cols):
-            turned = bank(P, 1)
+            turned = psum_turn.tile([P, P], F32, name="turned")
             nc.tensor.transpose(turned[:], rows[:], ident[:])
             nc.scalar.copy(out=cols[:], in_=turned[:, row0 : row0 + cols.shape[1]])
 
@@ -146,7 +147,7 @@ def tile_list_bell_discriminant_kernel(
             b, t = divmod(s, PACK)
             u, lo = divmod(j0, BANK)
             if a == 0:
-                acc[part] = bank(width, 0)
+                acc[part] = bank(width)
             n = BANK if width == BANK else P
             for j in range(0, width, n):
                 nc.tensor.matmul_mx(
@@ -346,7 +347,7 @@ def tile_list_bell_discriminant_kernel(
             width = cols.stop - cols.start
             shared = HALF // width
             for c0 in range(0, N_TILES, shared):
-                group = bank(HALF, min(j, 1))
+                group = bank(HALF)
                 for lo in range(shared):
                     sums[j, c0 + lo] = group[:, width * lo : width * (lo + 1)]
                     second_product(sums[j, c0 + lo], c0 + lo, 0, z_wd[0][:, cols], z_sc[0][:, cols], lo == 0, False)

@@ -42,6 +42,7 @@ def tile_list_bell_discriminant_kernel(
         work = ctx.enter_context(tc.tile_pool(name="work", bufs=WORK_BUFS))
         psum = ctx.enter_context(tc.psum_pool(name="psum", bufs=4))
         psum_turn = ctx.enter_context(tc.psum_pool(name="psum_turn", bufs=1))
+        psum_last = ctx.enter_context(tc.psum_pool(name="psum_last", bufs=2))
 
         def held(shape, dtype, name):
             return keep.tile(shape, dtype, name=name, align_bytes=64)
@@ -66,9 +67,9 @@ def tile_list_bell_discriminant_kernel(
         ident = held([P, P], F32, "ident")
         gain_sb = held([P, SLICES], F32, "gain_sb")
         cut_sb = held([P, N_TILES], F32, "cut_sb")
-        wl_bf = [held([P, N, PACK], BF16, "wl_bf%d" % b) for b in range(2)]
-        wl_wd = {0: held([P, N], U32, "wl_wd0")}
-        wl_sc = [held([P, N], U8, "wl_sc%d" % b) for b in range(2)]
+        wl_bf = held([P, 2 * N, PACK], BF16, "wl_bf")
+        wl_wd = held([P, 2 * N], U32, "wl_wd")
+        wl_sc = held([P, 2 * N], U8, "wl_sc")
         h_sb = [held([P, S], F32, "h_sb%d" % s) for s in range(SLICES)]
 
         for a in range(2):
@@ -184,186 +185,169 @@ def tile_list_bell_discriminant_kernel(
             first_product(part, 1)
             empty(part, copy)
         order_w4(1)
-        finish_h(1)
-        def interleave(copy, dst, src):
-            copy(
-                out=dst.rearrange("p (c i) t -> p c t i", i=4),
-                in_=src.rearrange("p t (c i) -> p c t i", i=4),
-            )
+
+        def rows_view(ap):
+            return ap.rearrange("p t (c i) -> p c t i", i=4)
+
+        def words_view(ap):
+            return ap.rearrange("p (c i) t -> p c t i", i=4)
 
         def quantize(grouped, codes, scales):
             nc.vector.quantize_mx(out=codes.bitcast(FP8X4), scales=scales, in_=grouped.rearrange("p m t -> p (m t)"))
 
+        whole = slice(0, M)
         halves = (slice(0, HALF), slice(HALF, M))
 
-        def entries(cols):
-            return slice(cols.start // PER_COLUMN, cols.stop // PER_COLUMN)
-
-        def pair_tile(name):
-            return work.tile([P, 2, M], F32, name=name, tag=name)
-
-        def pick(dst, s, picks):
-            nc.vector.tensor_copy(dst, h_sb[s][:].indirect(picks[:]))
-
-        def pick_cross(dst, s, cols, prime):
-            nc.vector.tensor_tensor(dst, h_sb[s][:].indirect(tierce_list[:, entries(cols)]), prime, ALU.mult)
-
-        def square_of(dst, src):
-            nc.scalar.activation(out=dst, in_=src, func=ACT.Square)
+        def window(s, picks, cols):
+            return h_sb[s][:].indirect(picks[:, cols.start // PER_COLUMN : cols.stop // PER_COLUMN])
 
         def scale(dst, src, s):
             nc.scalar.activation(out=dst, in_=src, func=ACT.Copy, scale=gain_sb[:, s : s + 1])
 
-        def combine(s, cols, cross, scaled):
-            nc.vector.scalar_tensor_tensor(
-                z1_part(cols)[:, s - PACK, :], cross, minus_gain[:, s : s + 1], scaled, ALU.mult, ALU.add
+        def pick_prime(picked, scaled, s, cols):
+            nc.vector.tensor_copy(picked, window(s, prime_list, cols))
+            scale(scaled, picked, s)
+
+        def pick_hum(picked, s, cols):
+            nc.vector.tensor_copy(picked, window(s, hum_list, cols))
+            square = work.tile([P, cols.stop - cols.start], F32, name="square", tag="square")
+            nc.scalar.activation(out=square[:], in_=picked, func=ACT.Square)
+            return square
+
+        def pick_cross(dst, s, cols, scaled_prime):
+            nc.vector.tensor_tensor(dst, window(s, tierce_list, cols), scaled_prime, ALU.mult)
+
+        def difference(engine, z, squares, cross):
+            engine.tensor_tensor(words_view(z), rows_view(squares), rows_view(cross), ALU.subtract)
+
+        def h_half(s, j0):
+            part = (s, j0, BANK)
+            first_product(part, 0)
+            first_product(part, 1)
+            empty(part, nc.scalar.copy)
+
+        finish_h(1)
+        turn(vec_rows[0], 0, gain_sb)
+        finish_h(2)
+        for b in range(2):
+            nc.gpsimd.tensor_scalar(
+                words_view(wl_bf[:, N * b : N * (b + 1), :]), rows_view(wl_raw[:, b]), 1.0, 0.0, ALU.mult, ALU.add
             )
 
+        picks = held([P, 2, PACK, M], F32, "picks0")
+        squares0 = held([P, PACK, M], F32, "squares0")
+        early = held([P, PACK - 1, M], F32, "primes0")
+        primes = [early[:, t, :] for t in range(PACK - 1)] + [held([P, M], F32, "prime3")[:]]
+        for s in range(PACK):
+            pick_prime(picks[:, 0, s, :], primes[s], s, whole)
+            square = pick_hum(picks[:, 1, s, :], s, whole)
+            h_half(s + 3, 0)
+            scale(squares0[:, s, :], square[:], s)
+            h_half(s + 3, BANK)
+        finish_h(SLICES - 1)
+        quantize(wl_bf[:], wl_wd[:], wl_sc[:])
+        cross = held([P, PACK, M], F32, "window1")
+        for s in range(PACK):
+            pick_cross(cross[:, s, :], s, whole, primes[s])
+        z0 = held([P, M, PACK], BF16, "z0")
+        difference(nc.gpsimd, z0[:], squares0[:], cross[:])
+
+        last = SLICES - 1
+        picks = held([P, 3 * M + HALF + PACK * HALF], F32, "primes0")
+        early = held([P, PACK - 1, M], F32, "primes1")
+        last_prime = [held([P, HALF], F32, "prime7%d" % j) for j in range(2)]
+        squares = [held([P, PACK, HALF], F32, "squares1%d" % j) for j in range(2)]
+        hum0 = 3 * M + HALF
+        waiting = None
+        for t in range(PACK):
+            s = PACK + t
+            if s < last:
+                pick_prime(picks[:, M * t : M * (t + 1)], early[:, t, :], s, whole)
+            else:
+                pick_prime(picks[:, M * t : M * t + HALF], last_prime[0][:], s, halves[0])
+            if waiting is not None:
+                scale(*waiting)
+            square = pick_hum(picks[:, hum0 + HALF * t : hum0 + HALF * (t + 1)], s, halves[0])
+            waiting = (squares[0][:, t, :], square[:], s)
+        scale(*waiting)
+        z0_wd, z0_sc = held([P, M], U32, "z0_wd"), held([P, M], U8, "z0_sc")
+        quantize(z0[:], z0_wd[:], z0_sc[:])
+        cross = held([P, PACK, M], F32, "window1")
+        for t in range(PACK - 1):
+            pick_cross(cross[:, t, :], PACK + t, whole, early[:, t, :])
+        pick_cross(cross[:, PACK - 1, halves[0]], last, halves[0], last_prime[0][:])
+        z_first = held([P, HALF, PACK], BF16, "z_first")
+        difference(nc.gpsimd, z_first[:], squares[0][:], cross[:, :, halves[0]])
+
         def second_product(sums, c, b, z_wd, z_sc, start, stop):
+            cols = slice(N * b + P * c, N * b + P * (c + 1))
             nc.tensor.matmul_mx(
                 out=sums,
-                lhsT=wl_wd[b][:, P * c : P * (c + 1)].bitcast(FP8X4),
-                lhsT_scale=wl_sc[b][:, P * c : P * (c + 1)],
+                lhsT=wl_wd[:, cols].bitcast(FP8X4),
+                lhsT_scale=wl_sc[:, cols],
                 rhs=z_wd.bitcast(FP8X4),
                 rhs_scale=z_sc,
                 start=start,
                 stop=stop,
             )
 
-        def store(result, c0, tiles, m0, w):
-            nc.sync.dma_start(
-                out=out[P * c0 : P * (c0 + tiles), m0 : m0 + w].rearrange("(c p) m -> p c m", p=P), in_=result
-            )
+        chunks = (halves[0], slice(HALF, HALF + P), slice(HALF + P, M))
+        groups = {}
+        for j, cols in enumerate(chunks):
+            width = cols.stop - cols.start
+            for c0 in range(0, N_TILES, 2):
+                if j < 2:
+                    groups[j, c0] = bank(2 * width)
+                else:
+                    groups[j, c0] = psum_last.tile([P, 2 * width], F32, name="last_bank", tag="last_bank")
+                for lo in range(2):
+                    sums = groups[j, c0][:, width * lo : width * (lo + 1)]
+                    second_product(sums, c0 + lo, 0, z0_wd[:, cols], z0_sc[:, cols], lo == 0, False)
 
-        def cast_wl(b, c):
-            cols = slice(P * c, P * (c + 1))
-            interleave(nc.scalar.copy, wl_bf[b][:, cols, :], wl_raw[:, b, :, cols])
-
-        z0_rows = held([P, PACK, M], BF16, "z0_rows")
-        z1_rows = [held([P, PACK, HALF], BF16, "z1_rows%d" % j) for j in range(2)]
-        z_bf = [held([P, M, PACK], BF16, "z_bf%d" % b) for b in range(2)]
-        z_wd = {1: held([P, M], U32, "z_wd1")}
-        z_sc = [held([P, M], U8, "z_sc%d" % b) for b in range(2)]
-
-        def z1_part(cols):
-            j = cols.start // HALF
-            return z1_rows[j][:, :, cols.start - HALF * j : cols.stop - HALF * j]
-
-        whole = slice(0, M)
-        diff = {}
-
-        def apply_gain(s):
-            if s < PACK:
-                scale(z0_rows[:, s, :], diff[s][:], s)
-            else:
-                for cols in halves:
-                    scale(z1_part(cols)[:, s - PACK, :], diff[s][:, cols], s)
-
-        def picks_of(s0):
-            picks = held([P, 2, 2, M], F32, "after_diff%d" % (s0 - 3))
-            return picks[:, 0], picks[:, 1]
-
-        finish_h(2)
-        turn(vec_rows[0], 0, gain_sb)
-        minus_gain = held([P, SLICES], F32, "minus_gain")
-        nc.scalar.activation(out=minus_gain[:], in_=gain_sb[:], func=ACT.Copy, scale=-1.0)
-        for s0 in range(0, SLICES - 2, 2):
-            hum, prime = picks_of(s0)
-            square = pair_tile("square")
-            for i in range(2):
-                pick(prime[:, i, :], s0 + i, prime_list)
-                pick(hum[:, i, :], s0 + i, hum_list)
-            square_of(square[:, 0, :], hum[:, 0, :])
-            if s0 > 0:
-                apply_gain(s0 - 2)
-                apply_gain(s0 - 1)
-            finish_h(s0 + 3)
-            square_of(square[:, 1, :], hum[:, 1, :])
-            if s0 + 4 < SLICES:
-                finish_h(s0 + 4)
-            cross = held([P, 2, M], F32, "after_diff%d" % (s0 - 2))
-            for i in range(2):
-                pick_cross(cross[:, i, :], s0 + i, whole, prime[:, i, :])
-            for i in range(2):
-                diff[s0 + i] = held([P, M], F32, "after_diff%d" % (s0 + i))
-                nc.gpsimd.tensor_tensor(diff[s0 + i][:], square[:, i, :], cross[:, i, :], ALU.subtract)
-            if s0 < PACK:
-                b = s0 // 2
-                for c in range(N_TILES):
-                    cast_wl(b, c)
-                if b == 0:
-                    quantize(wl_bf[0][:], wl_wd[0][:], wl_sc[0][:])
-            else:
-                for c in range(M // P):
-                    cols = slice(P * c, P * (c + 1))
-                    interleave(nc.scalar.copy, z_bf[0][:, cols, :], z0_rows[:, :, cols])
-
-        s0 = SLICES - 2
-        hum, prime = picks_of(s0)
-        square, scaled = held([P, 2, M], F32, "last_square"), pair_tile("scaled")
-        for dst, picks in ((hum, hum_list), (prime, prime_list)):
-            for i in range(2):
-                pick(dst[:, i, :], s0 + i, picks)
-        for i in range(2):
-            square_of(square[:, i, :], hum[:, i, :])
-            scale(scaled[:, i, :], square[:, i, :], s0 + i)
-        apply_gain(s0 - 2)
-        apply_gain(s0 - 1)
-        def multiply(j):
-            cols = chunks[j]
-            shared = HALF // (cols.stop - cols.start)
-            quantize(z_bf[1][:, cols, :], z_wd[1][:, cols], z_sc[1][:, cols])
+        def multiply(j, z):
+            width = chunks[j].stop - chunks[j].start
+            z_wd, z_sc = held([P, width], U32, "z_wd%d" % j), held([P, width], U8, "z_sc%d" % j)
+            quantize(z, z_wd[:], z_sc[:])
             for c in range(N_TILES):
-                second_product(sums[j, c], c, 1, z_wd[1][:, cols], z_sc[1][:, cols], False, c % shared == shared - 1)
+                c0, lo = c - c % 2, c % 2
+                second_product(groups[j, c0][:, width * lo : width * (lo + 1)], c, 1, z_wd[:], z_sc[:], False, lo == 1)
 
         def leave(j, on_vector):
             cols = chunks[j]
             width = cols.stop - cols.start
             for c0 in range(0, N_TILES, 2):
                 result = held([P, 2, width], F32, "result%d%d" % (j, c0))
-                for lo in range(2):
-                    c = c0 + lo
-                    if on_vector:
-                        nc.vector.tensor_scalar(result[:, lo, :], sums[j, c], cut_sb[:, c : c + 1], None, ALU.add)
-                    else:
+                sums = groups[j, c0][:].rearrange("p (c m) -> p c m", c=2)
+                if on_vector:
+                    bias = cut_sb[:, c0 : c0 + 2].unsqueeze(2).to_broadcast([P, 2, width])
+                    nc.vector.tensor_tensor(result[:], sums, bias, ALU.add)
+                else:
+                    for lo in range(2):
+                        c = c0 + lo
                         nc.scalar.activation(
-                            out=result[:, lo, :], in_=sums[j, c], func=ACT.Identity, bias=cut_sb[:, c : c + 1]
+                            out=result[:, lo, :], in_=sums[:, lo, :], func=ACT.Identity, bias=cut_sb[:, c : c + 1]
                         )
-                store(result[:], c0, 2, cols.start, width)
+                nc.sync.dma_start(
+                    out=out[P * c0 : P * (c0 + 2), cols].rearrange("(c p) m -> p c m", p=P), in_=result[:]
+                )
 
-        cross = held([P, 2, HALF], F32, "end_cross")
-        for i in range(2):
-            pick_cross(cross[:, i, :], s0 + i, halves[0], prime[:, i, halves[0]])
-        for i in range(2):
-            combine(s0 + i, halves[0], cross[:, i, :], scaled[:, i, halves[0]])
-        interleave(nc.scalar.copy, z_bf[1][:, halves[0], :], z1_rows[0][:])
-        late_words = held([P, 2, M], U32, "last_square")
-        z_wd[0], wl_wd[1] = late_words[:, 0, :], late_words[:, 1, :]
-        quantize(z_bf[0][:], z_wd[0], z_sc[0][:])
-        quantize(wl_bf[1][:], wl_wd[1], wl_sc[1][:])
-        chunks = (halves[0], slice(HALF, HALF + P), slice(HALF + P, M))
-        sums = {}
-        for j, cols in enumerate(chunks):
-            width = cols.stop - cols.start
-            shared = HALF // width
-            for c0 in range(0, N_TILES, shared):
-                group = bank(HALF)
-                for lo in range(shared):
-                    sums[j, c0 + lo] = group[:, width * lo : width * (lo + 1)]
-                    second_product(sums[j, c0 + lo], c0 + lo, 0, z_wd[0][:, cols], z_sc[0][:, cols], lo == 0, False)
-
-        multiply(0)
+        picks = held([P, PACK + 1, HALF], F32, "primes1")
+        pick_prime(picks[:, PACK, :], last_prime[1][:], last, halves[1])
+        waiting = None
+        for t in range(PACK):
+            square = pick_hum(picks[:, t, :], PACK + t, halves[1])
+            if waiting is not None:
+                scale(*waiting)
+            waiting = (squares[1][:, t, :], square[:], PACK + t)
+        scale(*waiting)
+        pick_cross(cross[:, PACK - 1, halves[1]], last, halves[1], last_prime[1][:])
+        multiply(0, z_first[:])
+        z_last = held([P, HALF, PACK], BF16, "squares10")
+        for j in (1, 2):
+            lo = slice(P * (j - 1), P * j)
+            difference(nc.vector, z_last[:, lo, :], squares[1][:, :, lo], cross[:, :, chunks[j]])
+        for j in (1, 2):
+            multiply(j, z_last[:, P * (j - 1) : P * j, :])
         leave(0, False)
-        cross = held([P, 2, HALF], F32, "z1_rows0")
-        pick_cross(cross[:, 0, :], s0, halves[1], prime[:, 0, halves[1]])
-        pick_cross(cross[:, 1, :P], s0 + 1, chunks[1], prime[:, 1, chunks[1]])
-        combine(s0, halves[1], cross[:, 0, :], scaled[:, 0, halves[1]])
-        pick_cross(cross[:, 1, P:], s0 + 1, chunks[2], prime[:, 1, chunks[2]])
-        combine(s0 + 1, chunks[1], cross[:, 1, :P], scaled[:, 1, chunks[1]])
-        combine(s0 + 1, chunks[2], cross[:, 1, P:], scaled[:, 1, chunks[2]])
-        for j in (1, 2):
-            interleave(nc.vector.tensor_copy, z_bf[1][:, chunks[j], :], z1_part(chunks[j]))
-        for j in (1, 2):
-            multiply(j)
         leave(1, False)
         leave(2, True)

@@ -176,7 +176,7 @@ def tile_list_bell_discriminant_kernel(
         for part in parts:
             first_product(part, 0)
         gather_words(1)
-        wl_raw = held([P, 2, PACK, N], F32, "window1")
+        wl_raw = held([P, 2, PACK, N], F32, "cross0")
         for b in range(2):
             rows = wl[PASS * b : PASS * (b + 1), :].rearrange("(g t i) n -> t g i n", t=PACK, i=RUN)
             for t in range(PACK):
@@ -246,38 +246,45 @@ def tile_list_bell_discriminant_kernel(
             h_half(s + 3, BANK)
         finish_h(SLICES - 1)
         quantize(wl_bf[:], wl_wd[:], wl_sc[:])
-        cross = held([P, PACK, M], F32, "window1")
+        cross = held([P, PACK, M], F32, "cross0")
         for s in range(PACK):
             pick_cross(cross[:, s, :], s, whole, primes[s])
         z0 = held([P, M, PACK], BF16, "z0")
         difference(nc.gpsimd, z0[:], squares0[:], cross[:])
 
-        last = SLICES - 1
-        picks = held([P, 3 * M + HALF + PACK * HALF], F32, "primes0")
-        early = held([P, PACK - 1, M], F32, "primes1")
-        last_prime = [held([P, HALF], F32, "prime7%d" % j) for j in range(2)]
+        kept = 2
+        full = PACK - kept
+        picks = held([P, full * M + kept * HALF + PACK * HALF], F32, "primes0")
+        hums = picks[:, full * M + kept * HALF :].rearrange("p (t m) -> p t m", t=PACK)
+        full_primes = held([P, full, M], F32, "primes1")
+        primes = {}
+        for t in range(PACK):
+            for j in range(2):
+                if t < full:
+                    primes[t, j] = full_primes[:, t, halves[j]]
+                else:
+                    primes[t, j] = held([P, HALF], F32, "prime%d%d" % (PACK + t, j))[:]
         squares = [held([P, PACK, HALF], F32, "squares1%d" % j) for j in range(2)]
-        hum0 = 3 * M + HALF
         waiting = None
         for t in range(PACK):
             s = PACK + t
-            if s < last:
-                pick_prime(picks[:, M * t : M * (t + 1)], early[:, t, :], s, whole)
+            if t < full:
+                pick_prime(picks[:, M * t : M * (t + 1)], full_primes[:, t, :], s, whole)
             else:
-                pick_prime(picks[:, M * t : M * t + HALF], last_prime[0][:], s, halves[0])
+                lo = M * full + HALF * (t - full)
+                pick_prime(picks[:, lo : lo + HALF], primes[t, 0], s, halves[0])
             if waiting is not None:
                 scale(*waiting)
-            square = pick_hum(picks[:, hum0 + HALF * t : hum0 + HALF * (t + 1)], s, halves[0])
+            square = pick_hum(hums[:, t, :], s, halves[0])
             waiting = (squares[0][:, t, :], square[:], s)
         scale(*waiting)
         z0_wd, z0_sc = held([P, M], U32, "z0_wd"), held([P, M], U8, "z0_sc")
         quantize(z0[:], z0_wd[:], z0_sc[:])
-        cross = held([P, PACK, M], F32, "window1")
-        for t in range(PACK - 1):
-            pick_cross(cross[:, t, :], PACK + t, whole, early[:, t, :])
-        pick_cross(cross[:, PACK - 1, halves[0]], last, halves[0], last_prime[0][:])
+        cross = held([P, PACK, HALF], F32, "cross0")
+        for t in range(PACK):
+            pick_cross(cross[:, t, :], PACK + t, halves[0], primes[t, 0])
         z_first = held([P, HALF, PACK], BF16, "z_first")
-        difference(nc.gpsimd, z_first[:], squares[0][:], cross[:, :, halves[0]])
+        difference(nc.gpsimd, z_first[:], squares[0][:], cross[:])
 
         def second_product(sums, c, b, z_wd, z_sc, start, stop):
             cols = slice(N * b + P * c, N * b + P * (c + 1))
@@ -312,27 +319,25 @@ def tile_list_bell_discriminant_kernel(
                 c0, lo = c - c % 2, c % 2
                 second_product(groups[j, c0][:, width * lo : width * (lo + 1)], c, 1, z_wd[:], z_sc[:], False, lo == 1)
 
-        def leave(j, on_vector):
+        def leave(j, c0, on_vector):
             cols = chunks[j]
             width = cols.stop - cols.start
-            for c0 in range(0, N_TILES, 2):
-                result = held([P, 2, width], F32, "result%d%d" % (j, c0))
-                sums = groups[j, c0][:].rearrange("p (c m) -> p c m", c=2)
-                if on_vector:
-                    bias = cut_sb[:, c0 : c0 + 2].unsqueeze(2).to_broadcast([P, 2, width])
-                    nc.vector.tensor_tensor(result[:], sums, bias, ALU.add)
-                else:
-                    for lo in range(2):
-                        c = c0 + lo
-                        nc.scalar.activation(
-                            out=result[:, lo, :], in_=sums[:, lo, :], func=ACT.Identity, bias=cut_sb[:, c : c + 1]
-                        )
-                nc.sync.dma_start(
-                    out=out[P * c0 : P * (c0 + 2), cols].rearrange("(c p) m -> p c m", p=P), in_=result[:]
-                )
+            result = held([P, 2, width], F32, "result%d%d" % (j, c0))
+            sums = groups[j, c0][:].rearrange("p (c m) -> p c m", c=2)
+            if on_vector:
+                bias = cut_sb[:, c0 : c0 + 2].unsqueeze(2).to_broadcast([P, 2, width])
+                nc.vector.tensor_tensor(result[:], sums, bias, ALU.add)
+            else:
+                for lo in range(2):
+                    c = c0 + lo
+                    nc.scalar.activation(
+                        out=result[:, lo, :], in_=sums[:, lo, :], func=ACT.Identity, bias=cut_sb[:, c : c + 1]
+                    )
+            nc.sync.dma_start(out=out[P * c0 : P * (c0 + 2), cols].rearrange("(c p) m -> p c m", p=P), in_=result[:])
 
-        picks = held([P, PACK + 1, HALF], F32, "primes1")
-        pick_prime(picks[:, PACK, :], last_prime[1][:], last, halves[1])
+        picks = held([P, PACK + kept, HALF], F32, "prime%d0" % (PACK + full))
+        for t in range(full, PACK):
+            pick_prime(picks[:, PACK + t - full, :], primes[t, 1], PACK + t, halves[1])
         waiting = None
         for t in range(PACK):
             square = pick_hum(picks[:, t, :], PACK + t, halves[1])
@@ -340,14 +345,27 @@ def tile_list_bell_discriminant_kernel(
                 scale(*waiting)
             waiting = (squares[1][:, t, :], square[:], PACK + t)
         scale(*waiting)
-        pick_cross(cross[:, PACK - 1, halves[1]], last, halves[1], last_prime[1][:])
         multiply(0, z_first[:])
-        z_last = held([P, HALF, PACK], BF16, "squares10")
-        for j in (1, 2):
-            lo = slice(P * (j - 1), P * j)
-            difference(nc.vector, z_last[:, lo, :], squares[1][:, :, lo], cross[:, :, chunks[j]])
-        for j in (1, 2):
-            multiply(j, z_last[:, P * (j - 1) : P * j, :])
-        leave(0, False)
-        leave(1, False)
-        leave(2, True)
+        cross = held([P, 2, PACK, P], F32, "squares10")
+        z_last = [held([P, P, PACK], BF16, "z_last%d" % q) for q in range(2)]
+
+        def quarter_cross(q, t):
+            pick_cross(cross[:, q, t, :], PACK + t, chunks[1 + q], primes[t, 1][:, P * q : P * (q + 1)])
+
+        def quarter_difference(q):
+            difference(nc.vector, z_last[q][:], squares[1][:, :, P * q : P * (q + 1)], cross[:, q])
+
+        for t in range(PACK):
+            quarter_cross(0, t)
+        quarter_cross(1, 0)
+        quarter_difference(0)
+        for t in range(1, PACK):
+            quarter_cross(1, t)
+        multiply(1, z_last[0][:])
+        quarter_difference(1)
+        multiply(2, z_last[1][:])
+        for j in range(2):
+            for c0 in range(0, N_TILES, 2):
+                leave(j, c0, False)
+        leave(2, 0, True)
+        leave(2, 2, False)

@@ -187,10 +187,10 @@ def tile_list_bell_discriminant_kernel(
         order_w4(1)
 
         def rows_view(ap):
-            return ap.rearrange("p t (c i) -> p c t i", i=4)
+            return ap.rearrange("p t (c i) -> p c t i", i=2)
 
         def words_view(ap):
-            return ap.rearrange("p (c i) t -> p c t i", i=4)
+            return ap.rearrange("p (c i) t -> p c t i", i=2)
 
         def quantize(grouped, codes, scales):
             nc.vector.quantize_mx(out=codes.bitcast(FP8X4), scales=scales, in_=grouped.rearrange("p m t -> p (m t)"))

@@ -105,8 +105,8 @@ def tile_list_bell_discriminant_kernel(
 
         turn(vec_rows[1], CUT0, cut_sb)
 
-        def order_w4(b):
-            nc.vector.tensor_copy(
+        def order_w4(b, engine):
+            engine.tensor_copy(
                 out=w4_wd[b][:].bitcast(I32).rearrange("p a (t g w) -> p a t g w", t=PACK, w=4),
                 in_=w4_raw[b][:].rearrange("p a (g t w) -> p a t g w", t=PACK, w=4),
             )
@@ -124,7 +124,7 @@ def tile_list_bell_discriminant_kernel(
         )
         nc.vector.tensor_copy(picked_sc[:], tab_sc[:].indirect(offs_sb[:]))
         nc.vector.tensor_copy(out=staged[:, : S // 4], in_=picked_sc[:].bitcast(I32))
-        order_w4(0)
+        order_w4(0, nc.vector)
         for a in range(2):
             for q in range(4):
                 row = ROW0[a] + 4 * q
@@ -181,10 +181,10 @@ def tile_list_bell_discriminant_kernel(
             rows = wl[PASS * b : PASS * (b + 1), :].rearrange("(g t i) n -> t g i n", t=PACK, i=RUN)
             for t in range(PACK):
                 nc.sync.dma_start(out=wl_raw[:, b, t, :], in_=rows[t])
-        for part, copy in zip(parts, (nc.scalar.copy, nc.scalar.copy, nc.vector.tensor_copy)):
+        for part, copy in zip(parts, (nc.scalar.copy, nc.vector.tensor_copy, nc.vector.tensor_copy)):
             first_product(part, 1)
             empty(part, copy)
-        order_w4(1)
+        order_w4(1, nc.gpsimd)
 
         def rows_view(ap):
             return ap.rearrange("p t (c i) -> p c t i", i=2)
@@ -278,8 +278,9 @@ def tile_list_bell_discriminant_kernel(
             square = pick_hum(hums[:, t, :], s, halves[0])
             waiting = (squares[0][:, t, :], square[:], s)
         scale(*waiting)
-        z0_wd, z0_sc = held([P, M], U32, "z0_wd"), held([P, M], U8, "z0_sc")
-        quantize(z0[:], z0_wd[:], z0_sc[:])
+        z0_wd = {0: held([P, HALF], U32, "z0_wd")}
+        z0_sc = [held([P, HALF], U8, "z0_sc%d" % j) for j in range(2)]
+        quantize(z0[:, halves[0], :], z0_wd[0][:], z0_sc[0][:])
         cross = held([P, PACK, HALF], F32, "cross0")
         for t in range(PACK):
             pick_cross(cross[:, t, :], PACK + t, halves[0], primes[t, 0])
@@ -300,8 +301,11 @@ def tile_list_bell_discriminant_kernel(
 
         chunks = (halves[0], slice(HALF, HALF + P), slice(HALF + P, M))
         groups = {}
-        for j, cols in enumerate(chunks):
-            width = cols.stop - cols.start
+
+        def open_sums(j):
+            half, first = divmod(chunks[j].start, HALF)
+            width = chunks[j].stop - chunks[j].start
+            cols = slice(first, first + width)
             for c0 in range(0, N_TILES, 2):
                 if j < 2:
                     groups[j, c0] = bank(2 * width)
@@ -309,7 +313,9 @@ def tile_list_bell_discriminant_kernel(
                     groups[j, c0] = psum_last.tile([P, 2 * width], F32, name="last_bank", tag="last_bank")
                 for lo in range(2):
                     sums = groups[j, c0][:, width * lo : width * (lo + 1)]
-                    second_product(sums, c0 + lo, 0, z0_wd[:, cols], z0_sc[:, cols], lo == 0, False)
+                    second_product(sums, c0 + lo, 0, z0_wd[half][:, cols], z0_sc[half][:, cols], lo == 0, False)
+
+        open_sums(0)
 
         def multiply(j, z):
             width = chunks[j].stop - chunks[j].start
@@ -346,6 +352,10 @@ def tile_list_bell_discriminant_kernel(
             waiting = (squares[1][:, t, :], square[:], PACK + t)
         scale(*waiting)
         multiply(0, z_first[:])
+        z0_wd[1] = held([P, HALF], U32, "cross0")
+        quantize(z0[:, halves[1], :], z0_wd[1][:], z0_sc[1][:])
+        for j in (1, 2):
+            open_sums(j)
         cross = held([P, 2, PACK, P], F32, "squares10")
         z_last = [held([P, P, PACK], BF16, "z_last%d" % q) for q in range(2)]
 
@@ -363,9 +373,10 @@ def tile_list_bell_discriminant_kernel(
             quarter_cross(1, t)
         multiply(1, z_last[0][:])
         quarter_difference(1)
+        for c0 in range(0, N_TILES, 2):
+            leave(0, c0, False)
+        leave(1, 0, True)
+        leave(1, 2, False)
         multiply(2, z_last[1][:])
-        for j in range(2):
-            for c0 in range(0, N_TILES, 2):
-                leave(j, c0, False)
-        leave(2, 0, True)
-        leave(2, 2, False)
+        leave(2, 0, False)
+        leave(2, 2, True)

@@ -42,7 +42,7 @@ def tile_list_bell_discriminant_kernel(
         work = ctx.enter_context(tc.tile_pool(name="work", bufs=WORK_BUFS))
         psum = ctx.enter_context(tc.psum_pool(name="psum", bufs=4))
         psum_turn = ctx.enter_context(tc.psum_pool(name="psum_turn", bufs=1))
-        psum_last = ctx.enter_context(tc.psum_pool(name="psum_last", bufs=2))
+        psum_last = ctx.enter_context(tc.psum_pool(name="psum_last", bufs=3))
 
         def held(shape, dtype, name):
             return keep.tile(shape, dtype, name=name, align_bytes=64)
@@ -231,7 +231,7 @@ def tile_list_bell_discriminant_kernel(
         finish_h(2)
         for b in range(2):
             nc.gpsimd.tensor_scalar(
-                words_view(wl_bf[:, N * b : N * (b + 1), :]), rows_view(wl_raw[:, b]), 1.0, 0.0, ALU.mult, ALU.add
+                wl_bf[:, N * b : N * (b + 1), :], wl_raw[:, b].rearrange("p t n -> p n t"), 1.0, 0.0, ALU.mult, ALU.add
             )
 
         picks = held([P, 2, PACK, M], F32, "picks0")
@@ -278,9 +278,15 @@ def tile_list_bell_discriminant_kernel(
             square = pick_hum(hums[:, t, :], s, halves[0])
             waiting = (squares[0][:, t, :], square[:], s)
         scale(*waiting)
-        z0_wd = {0: held([P, HALF], U32, "z0_wd")}
-        z0_sc = [held([P, HALF], U8, "z0_sc%d" % j) for j in range(2)]
-        quantize(z0[:, halves[0], :], z0_wd[0][:], z0_sc[0][:])
+        chunks = (halves[0], slice(HALF, HALF + P), slice(HALF + P, M))
+        z0_wd, z0_sc = {}, {}
+
+        def quantize_z0(j, name):
+            width = chunks[j].stop - chunks[j].start
+            z0_wd[j], z0_sc[j] = held([P, width], U32, name), held([P, width], U8, "z0_sc%d" % j)
+            quantize(z0[:, chunks[j], :], z0_wd[j][:], z0_sc[j][:])
+
+        quantize_z0(0, "z0_wd")
         cross = held([P, PACK, HALF], F32, "cross0")
         for t in range(PACK):
             pick_cross(cross[:, t, :], PACK + t, halves[0], primes[t, 0])
@@ -299,47 +305,45 @@ def tile_list_bell_discriminant_kernel(
                 stop=stop,
             )
 
-        chunks = (halves[0], slice(HALF, HALF + P), slice(HALF + P, M))
+        banks = (((0, 1), (2, 3)), ((0, 1), (2, 3)), ((0, 1), (2,), (3,)))
         groups = {}
 
         def open_sums(j):
-            half, first = divmod(chunks[j].start, HALF)
             width = chunks[j].stop - chunks[j].start
-            cols = slice(first, first + width)
-            for c0 in range(0, N_TILES, 2):
+            for tiles in banks[j]:
                 if j < 2:
-                    groups[j, c0] = bank(2 * width)
+                    groups[j, tiles] = bank(len(tiles) * width)
                 else:
-                    groups[j, c0] = psum_last.tile([P, 2 * width], F32, name="last_bank", tag="last_bank")
-                for lo in range(2):
-                    sums = groups[j, c0][:, width * lo : width * (lo + 1)]
-                    second_product(sums, c0 + lo, 0, z0_wd[half][:, cols], z0_sc[half][:, cols], lo == 0, False)
-
-        open_sums(0)
+                    groups[j, tiles] = psum_last.tile([P, len(tiles) * width], F32, name="last_bank", tag="last_bank")
+                for lo, c in enumerate(tiles):
+                    sums = groups[j, tiles][:, width * lo : width * (lo + 1)]
+                    second_product(sums, c, 0, z0_wd[j][:], z0_sc[j][:], lo == 0, False)
 
         def multiply(j, z):
             width = chunks[j].stop - chunks[j].start
             z_wd, z_sc = held([P, width], U32, "z_wd%d" % j), held([P, width], U8, "z_sc%d" % j)
             quantize(z, z_wd[:], z_sc[:])
-            for c in range(N_TILES):
-                c0, lo = c - c % 2, c % 2
-                second_product(groups[j, c0][:, width * lo : width * (lo + 1)], c, 1, z_wd[:], z_sc[:], False, lo == 1)
+            for tiles in banks[j]:
+                for lo, c in enumerate(tiles):
+                    sums = groups[j, tiles][:, width * lo : width * (lo + 1)]
+                    second_product(sums, c, 1, z_wd[:], z_sc[:], False, lo == len(tiles) - 1)
 
         def leave(j, c0, on_vector):
             cols = chunks[j]
             width = cols.stop - cols.start
             result = held([P, 2, width], F32, "result%d%d" % (j, c0))
-            sums = groups[j, c0][:].rearrange("p (c m) -> p c m", c=2)
-            if on_vector:
-                bias = cut_sb[:, c0 : c0 + 2].unsqueeze(2).to_broadcast([P, 2, width])
-                nc.vector.tensor_tensor(result[:], sums, bias, ALU.add)
-            else:
-                for lo in range(2):
-                    c = c0 + lo
-                    nc.scalar.activation(
-                        out=result[:, lo, :], in_=sums[:, lo, :], func=ACT.Identity, bias=cut_sb[:, c : c + 1]
-                    )
+            for tiles in banks[j]:
+                for lo, c in enumerate(tiles):
+                    if c - c % 2 == c0:
+                        sums = groups[j, tiles][:, width * lo : width * (lo + 1)]
+                        bias = cut_sb[:, c : c + 1]
+                        if on_vector:
+                            nc.vector.tensor_scalar(result[:, c - c0, :], sums, bias, None, ALU.add)
+                        else:
+                            nc.scalar.activation(out=result[:, c - c0, :], in_=sums, func=ACT.Identity, bias=bias)
             nc.sync.dma_start(out=out[P * c0 : P * (c0 + 2), cols].rearrange("(c p) m -> p c m", p=P), in_=result[:])
+
+        open_sums(0)
 
         picks = held([P, PACK + kept, HALF], F32, "prime%d0" % (PACK + full))
         for t in range(full, PACK):
@@ -352,10 +356,10 @@ def tile_list_bell_discriminant_kernel(
             waiting = (squares[1][:, t, :], square[:], PACK + t)
         scale(*waiting)
         multiply(0, z_first[:])
-        z0_wd[1] = held([P, HALF], U32, "cross0")
-        quantize(z0[:, halves[1], :], z0_wd[1][:], z0_sc[1][:])
-        for j in (1, 2):
-            open_sums(j)
+        quantize_z0(1, "cross0")
+        open_sums(1)
+        quantize_z0(2, "prime%d0" % (SLICES - 1))
+        open_sums(2)
         cross = held([P, 2, PACK, P], F32, "squares10")
         z_last = [held([P, P, PACK], BF16, "z_last%d" % q) for q in range(2)]
 
@@ -373,10 +377,7 @@ def tile_list_bell_discriminant_kernel(
             quarter_cross(1, t)
         multiply(1, z_last[0][:])
         quarter_difference(1)
-        for c0 in range(0, N_TILES, 2):
-            leave(0, c0, False)
-        leave(1, 0, True)
-        leave(1, 2, False)
         multiply(2, z_last[1][:])
-        leave(2, 0, False)
-        leave(2, 2, True)
+        for j in range(3):
+            for c0 in range(0, N_TILES, 2):
+                leave(j, c0, (j, c0) == (2, 2))

@@ -60,14 +60,15 @@ def tile_list_bell_discriminant_kernel(
         staged = held([P, (S + H) // 4], I32, "staged")
         planes = [held([P, S + H], U8, "planes%d" % a) for a in range(2)]
         w4_raw = {}
-        w4_wd = [held([P, 2, 2 * PASS], U8, "w4_wd%d" % b) for b in range(2)]
+        w4_wd = {}
         tab_wd = [held([P, T], I32, "window%d" % a) for a in range(2)]
         v_wd = [[held([P, BANK], U32, "v_wd%d%d" % (a, u)) for u in range(2)] for a in range(2)]
         vec_rows = [held([P, P], F32, name) for name in ("gain_rows", "cut_rows")]
         ident = held([P, P], F32, "ident")
         gain_sb = held([P, SLICES], F32, "gain_sb")
         cut_sb = held([P, N_TILES], F32, "cut_sb")
-        wl_bf = held([P, 2 * N, PACK], BF16, "wl_bf")
+        wl_parts = (slice(0, N), slice(N, N + N // 2), slice(N + N // 2, 2 * N))
+        wl_bf = [held([P, part.stop - part.start, PACK], BF16, "wl_bf%d" % part.start) for part in wl_parts]
         wl_wd = held([P, 2 * N], U32, "wl_wd")
         wl_sc = held([P, 2 * N], U8, "wl_sc")
         h_sb = [held([P, S], F32, "h_sb%d" % s) for s in range(SLICES)]
@@ -82,21 +83,19 @@ def tile_list_bell_discriminant_kernel(
             nc.gpsimd.memset(vec_rows[1][rows, :], 0.0)
         make_identity(nc, ident[:])
 
-        def load_w4(b, name):
-            w4_raw[b] = held([P, 2, PASS // 2], I32, name)
-            nc.sync.dma_start(
-                out=w4_raw[b][:],
-                in_=w4_words[:, :, 2 * PASS * b : 2 * PASS * (b + 1)].bitcast(I32).rearrange("a p c -> p a c"),
-            )
+        def load_w4(a, b, name):
+            w4_raw[a, b] = held([P, PASS // 2], I32, name)
+            nc.sync.dma_start(out=w4_raw[a, b][:], in_=w4_words[a, :, 2 * PASS * b : 2 * PASS * (b + 1)].bitcast(I32))
 
         nc.scalar.dma_start(out=vec_rows[1][CUT0:32, :], in_=cut.rearrange("(c p) -> c p", p=P))
         nc.sync.dma_start(offs_sb[:], offs)
         for dst, src in ((tab_sc[:].bitcast(I32), tab_scales), (w4_sc_raw[:], w4_scales)):
             for a in range(2):
                 nc.sync.dma_start(out=dst[ROW0[a] : ROW0[a] + BLOCKS, :], in_=src[a].bitcast(I32))
-        load_w4(0, "w4_raw")
+        load_w4(0, 0, "w4_raw00")
         for a in range(2):
             nc.sync.dma_start(out=tab_wd[a][:], in_=tab_words[a].rearrange("p t i -> p (t i)").bitcast(I32))
+        load_w4(1, 0, "w4_raw10")
 
         def turn(rows, row0, cols):
             turned = psum_turn.tile([P, P], F32, name="turned")
@@ -105,11 +104,15 @@ def tile_list_bell_discriminant_kernel(
 
         turn(vec_rows[1], CUT0, cut_sb)
 
-        def order_w4(b, engine):
+        def order_w4(a, s0, count, engine):
+            b, t0 = divmod(s0, PACK)
+            ordered = held([P, count, 2 * P], U8, "w4_wd%d%d" % (a, s0))
             engine.tensor_copy(
-                out=w4_wd[b][:].bitcast(I32).rearrange("p a (t g w) -> p a t g w", t=PACK, w=4),
-                in_=w4_raw[b][:].rearrange("p a (g t w) -> p a t g w", t=PACK, w=4),
+                out=ordered[:].bitcast(I32).rearrange("p t (g w) -> p t g w", w=4),
+                in_=w4_raw[a, b][:].rearrange("p (g t w) -> p t g w", t=PACK, w=4)[:, t0 : t0 + count],
             )
+            for t in range(count):
+                w4_wd[a, s0 + t] = ordered[:, t, :]
 
         def gather_words(a):
             columns = BANK // PER_COLUMN
@@ -124,7 +127,9 @@ def tile_list_bell_discriminant_kernel(
         )
         nc.vector.tensor_copy(picked_sc[:], tab_sc[:].indirect(offs_sb[:]))
         nc.vector.tensor_copy(out=staged[:, : S // 4], in_=picked_sc[:].bitcast(I32))
-        order_w4(0, nc.vector)
+        order_w4(0, 0, PACK, nc.vector)
+        order_w4(1, 0, 1, nc.gpsimd)
+        order_w4(1, 1, PACK - 1, nc.gpsimd)
         for a in range(2):
             for q in range(4):
                 row = ROW0[a] + 4 * q
@@ -133,7 +138,8 @@ def tile_list_bell_discriminant_kernel(
         for list_sb, src in zip(pos_sb, (pos1, pos2, pos3)):
             nc.sync.dma_start(list_sb[:], src)
         gather_words(0)
-        load_w4(1, "window0")
+        for a in range(2):
+            load_w4(a, 1, "w4_raw%d1" % a)
 
         for b in range(2):
             nc.sync.dma_start(
@@ -145,7 +151,6 @@ def tile_list_bell_discriminant_kernel(
 
         def first_product(part, a):
             s, j0, width = part
-            b, t = divmod(s, PACK)
             u, lo = divmod(j0, BANK)
             if a == 0:
                 acc[part] = bank(width)
@@ -153,7 +158,7 @@ def tile_list_bell_discriminant_kernel(
             for j in range(0, width, n):
                 nc.tensor.matmul_mx(
                     out=acc[part][:, j : j + n],
-                    lhsT=w4_wd[b][:, a, 2 * P * t : 2 * P * (t + 1)].bitcast(FP4X4),
+                    lhsT=w4_wd[a, s].bitcast(FP4X4),
                     lhsT_scale=planes[a][:, S + P * s : S + P * (s + 1)],
                     rhs=v_wd[a][u][:, lo + j : lo + j + n].bitcast(FP8X4),
                     rhs_scale=planes[a][:, j0 + j : j0 + j + n],
@@ -176,7 +181,7 @@ def tile_list_bell_discriminant_kernel(
         for part in parts:
             first_product(part, 0)
         gather_words(1)
-        wl_raw = held([P, 2, PACK, N], F32, "cross0")
+        wl_raw = held([P, 2, PACK, N], F32, "wl_raw")
         for b in range(2):
             rows = wl[PASS * b : PASS * (b + 1), :].rearrange("(g t i) n -> t g i n", t=PACK, i=RUN)
             for t in range(PACK):
@@ -184,13 +189,17 @@ def tile_list_bell_discriminant_kernel(
         for part, copy in zip(parts, (nc.scalar.copy, nc.vector.tensor_copy, nc.vector.tensor_copy)):
             first_product(part, 1)
             empty(part, copy)
-        order_w4(1, nc.gpsimd)
+        for a in range(2):
+            order_w4(a, PACK, PACK, nc.gpsimd)
 
         def rows_view(ap):
             return ap.rearrange("p t (c i) -> p c t i", i=2)
 
         def words_view(ap):
             return ap.rearrange("p (c i) t -> p c t i", i=2)
+
+        def in_turn(ap):
+            return ap.rearrange("p t m -> p m t")
 
         def quantize(grouped, codes, scales):
             nc.vector.quantize_mx(out=codes.bitcast(FP8X4), scales=scales, in_=grouped.rearrange("p m t -> p (m t)"))
@@ -208,17 +217,23 @@ def tile_list_bell_discriminant_kernel(
             nc.vector.tensor_copy(picked, window(s, prime_list, cols))
             scale(scaled, picked, s)
 
-        def pick_hum(picked, s, cols):
-            nc.vector.tensor_copy(picked, window(s, hum_list, cols))
-            square = work.tile([P, cols.stop - cols.start], F32, name="square", tag="square")
+        def square_of(picked):
+            square = work.tile([P, picked.shape[1]], F32, name="square", tag="square")
             nc.scalar.activation(out=square[:], in_=picked, func=ACT.Square)
             return square
+
+        def pick_hum(picked, s, cols):
+            nc.vector.tensor_copy(picked, window(s, hum_list, cols))
+            return square_of(picked)
 
         def pick_cross(dst, s, cols, scaled_prime):
             nc.vector.tensor_tensor(dst, window(s, tierce_list, cols), scaled_prime, ALU.mult)
 
         def difference(engine, z, squares, cross):
-            engine.tensor_tensor(words_view(z), rows_view(squares), rows_view(cross), ALU.subtract)
+            if engine is nc.gpsimd:
+                engine.tensor_tensor(z, in_turn(squares), in_turn(cross), ALU.subtract)
+            else:
+                engine.tensor_tensor(words_view(z), rows_view(squares), rows_view(cross), ALU.subtract)
 
         def h_half(s, j0):
             part = (s, j0, BANK)
@@ -229,23 +244,31 @@ def tile_list_bell_discriminant_kernel(
         finish_h(1)
         turn(vec_rows[0], 0, gain_sb)
         finish_h(2)
-        for b in range(2):
-            nc.gpsimd.tensor_scalar(
-                wl_bf[:, N * b : N * (b + 1), :], wl_raw[:, b].rearrange("p t n -> p n t"), 1.0, 0.0, ALU.mult, ALU.add
-            )
+        finish_h(3)
+        for b, width in ((0, N), (1, N // 2)):
+            nc.gpsimd.tensor_scalar(wl_bf[b][:], in_turn(wl_raw[:, b, :, :width]), 1.0, 0.0, ALU.mult, ALU.add)
 
-        picks = held([P, 2, PACK, M], F32, "picks0")
+        picked_primes, hums = held([P, PACK, M], F32, "cross0"), held([P, PACK, M], F32, "hums0")
         squares0 = held([P, PACK, M], F32, "squares0")
         early = held([P, PACK - 1, M], F32, "primes0")
         primes = [early[:, t, :] for t in range(PACK - 1)] + [held([P, M], F32, "prime3")[:]]
+        square = {}
         for s in range(PACK):
-            pick_prime(picks[:, 0, s, :], primes[s], s, whole)
-            square = pick_hum(picks[:, 1, s, :], s, whole)
-            h_half(s + 3, 0)
-            scale(squares0[:, s, :], square[:], s)
-            h_half(s + 3, BANK)
-        finish_h(SLICES - 1)
-        quantize(wl_bf[:], wl_wd[:], wl_sc[:])
+            pick_prime(picked_primes[:, s, :], primes[s], s, whole)
+            nc.vector.tensor_copy(hums[:, s, :], window(s, hum_list, whole))
+            if s == 1:
+                nc.scalar.copy(out=words_view(wl_bf[2][:]), in_=rows_view(wl_raw[:, 1, :, N // 2 :]))
+            if s == 2:
+                square = {t: square_of(hums[:, t, :]) for t in (0, 1)}
+        for t in (0, 1):
+            scale(squares0[:, t, :], square[t][:], t)
+        square = {t: square_of(hums[:, t, :]) for t in (2, 3)}
+        for t in (2, 3):
+            scale(squares0[:, t, :], square[t][:], t)
+        for s in range(PACK, SLICES):
+            finish_h(s)
+        for part, grouped in zip(wl_parts, wl_bf):
+            quantize(grouped[:], wl_wd[:, part], wl_sc[:, part])
         cross = held([P, PACK, M], F32, "cross0")
         for s in range(PACK):
             pick_cross(cross[:, s, :], s, whole, primes[s])
@@ -254,8 +277,8 @@ def tile_list_bell_discriminant_kernel(
 
         kept = 2
         full = PACK - kept
-        picks = held([P, full * M + kept * HALF + PACK * HALF], F32, "primes0")
-        hums = picks[:, full * M + kept * HALF :].rearrange("p (t m) -> p t m", t=PACK)
+        picks, half_picks = held([P, full, M], F32, "primes0"), held([P, kept, HALF], F32, "half_picks")
+        hums = held([P, PACK, HALF], F32, "prime3")
         full_primes = held([P, full, M], F32, "primes1")
         primes = {}
         for t in range(PACK):
@@ -269,10 +292,9 @@ def tile_list_bell_discriminant_kernel(
         for t in range(PACK):
             s = PACK + t
             if t < full:
-                pick_prime(picks[:, M * t : M * (t + 1)], full_primes[:, t, :], s, whole)
+                pick_prime(picks[:, t, :], full_primes[:, t, :], s, whole)
             else:
-                lo = M * full + HALF * (t - full)
-                pick_prime(picks[:, lo : lo + HALF], primes[t, 0], s, halves[0])
+                pick_prime(half_picks[:, t - full, :], primes[t, 0], s, halves[0])
             if waiting is not None:
                 scale(*waiting)
             square = pick_hum(hums[:, t, :], s, halves[0])
@@ -281,13 +303,12 @@ def tile_list_bell_discriminant_kernel(
         chunks = (halves[0], slice(HALF, HALF + P), slice(HALF + P, M))
         z0_wd, z0_sc = {}, {}
 
-        def quantize_z0(j, name):
-            width = chunks[j].stop - chunks[j].start
-            z0_wd[j], z0_sc[j] = held([P, width], U32, name), held([P, width], U8, "z0_sc%d" % j)
-            quantize(z0[:, chunks[j], :], z0_wd[j][:], z0_sc[j][:])
+        def quantize_z0(j, codes):
+            z0_wd[j], z0_sc[j] = codes, held([P, codes.shape[1]], U8, "z0_sc%d" % j)
+            quantize(z0[:, chunks[j], :], codes, z0_sc[j][:])
 
-        quantize_z0(0, "z0_wd")
-        cross = held([P, PACK, HALF], F32, "cross0")
+        quantize_z0(0, held([P, HALF], U32, "primes0")[:])
+        cross = held([P, PACK, HALF], F32, "half_picks")
         for t in range(PACK):
             pick_cross(cross[:, t, :], PACK + t, halves[0], primes[t, 0])
         z_first = held([P, HALF, PACK], BF16, "z_first")
@@ -317,7 +338,7 @@ def tile_list_bell_discriminant_kernel(
                     groups[j, tiles] = psum_last.tile([P, len(tiles) * width], F32, name="last_bank", tag="last_bank")
                 for lo, c in enumerate(tiles):
                     sums = groups[j, tiles][:, width * lo : width * (lo + 1)]
-                    second_product(sums, c, 0, z0_wd[j][:], z0_sc[j][:], lo == 0, False)
+                    second_product(sums, c, 0, z0_wd[j], z0_sc[j][:], lo == 0, False)
 
         def multiply(j, z):
             width = chunks[j].stop - chunks[j].start
@@ -356,9 +377,9 @@ def tile_list_bell_discriminant_kernel(
             waiting = (squares[1][:, t, :], square[:], PACK + t)
         scale(*waiting)
         multiply(0, z_first[:])
-        quantize_z0(1, "cross0")
+        quantize_z0(1, held([P, P], U32, "half_picks")[:])
         open_sums(1)
-        quantize_z0(2, "prime%d0" % (SLICES - 1))
+        quantize_z0(2, held([P, P], U32, "prime%d0" % (SLICES - 1))[:])
         open_sums(2)
         cross = held([P, 2, PACK, P], F32, "squares10")
         z_last = [held([P, P, PACK], BF16, "z_last%d" % q) for q in range(2)]

@@ -230,10 +230,7 @@ def tile_list_bell_discriminant_kernel(
             nc.vector.tensor_tensor(dst, window(s, tierce_list, cols), scaled_prime, ALU.mult)
 
         def difference(engine, z, squares, cross):
-            if engine is nc.gpsimd:
-                engine.tensor_tensor(z, in_turn(squares), in_turn(cross), ALU.subtract)
-            else:
-                engine.tensor_tensor(words_view(z), rows_view(squares), rows_view(cross), ALU.subtract)
+            engine.tensor_tensor(words_view(z), rows_view(squares), rows_view(cross), ALU.subtract)
 
         def h_half(s, j0):
             part = (s, j0, BANK)

@@ -29,7 +29,8 @@ SLICES = H // P
 N_TILES = N // P
 HALF = M // 2
 CUT0 = 32 - N_TILES
-WORK_BUFS = 2
+EARLY_HUMS = 256
+WORK_BUFS = 4
 
 
 def tile_list_bell_discriminant_kernel(
@@ -127,7 +128,7 @@ def tile_list_bell_discriminant_kernel(
         )
         nc.vector.tensor_copy(picked_sc[:], tab_sc[:].indirect(offs_sb[:]))
         nc.vector.tensor_copy(out=staged[:, : S // 4], in_=picked_sc[:].bitcast(I32))
-        order_w4(0, 0, PACK, nc.vector)
+        order_w4(0, 0, PACK, nc.gpsimd)
         order_w4(1, 0, 1, nc.gpsimd)
         order_w4(1, 1, PACK - 1, nc.gpsimd)
         for a in range(2):
@@ -272,44 +273,48 @@ def tile_list_bell_discriminant_kernel(
         z0 = held([P, M, PACK], BF16, "z0")
         difference(nc.gpsimd, z0[:], squares0[:], cross[:])
 
-        kept = 2
-        full = PACK - kept
-        picks, half_picks = held([P, full, M], F32, "primes0"), held([P, kept, HALF], F32, "half_picks")
-        hums = held([P, PACK, HALF], F32, "prime3")
-        full_primes = held([P, full, M], F32, "primes1")
-        primes = {}
-        for t in range(PACK):
-            for j in range(2):
-                if t < full:
-                    primes[t, j] = full_primes[:, t, halves[j]]
-                else:
-                    primes[t, j] = held([P, HALF], F32, "prime%d%d" % (PACK + t, j))[:]
-        squares = [held([P, PACK, HALF], F32, "squares1%d" % j) for j in range(2)]
+        chunks = (halves[0], slice(HALF, HALF + P), slice(HALF + P, M))
+        front, first, second, back = slice(0, M - P), slice(0, EARLY_HUMS), slice(EARLY_HUMS, M - P), chunks[2]
+
+        def width_of(cols):
+            return cols.stop - cols.start
+
+        def square_run(cols, hums, name):
+            squares = held([P, PACK, width_of(cols)], F32, name)
+            waiting = None
+            for t in range(PACK):
+                square = pick_hum(hums[:, t, :], PACK + t, cols)
+                if waiting is not None:
+                    scale(*waiting)
+                waiting = (squares[:, t, :], square[:], PACK + t)
+            scale(*waiting)
+            return squares
+
+        picked = [held([P, 2, M - P], F32, name) for name in ("primes0", "picked_primes67")]
+        hums = held([P, PACK, EARLY_HUMS], F32, "prime3")
+        primes = [held([P, M - P], F32, "front_prime%d" % t) for t in range(PACK)]
+        first_squares = held([P, PACK, EARLY_HUMS], F32, "first_squares")
         waiting = None
         for t in range(PACK):
             s = PACK + t
-            if t < full:
-                pick_prime(picks[:, t, :], full_primes[:, t, :], s, whole)
-            else:
-                pick_prime(half_picks[:, t - full, :], primes[t, 0], s, halves[0])
+            pick_prime(picked[t // 2][:, t % 2, :], primes[t][:], s, front)
             if waiting is not None:
                 scale(*waiting)
-            square = pick_hum(hums[:, t, :], s, halves[0])
-            waiting = (squares[0][:, t, :], square[:], s)
+            square = pick_hum(hums[:, t, :], s, first)
+            waiting = (first_squares[:, t, :], square[:], s)
         scale(*waiting)
-        chunks = (halves[0], slice(HALF, HALF + P), slice(HALF + P, M))
         z0_wd, z0_sc = {}, {}
 
-        def quantize_z0(j, codes):
-            z0_wd[j], z0_sc[j] = codes, held([P, codes.shape[1]], U8, "z0_sc%d" % j)
-            quantize(z0[:, chunks[j], :], codes, z0_sc[j][:])
+        def quantize_z0(j, name):
+            z0_wd[j], z0_sc[j] = held([P, HALF], U32, name), held([P, HALF], U8, "z0_sc%d" % j)
+            quantize(z0[:, halves[j], :], z0_wd[j][:], z0_sc[j][:])
 
-        quantize_z0(0, held([P, HALF], U32, "primes0")[:])
-        cross = held([P, PACK, HALF], F32, "half_picks")
+        quantize_z0(0, "primes0")
+        cross = held([P, PACK, M - P], F32, "picked_primes67")
         for t in range(PACK):
-            pick_cross(cross[:, t, :], PACK + t, halves[0], primes[t, 0])
-        z_first = held([P, HALF, PACK], BF16, "z_first")
-        difference(nc.gpsimd, z_first[:], squares[0][:], cross[:])
+            pick_cross(cross[:, t, :], PACK + t, front, primes[t][:])
+        z_front = held([P, M - P, PACK], BF16, "z_front")
+        difference(nc.gpsimd, z_front[:, first, :], first_squares[:], cross[:, :, first])
 
         def second_product(sums, c, b, z_wd, z_sc, start, stop):
             cols = slice(N * b + P * c, N * b + P * (c + 1))
@@ -327,7 +332,9 @@ def tile_list_bell_discriminant_kernel(
         groups = {}
 
         def open_sums(j):
-            width = chunks[j].stop - chunks[j].start
+            width = width_of(chunks[j])
+            half, lo0 = divmod(chunks[j].start, HALF)
+            cols = slice(lo0, lo0 + width)
             for tiles in banks[j]:
                 if j < 2:
                     groups[j, tiles] = bank(len(tiles) * width)
@@ -335,11 +342,11 @@ def tile_list_bell_discriminant_kernel(
                     groups[j, tiles] = psum_last.tile([P, len(tiles) * width], F32, name="last_bank", tag="last_bank")
                 for lo, c in enumerate(tiles):
                     sums = groups[j, tiles][:, width * lo : width * (lo + 1)]
-                    second_product(sums, c, 0, z0_wd[j], z0_sc[j][:], lo == 0, False)
+                    second_product(sums, c, 0, z0_wd[half][:, cols], z0_sc[half][:, cols], lo == 0, False)
 
-        def multiply(j, z):
-            width = chunks[j].stop - chunks[j].start
-            z_wd, z_sc = held([P, width], U32, "z_wd%d" % j), held([P, width], U8, "z_sc%d" % j)
+        def multiply(j, z, name):
+            width = width_of(chunks[j])
+            z_wd, z_sc = held([P, width], U32, name), held([P, width], U8, "z_sc%d" % j)
             quantize(z, z_wd[:], z_sc[:])
             for tiles in banks[j]:
                 for lo, c in enumerate(tiles):
@@ -363,39 +370,25 @@ def tile_list_bell_discriminant_kernel(
 
         open_sums(0)
 
-        picks = held([P, PACK + kept, HALF], F32, "prime%d0" % (PACK + full))
-        for t in range(full, PACK):
-            pick_prime(picks[:, PACK + t - full, :], primes[t, 1], PACK + t, halves[1])
-        waiting = None
+        hums = held([P, PACK, width_of(second)], F32, "front_prime2")
+        second_squares = square_run(second, hums, "second_squares")
+        difference(nc.gpsimd, z_front[:, second, :], second_squares[:], cross[:, :, second])
+        picked = held([P, 2, PACK, P], F32, "front_prime3")
+        primes = [held([P, P], F32, "back_prime%d" % t) for t in range(PACK)]
         for t in range(PACK):
-            square = pick_hum(picks[:, t, :], PACK + t, halves[1])
-            if waiting is not None:
-                scale(*waiting)
-            waiting = (squares[1][:, t, :], square[:], PACK + t)
-        scale(*waiting)
-        multiply(0, z_first[:])
-        quantize_z0(1, held([P, P], U32, "half_picks")[:])
-        open_sums(1)
-        quantize_z0(2, held([P, P], U32, "prime%d0" % (SLICES - 1))[:])
-        open_sums(2)
-        cross = held([P, 2, PACK, P], F32, "squares10")
-        z_last = [held([P, P, PACK], BF16, "z_last%d" % q) for q in range(2)]
-
-        def quarter_cross(q, t):
-            pick_cross(cross[:, q, t, :], PACK + t, chunks[1 + q], primes[t, 1][:, P * q : P * (q + 1)])
-
-        def quarter_difference(q):
-            difference(nc.vector, z_last[q][:], squares[1][:, :, P * q : P * (q + 1)], cross[:, q])
-
+            pick_prime(picked[:, 0, t, :], primes[t][:], PACK + t, back)
+        back_squares = square_run(back, picked[:, 1], "back_squares")
+        multiply(0, z_front[:, chunks[0], :], "z_wd0")
+        quantize_z0(1, "picked_primes67")
+        for j in (1, 2):
+            open_sums(j)
+        cross = held([P, PACK, P], F32, "second_squares")
         for t in range(PACK):
-            quarter_cross(0, t)
-        quarter_cross(1, 0)
-        quarter_difference(0)
-        for t in range(1, PACK):
-            quarter_cross(1, t)
-        multiply(1, z_last[0][:])
-        quarter_difference(1)
-        multiply(2, z_last[1][:])
+            pick_cross(cross[:, t, :], PACK + t, back, primes[t][:])
+        multiply(1, z_front[:, chunks[1], :], "back_prime2")
+        z_back = held([P, P, PACK], BF16, "z_back")
+        difference(nc.vector, z_back[:], back_squares[:], cross[:])
+        multiply(2, z_back[:], "z_wd2")
         for j in range(3):
             for c0 in range(0, N_TILES, 2):
                 leave(j, c0, (j, c0) == (2, 2))

@@ -306,8 +306,9 @@ def tile_list_bell_discriminant_kernel(
         z0_wd, z0_sc = {}, {}
 
         def quantize_z0(j, name):
-            z0_wd[j], z0_sc[j] = held([P, HALF], U32, name), held([P, HALF], U8, "z0_sc%d" % j)
-            quantize(z0[:, halves[j], :], z0_wd[j][:], z0_sc[j][:])
+            width = width_of(chunks[j])
+            z0_wd[j], z0_sc[j] = held([P, width], U32, name), held([P, width], U8, "z0_sc%d" % j)
+            quantize(z0[:, chunks[j], :], z0_wd[j][:], z0_sc[j][:])
 
         quantize_z0(0, "primes0")
         cross = held([P, PACK, M - P], F32, "picked_primes67")
@@ -333,8 +334,6 @@ def tile_list_bell_discriminant_kernel(
 
         def open_sums(j):
             width = width_of(chunks[j])
-            half, lo0 = divmod(chunks[j].start, HALF)
-            cols = slice(lo0, lo0 + width)
             for tiles in banks[j]:
                 if j < 2:
                     groups[j, tiles] = bank(len(tiles) * width)
@@ -342,7 +341,7 @@ def tile_list_bell_discriminant_kernel(
                     groups[j, tiles] = psum_last.tile([P, len(tiles) * width], F32, name="last_bank", tag="last_bank")
                 for lo, c in enumerate(tiles):
                     sums = groups[j, tiles][:, width * lo : width * (lo + 1)]
-                    second_product(sums, c, 0, z0_wd[half][:, cols], z0_sc[half][:, cols], lo == 0, False)
+                    second_product(sums, c, 0, z0_wd[j][:], z0_sc[j][:], lo == 0, False)
 
         def multiply(j, z, name):
             width = width_of(chunks[j])
@@ -380,12 +379,13 @@ def tile_list_bell_discriminant_kernel(
         back_squares = square_run(back, picked[:, 1], "back_squares")
         multiply(0, z_front[:, chunks[0], :], "z_wd0")
         quantize_z0(1, "picked_primes67")
-        for j in (1, 2):
-            open_sums(j)
+        open_sums(1)
+        multiply(1, z_front[:, chunks[1], :], "z_wd1")
         cross = held([P, PACK, P], F32, "second_squares")
         for t in range(PACK):
             pick_cross(cross[:, t, :], PACK + t, back, primes[t][:])
-        multiply(1, z_front[:, chunks[1], :], "back_prime2")
+        quantize_z0(2, "back_prime2")
+        open_sums(2)
         z_back = held([P, P, PACK], BF16, "z_back")
         difference(nc.vector, z_back[:], back_squares[:], cross[:])
         multiply(2, z_back[:], "z_wd2")

@@ -29,8 +29,6 @@ SLICES = H // P
 N_TILES = N // P
 HALF = M // 2
 CUT0 = 32 - N_TILES
-EARLY_HUMS = 256
-WORK_BUFS = 4
 
 
 def tile_list_bell_discriminant_kernel(
@@ -40,16 +38,13 @@ def tile_list_bell_discriminant_kernel(
     with ExitStack() as ctx:
         lists = ctx.enter_context(tc.tile_pool(name="lists", bufs=1))
         keep = ctx.enter_context(tc.tile_pool(name="keep", bufs=1))
-        work = ctx.enter_context(tc.tile_pool(name="work", bufs=WORK_BUFS))
-        psum = ctx.enter_context(tc.psum_pool(name="psum", bufs=4))
-        psum_turn = ctx.enter_context(tc.psum_pool(name="psum_turn", bufs=1))
-        psum_last = ctx.enter_context(tc.psum_pool(name="psum_last", bufs=3))
+        psum = ctx.enter_context(tc.psum_pool(name="psum", bufs=1))
 
         def held(shape, dtype, name):
             return keep.tile(shape, dtype, name=name, align_bytes=64)
 
-        def bank(width):
-            return psum.tile([P, width], F32, name="bank", tag="bank")
+        def bank(number, width):
+            return psum.tile([P, width], F32, name="bank%d" % number)
 
         offs_sb = lists.tile([P, S // PER_COLUMN], U16, name="offs_sb")
         pos_sb = [lists.tile([P, M // PER_COLUMN], U16, name="pos_sb%d" % i) for i in range(3)]
@@ -68,8 +63,7 @@ def tile_list_bell_discriminant_kernel(
         ident = held([P, P], F32, "ident")
         gain_sb = held([P, SLICES], F32, "gain_sb")
         cut_sb = held([P, N_TILES], F32, "cut_sb")
-        wl_parts = (slice(0, N), slice(N, N + N // 2), slice(N + N // 2, 2 * N))
-        wl_bf = [held([P, part.stop - part.start, PACK], BF16, "wl_bf%d" % part.start) for part in wl_parts]
+        wl_parts = (slice(0, N), slice(N, N + P), slice(N + P, 2 * N))
         wl_wd = held([P, 2 * N], U32, "wl_wd")
         wl_sc = held([P, 2 * N], U8, "wl_sc")
         h_sb = [held([P, S], F32, "h_sb%d" % s) for s in range(SLICES)]
@@ -98,12 +92,12 @@ def tile_list_bell_discriminant_kernel(
             nc.sync.dma_start(out=tab_wd[a][:], in_=tab_words[a].rearrange("p t i -> p (t i)").bitcast(I32))
         load_w4(1, 0, "w4_raw10")
 
-        def turn(rows, row0, cols):
-            turned = psum_turn.tile([P, P], F32, name="turned")
+        def turn(rows, row0, cols, copy):
+            turned = bank(7, P)
             nc.tensor.transpose(turned[:], rows[:], ident[:])
-            nc.scalar.copy(out=cols[:], in_=turned[:, row0 : row0 + cols.shape[1]])
+            copy(out=cols[:], in_=turned[:, row0 : row0 + cols.shape[1]])
 
-        turn(vec_rows[1], CUT0, cut_sb)
+        turn(vec_rows[1], CUT0, cut_sb, nc.scalar.copy)
 
         def order_w4(a, s0, count, engine):
             b, t0 = divmod(s0, PACK)
@@ -150,48 +144,52 @@ def tile_list_bell_discriminant_kernel(
 
         acc = {}
 
-        def first_product(part, a):
+        def first_product(part, a, number=None):
             s, j0, width = part
             u, lo = divmod(j0, BANK)
             if a == 0:
-                acc[part] = bank(width)
-            n = BANK if width == BANK else P
-            for j in range(0, width, n):
-                nc.tensor.matmul_mx(
-                    out=acc[part][:, j : j + n],
-                    lhsT=w4_wd[a, s].bitcast(FP4X4),
-                    lhsT_scale=planes[a][:, S + P * s : S + P * (s + 1)],
-                    rhs=v_wd[a][u][:, lo + j : lo + j + n].bitcast(FP8X4),
-                    rhs_scale=planes[a][:, j0 + j : j0 + j + n],
-                    start=(a == 0 and j == 0),
-                    stop=(a == 1 and j + n == width),
-                )
+                acc[part] = bank(number, width)
+            nc.tensor.matmul_mx(
+                out=acc[part][:],
+                lhsT=w4_wd[a, s].bitcast(FP4X4),
+                lhsT_scale=planes[a][:, S + P * s : S + P * (s + 1)],
+                rhs=v_wd[a][u][:, lo : lo + width].bitcast(FP8X4),
+                rhs_scale=planes[a][:, j0 : j0 + width],
+                start=(a == 0),
+                stop=(a == 1),
+            )
 
         def empty(part, copy):
             s, j0, width = part
             copy(out=h_sb[s][:, j0 : j0 + width], in_=acc[part][:])
 
-        def finish_h(s):
-            for j0 in (0, BANK):
-                part = (s, j0, BANK)
-                first_product(part, 0)
-                first_product(part, 1)
-                empty(part, nc.scalar.copy)
-
-        parts = [(0, 0, BANK), (0, BANK, HALF), (0, BANK + HALF, HALF)]
-        for part in parts:
-            first_product(part, 0)
+        fronts = [(s, 0, BANK) for s in range(3)]
+        backs = [(0, BANK, HALF), (0, BANK + HALF, HALF), (1, BANK, BANK), (2, BANK, BANK), (3, 0, BANK)]
+        for number, part in enumerate(fronts + backs):
+            first_product(part, 0, number)
         gather_words(1)
-        wl_raw = held([P, 2, PACK, N], F32, "wl_raw")
+        wl_raw = [held([P, PACK, N], F32, "wl_raw%d" % b) for b in range(2)]
         for b in range(2):
             rows = wl[PASS * b : PASS * (b + 1), :].rearrange("(g t i) n -> t g i n", t=PACK, i=RUN)
             for t in range(PACK):
-                nc.sync.dma_start(out=wl_raw[:, b, t, :], in_=rows[t])
-        for part, copy in zip(parts, (nc.scalar.copy, nc.vector.tensor_copy, nc.vector.tensor_copy)):
+                nc.sync.dma_start(out=wl_raw[b][:, t, :], in_=rows[t])
+        for part in fronts:
             first_product(part, 1)
-            empty(part, copy)
+            empty(part, nc.scalar.copy)
+        for part in backs:
+            first_product(part, 1)
+            empty(part, nc.vector.tensor_copy)
         for a in range(2):
             order_w4(a, PACK, PACK, nc.gpsimd)
+
+        def h_half(s, u, number, copy):
+            part = (s, BANK * u, BANK)
+            first_product(part, 0, number)
+            first_product(part, 1)
+            empty(part, copy)
+
+        h_half(3, 1, 0, nc.vector.tensor_copy)
+        turn(vec_rows[0], 0, gain_sb, nc.vector.tensor_copy)
 
         def rows_view(ap):
             return ap.rearrange("p t (c i) -> p c t i", i=2)
@@ -205,190 +203,159 @@ def tile_list_bell_discriminant_kernel(
         def quantize(grouped, codes, scales):
             nc.vector.quantize_mx(out=codes.bitcast(FP8X4), scales=scales, in_=grouped.rearrange("p m t -> p (m t)"))
 
-        whole = slice(0, M)
-        halves = (slice(0, HALF), slice(HALF, M))
+        def width_of(cols):
+            return cols.stop - cols.start
 
         def window(s, picks, cols):
             return h_sb[s][:].indirect(picks[:, cols.start // PER_COLUMN : cols.stop // PER_COLUMN])
 
-        def scale(dst, src, s):
-            nc.scalar.activation(out=dst, in_=src, func=ACT.Copy, scale=gain_sb[:, s : s + 1])
+        def pick(name, s, picks, cols, on_vector=False):
+            picked = held([P, width_of(cols)], F32, name)
+            if on_vector:
+                nc.vector.tensor_copy(picked[:], window(s, picks, cols))
+            else:
+                nc.scalar.activation(picked[:], window(s, picks, cols), ACT.Copy)
+            return picked
 
-        def pick_prime(picked, scaled, s, cols):
-            nc.vector.tensor_copy(picked, window(s, prime_list, cols))
-            scale(scaled, picked, s)
+        def product(dst, left, right, s):
+            nc.vector.scalar_tensor_tensor(dst, left, gain_sb[:, s : s + 1], right, ALU.mult, ALU.mult)
 
-        def square_of(picked):
-            square = work.tile([P, picked.shape[1]], F32, name="square", tag="square")
-            nc.scalar.activation(out=square[:], in_=picked, func=ACT.Square)
-            return square
-
-        def pick_hum(picked, s, cols):
-            nc.vector.tensor_copy(picked, window(s, hum_list, cols))
-            return square_of(picked)
-
-        def pick_cross(dst, s, cols, scaled_prime):
-            nc.vector.tensor_tensor(dst, window(s, tierce_list, cols), scaled_prime, ALU.mult)
-
-        def difference(engine, z, squares, cross):
-            engine.tensor_tensor(words_view(z), rows_view(squares), rows_view(cross), ALU.subtract)
-
-        def h_half(s, j0):
-            part = (s, j0, BANK)
-            first_product(part, 0)
-            first_product(part, 1)
-            empty(part, nc.scalar.copy)
-
-        finish_h(1)
-        turn(vec_rows[0], 0, gain_sb)
-        finish_h(2)
-        finish_h(3)
-        for b, width in ((0, N), (1, N // 2)):
-            nc.gpsimd.tensor_scalar(wl_bf[b][:], in_turn(wl_raw[:, b, :, :width]), 1.0, 0.0, ALU.mult, ALU.add)
-
-        picked_primes, hums = held([P, PACK, M], F32, "cross0"), held([P, PACK, M], F32, "hums0")
-        squares0 = held([P, PACK, M], F32, "squares0")
-        early = held([P, PACK - 1, M], F32, "primes0")
-        primes = [early[:, t, :] for t in range(PACK - 1)] + [held([P, M], F32, "prime3")[:]]
-        square = {}
-        for s in range(PACK):
-            pick_prime(picked_primes[:, s, :], primes[s], s, whole)
-            nc.vector.tensor_copy(hums[:, s, :], window(s, hum_list, whole))
-            if s == 1:
-                nc.scalar.copy(out=words_view(wl_bf[2][:]), in_=rows_view(wl_raw[:, 1, :, N // 2 :]))
-            if s == 2:
-                square = {t: square_of(hums[:, t, :]) for t in (0, 1)}
-        for t in (0, 1):
-            scale(squares0[:, t, :], square[t][:], t)
-        square = {t: square_of(hums[:, t, :]) for t in (2, 3)}
-        for t in (2, 3):
-            scale(squares0[:, t, :], square[t][:], t)
-        for s in range(PACK, SLICES):
-            finish_h(s)
-        for part, grouped in zip(wl_parts, wl_bf):
-            quantize(grouped[:], wl_wd[:, part], wl_sc[:, part])
-        cross = held([P, PACK, M], F32, "cross0")
-        for s in range(PACK):
-            pick_cross(cross[:, s, :], s, whole, primes[s])
-        z0 = held([P, M, PACK], BF16, "z0")
-        difference(nc.gpsimd, z0[:], squares0[:], cross[:])
-
-        chunks = (halves[0], slice(HALF, HALF + P), slice(HALF + P, M))
-        front, first, second, back = slice(0, M - P), slice(0, EARLY_HUMS), slice(EARLY_HUMS, M - P), chunks[2]
-
-        def width_of(cols):
-            return cols.stop - cols.start
-
-        def square_run(cols, hums, name):
-            squares = held([P, PACK, width_of(cols)], F32, name)
-            waiting = None
-            for t in range(PACK):
-                square = pick_hum(hums[:, t, :], PACK + t, cols)
-                if waiting is not None:
-                    scale(*waiting)
-                waiting = (squares[:, t, :], square[:], PACK + t)
-            scale(*waiting)
-            return squares
-
-        picked = [held([P, 2, M - P], F32, name) for name in ("primes0", "picked_primes67")]
-        hums = held([P, PACK, EARLY_HUMS], F32, "prime3")
-        primes = [held([P, M - P], F32, "front_prime%d" % t) for t in range(PACK)]
-        first_squares = held([P, PACK, EARLY_HUMS], F32, "first_squares")
-        waiting = None
-        for t in range(PACK):
-            s = PACK + t
-            pick_prime(picked[t // 2][:, t % 2, :], primes[t][:], s, front)
-            if waiting is not None:
-                scale(*waiting)
-            square = pick_hum(hums[:, t, :], s, first)
-            waiting = (first_squares[:, t, :], square[:], s)
-        scale(*waiting)
-        z0_wd, z0_sc = {}, {}
-
-        def quantize_z0(j, name):
-            width = width_of(chunks[j])
-            z0_wd[j], z0_sc[j] = held([P, width], U32, name), held([P, width], U8, "z0_sc%d" % j)
-            quantize(z0[:, chunks[j], :], z0_wd[j][:], z0_sc[j][:])
-
-        quantize_z0(0, "primes0")
-        cross = held([P, PACK, M - P], F32, "picked_primes67")
-        for t in range(PACK):
-            pick_cross(cross[:, t, :], PACK + t, front, primes[t][:])
-        z_front = held([P, M - P, PACK], BF16, "z_front")
-        difference(nc.gpsimd, z_front[:, first, :], first_squares[:], cross[:, :, first])
-
-        def second_product(sums, c, b, z_wd, z_sc, start, stop):
-            cols = slice(N * b + P * c, N * b + P * (c + 1))
-            nc.tensor.matmul_mx(
-                out=sums,
-                lhsT=wl_wd[:, cols].bitcast(FP8X4),
-                lhsT_scale=wl_sc[:, cols],
-                rhs=z_wd.bitcast(FP8X4),
-                rhs_scale=z_sc,
-                start=start,
-                stop=stop,
+        def difference(engine, name, squares, crosses, cols):
+            z = held([P, width_of(cols), PACK], BF16, name)
+            engine.tensor_tensor(
+                words_view(z[:]), rows_view(squares[:, :, cols]), rows_view(crosses[:, :, cols]), ALU.subtract
             )
+            return z
 
-        banks = (((0, 1), (2, 3)), ((0, 1), (2, 3)), ((0, 1), (2,), (3,)))
-        groups = {}
+        whole = slice(0, M)
+        front, back = slice(0, HALF), slice(HALF, M)
+        chunks = (front, slice(HALF, HALF + P), slice(HALF + P, M))
 
-        def open_sums(j):
+        wl_bf = {}
+
+        def cast_wl(k, name):
+            b, n0 = divmod(wl_parts[k].start, N)
+            width = width_of(wl_parts[k])
+            wl_bf[k] = held([P, width, PACK], BF16, name)
+            nc.gpsimd.tensor_scalar(wl_bf[k][:], in_turn(wl_raw[b][:, :, n0 : n0 + width]), 1.0, 0.0, ALU.mult, ALU.add)
+
+        def tierces_of(pair):
+            return {s: pick("tierce%d" % s, s, tierce_list, whole, on_vector=True) for s in pair}
+
+        def combine(s, tierce):
+            b, t = divmod(s, PACK)
+            prime = pick("prime%d" % s, s, prime_list, whole)
+            hum = pick("hum%d" % s, s, hum_list, whole)
+            product(crosses[b][:, t, :], prime[:], tierce[:], s)
+            product(squares[b][:, t, :], hum[:], hum[:], s)
+
+        squares = [held([P, PACK, M], F32, "squares%d" % b) for b in range(2)]
+        crosses = [held([P, PACK, M], F32, "crosses%d" % b) for b in range(2)]
+        cast_wl(0, "wl_bf0")
+        cast_wl(1, "wl_bf1")
+        tierce = tierces_of((0, 1))
+        combine(0, tierce[0])
+        combine(1, tierce[1])
+        cast_wl(2, "hum1")
+        tierce = tierces_of((2, 3))
+        combine(2, tierce[2])
+        for k, part in enumerate(wl_parts):
+            quantize(wl_bf[k][:], wl_wd[:, part], wl_sc[:, part])
+        combine(3, tierce[3])
+        z0_front = difference(nc.gpsimd, "z0_front", squares[0], crosses[0], front)
+
+        z_wd, z_sc = {}, {}
+
+        def quantize_z(b, j, z, name):
             width = width_of(chunks[j])
-            for tiles in banks[j]:
-                if j < 2:
-                    groups[j, tiles] = bank(len(tiles) * width)
-                else:
-                    groups[j, tiles] = psum_last.tile([P, len(tiles) * width], F32, name="last_bank", tag="last_bank")
-                for lo, c in enumerate(tiles):
-                    sums = groups[j, tiles][:, width * lo : width * (lo + 1)]
-                    second_product(sums, c, 0, z0_wd[j][:], z0_sc[j][:], lo == 0, False)
+            z_wd[b, j], z_sc[b, j] = held([P, width], U32, name), held([P, width], U8, "z_sc%d%d" % (b, j))
+            quantize(z, z_wd[b, j][:], z_sc[b, j][:])
 
-        def multiply(j, z, name):
+        homes = (((1, (0, 1)), (2, (2, 3))), ((3, (0, 1, 2)), (4, (3,))), ((0, (0, 1)), (7, (2,)), (5, (3,))))
+        sums = {}
+
+        def second_product(b, j):
             width = width_of(chunks[j])
-            z_wd, z_sc = held([P, width], U32, name), held([P, width], U8, "z_sc%d" % j)
-            quantize(z, z_wd[:], z_sc[:])
-            for tiles in banks[j]:
-                for lo, c in enumerate(tiles):
-                    sums = groups[j, tiles][:, width * lo : width * (lo + 1)]
-                    second_product(sums, c, 1, z_wd[:], z_sc[:], False, lo == len(tiles) - 1)
+            for number, tiles in homes[j]:
+                if b == 0:
+                    group = bank(number, len(tiles) * width)
+                    for lo, c in enumerate(tiles):
+                        sums[j, c] = group[:, width * lo : width * (lo + 1)]
+                for c in tiles:
+                    cols = slice(N * b + P * c, N * b + P * (c + 1))
+                    nc.tensor.matmul_mx(
+                        out=sums[j, c],
+                        lhsT=wl_wd[:, cols].bitcast(FP8X4),
+                        lhsT_scale=wl_sc[:, cols],
+                        rhs=z_wd[b, j][:].bitcast(FP8X4),
+                        rhs_scale=z_sc[b, j][:],
+                        start=(b == 0 and c == tiles[0]),
+                        stop=(b == 1 and c == tiles[-1]),
+                    )
 
-        def leave(j, c0, on_vector):
-            cols = chunks[j]
-            width = cols.stop - cols.start
-            result = held([P, 2, width], F32, "result%d%d" % (j, c0))
-            for tiles in banks[j]:
-                for lo, c in enumerate(tiles):
-                    if c - c % 2 == c0:
-                        sums = groups[j, tiles][:, width * lo : width * (lo + 1)]
-                        bias = cut_sb[:, c : c + 1]
-                        if on_vector:
-                            nc.vector.tensor_scalar(result[:, c - c0, :], sums, bias, None, ALU.add)
-                        else:
-                            nc.scalar.activation(out=result[:, c - c0, :], in_=sums, func=ACT.Identity, bias=bias)
-            nc.sync.dma_start(out=out[P * c0 : P * (c0 + 2), cols].rearrange("(c p) m -> p c m", p=P), in_=result[:])
+        results = {}
 
-        open_sums(0)
+        def add_cut(j, c, c0, count, on_vector):
+            if (j, c0) not in results:
+                results[j, c0] = held([P, count, width_of(chunks[j])], F32, "result%d%d" % (j, c0))
+            dst, bias = results[j, c0][:, c - c0, :], cut_sb[:, c : c + 1]
+            if on_vector:
+                nc.vector.tensor_scalar(dst, sums[j, c], bias, None, ALU.add)
+            else:
+                nc.scalar.activation(out=dst, in_=sums[j, c], func=ACT.Identity, bias=bias)
 
-        hums = held([P, PACK, width_of(second)], F32, "front_prime2")
-        second_squares = square_run(second, hums, "second_squares")
-        difference(nc.gpsimd, z_front[:, second, :], second_squares[:], cross[:, :, second])
-        picked = held([P, 2, PACK, P], F32, "front_prime3")
-        primes = [held([P, P], F32, "back_prime%d" % t) for t in range(PACK)]
-        for t in range(PACK):
-            pick_prime(picked[:, 0, t, :], primes[t][:], PACK + t, back)
-        back_squares = square_run(back, picked[:, 1], "back_squares")
-        multiply(0, z_front[:, chunks[0], :], "z_wd0")
-        quantize_z0(1, "picked_primes67")
-        open_sums(1)
-        multiply(1, z_front[:, chunks[1], :], "z_wd1")
-        cross = held([P, PACK, P], F32, "second_squares")
-        for t in range(PACK):
-            pick_cross(cross[:, t, :], PACK + t, back, primes[t][:])
-        quantize_z0(2, "back_prime2")
-        open_sums(2)
-        z_back = held([P, P, PACK], BF16, "z_back")
-        difference(nc.vector, z_back[:], back_squares[:], cross[:])
-        multiply(2, z_back[:], "z_wd2")
-        for j in range(3):
-            for c0 in range(0, N_TILES, 2):
-                leave(j, c0, (j, c0) == (2, 2))
+        def store(j, c0):
+            result = results[j, c0]
+            rows = out[P * c0 : P * (c0 + result.shape[1]), chunks[j]]
+            nc.sync.dma_start(out=rows.rearrange("(c p) m -> p c m", p=P), in_=result[:])
+
+        def finish_h(pair):
+            for s, numbers in zip(pair, ((0, 7), (5, 6))):
+                for u in range(2):
+                    h_half(s, u, numbers[u], nc.scalar.copy)
+
+        finish_h((4, 5))
+        tierce = tierces_of((4, 5))
+        combine(4, tierce[4])
+        combine(5, tierce[5])
+        z0_back = difference(nc.gpsimd, "hum5", squares[0], crosses[0], back)
+        finish_h((6, 7))
+        tierce = tierces_of((6, 7))
+        prime = {s: pick("prime%d" % s, s, prime_list, whole) for s in (6, 7)}
+        hum = {(s, cols.start): pick("hum%d_%d" % (s, cols.start), s, hum_list, cols) for cols in (front, back) for s in (6, 7)}
+
+        def square(s, cols):
+            product(squares[1][:, s - PACK, cols], hum[s, cols.start][:], hum[s, cols.start][:], s)
+
+        product(crosses[1][:, 2, :], prime[6][:], tierce[6][:], 6)
+        quantize_z(0, 0, z0_front[:], "z_wd00")
+        second_product(0, 0)
+        product(crosses[1][:, 3, :], prime[7][:], tierce[7][:], 7)
+        square(6, front)
+        square(7, front)
+        quantize_z(0, 1, z0_back[:, :P, :], "z_wd01")
+        second_product(0, 1)
+        z = difference(nc.vector, "z10", squares[1], crosses[1], front)
+        square(6, back)
+        quantize_z(1, 0, z[:], "z_wd10")
+        second_product(1, 0)
+        square(7, back)
+        for c in range(N_TILES):
+            add_cut(0, c, c - c % 2, 2, False)
+            if c % 2 == 1:
+                store(0, c - 1)
+        quantize_z(0, 2, z0_back[:, P:, :], "z_wd02")
+        second_product(0, 2)
+        z = difference(nc.vector, "z11", squares[1], crosses[1], chunks[1])
+        last_z = difference(nc.vector, "z12", squares[1], crosses[1], chunks[2])
+        quantize_z(1, 1, z[:], "z_wd11")
+        second_product(1, 1)
+        quantize_z(1, 2, last_z[:], "z_wd12")
+        second_product(1, 2)
+        for c in range(N_TILES):
+            add_cut(1, c, 0, N_TILES, False)
+        store(1, 0)
+        for c in range(N_TILES):
+            add_cut(2, c, c - c % 2, 2, True)
+            if c % 2 == 1:
+                store(2, c - 1)

@@ -63,7 +63,7 @@ def tile_list_bell_discriminant_kernel(
         ident = held([P, P], F32, "ident")
         gain_sb = held([P, SLICES], F32, "gain_sb")
         cut_sb = held([P, N_TILES], F32, "cut_sb")
-        wl_parts = (slice(0, N), slice(N, N + P), slice(N + P, 2 * N))
+        wl_parts = (slice(0, N), slice(N, N + N // 2), slice(N + N // 2, 2 * N))
         wl_wd = held([P, 2 * N], U32, "wl_wd")
         wl_sc = held([P, 2 * N], U8, "wl_sc")
         h_sb = [held([P, S], F32, "h_sb%d" % s) for s in range(SLICES)]
@@ -79,8 +79,8 @@ def tile_list_bell_discriminant_kernel(
         make_identity(nc, ident[:])
 
         def load_w4(a, b, name):
-            w4_raw[a, b] = held([P, PASS // 2], I32, name)
-            nc.sync.dma_start(out=w4_raw[a, b][:], in_=w4_words[a, :, 2 * PASS * b : 2 * PASS * (b + 1)].bitcast(I32))
+            w4_raw[a, b] = held([P, PASS // 2], I32, name)[:]
+            nc.sync.dma_start(out=w4_raw[a, b], in_=w4_words[a, :, 2 * PASS * b : 2 * PASS * (b + 1)].bitcast(I32))
 
         nc.scalar.dma_start(out=vec_rows[1][CUT0:32, :], in_=cut.rearrange("(c p) -> c p", p=P))
         nc.sync.dma_start(offs_sb[:], offs)
@@ -104,7 +104,7 @@ def tile_list_bell_discriminant_kernel(
             ordered = held([P, count, 2 * P], U8, "w4_wd%d%d" % (a, s0))
             engine.tensor_copy(
                 out=ordered[:].bitcast(I32).rearrange("p t (g w) -> p t g w", w=4),
-                in_=w4_raw[a, b][:].rearrange("p (g t w) -> p t g w", t=PACK, w=4)[:, t0 : t0 + count],
+                in_=w4_raw[a, b].rearrange("p (g t w) -> p t g w", t=PACK, w=4)[:, t0 : t0 + count],
             )
             for t in range(count):
                 w4_wd[a, s0 + t] = ordered[:, t, :]
@@ -133,14 +133,24 @@ def tile_list_bell_discriminant_kernel(
         for list_sb, src in zip(pos_sb, (pos1, pos2, pos3)):
             nc.sync.dma_start(list_sb[:], src)
         gather_words(0)
-        for a in range(2):
-            load_w4(a, 1, "w4_raw%d1" % a)
+        wl_raw = [held([P, PACK, N], F32, "wl_raw%d" % b) for b in range(2)]
 
+        def load_wl(b):
+            rows = wl[PASS * b : PASS * (b + 1), :].rearrange("(g t i) n -> t g i n", t=PACK, i=RUN)
+            for t in range(PACK):
+                nc.sync.dma_start(out=wl_raw[b][:, t, :], in_=rows[t])
+
+        late_w4 = held([P, 2, PASS // 2], I32, "late_w4")
+        nc.sync.dma_start(out=late_w4[:], in_=w4_words[:, :, 2 * PASS :].bitcast(I32).rearrange("a p w -> p a w"))
+        for a in range(2):
+            w4_raw[a, 1] = late_w4[:, a, :]
+        load_wl(0)
         for b in range(2):
             nc.sync.dma_start(
                 out=vec_rows[0][PACK * b : PACK * (b + 1), :],
                 in_=gain[PASS * b : PASS * (b + 1)].rearrange("(g t i) -> t g i", t=PACK, i=RUN),
             )
+        load_wl(1)
 
         acc = {}
 
@@ -168,19 +178,12 @@ def tile_list_bell_discriminant_kernel(
         for number, part in enumerate(fronts + backs):
             first_product(part, 0, number)
         gather_words(1)
-        wl_raw = [held([P, PACK, N], F32, "wl_raw%d" % b) for b in range(2)]
-        for b in range(2):
-            rows = wl[PASS * b : PASS * (b + 1), :].rearrange("(g t i) n -> t g i n", t=PACK, i=RUN)
-            for t in range(PACK):
-                nc.sync.dma_start(out=wl_raw[b][:, t, :], in_=rows[t])
         for part in fronts:
             first_product(part, 1)
             empty(part, nc.scalar.copy)
         for part in backs:
             first_product(part, 1)
             empty(part, nc.vector.tensor_copy)
-        for a in range(2):
-            order_w4(a, PACK, PACK, nc.gpsimd)
 
         def h_half(s, u, number, copy):
             part = (s, BANK * u, BANK)
@@ -233,11 +236,15 @@ def tile_list_bell_discriminant_kernel(
 
         wl_bf = {}
 
-        def cast_wl(k, name):
+        def cast_wl(k, name, on_vector=False):
             b, n0 = divmod(wl_parts[k].start, N)
             width = width_of(wl_parts[k])
             wl_bf[k] = held([P, width, PACK], BF16, name)
-            nc.gpsimd.tensor_scalar(wl_bf[k][:], in_turn(wl_raw[b][:, :, n0 : n0 + width]), 1.0, 0.0, ALU.mult, ALU.add)
+            rows = wl_raw[b][:, :, n0 : n0 + width]
+            if on_vector:
+                nc.vector.tensor_copy(out=words_view(wl_bf[k][:]), in_=rows_view(rows))
+            else:
+                nc.gpsimd.tensor_scalar(wl_bf[k][:], in_turn(rows), 1.0, 0.0, ALU.mult, ALU.add)
 
         def tierces_of(pair):
             return {s: pick("tierce%d" % s, s, tierce_list, whole, on_vector=True) for s in pair}
@@ -251,18 +258,17 @@ def tile_list_bell_discriminant_kernel(
 
         squares = [held([P, PACK, M], F32, "squares%d" % b) for b in range(2)]
         crosses = [held([P, PACK, M], F32, "crosses%d" % b) for b in range(2)]
+        for a in range(2):
+            order_w4(a, PACK, PACK, nc.gpsimd)
         cast_wl(0, "wl_bf0")
-        cast_wl(1, "wl_bf1")
         tierce = tierces_of((0, 1))
         combine(0, tierce[0])
         combine(1, tierce[1])
-        cast_wl(2, "hum1")
+        cast_wl(1, "hum1")
         tierce = tierces_of((2, 3))
         combine(2, tierce[2])
-        for k, part in enumerate(wl_parts):
-            quantize(wl_bf[k][:], wl_wd[:, part], wl_sc[:, part])
         combine(3, tierce[3])
-        z0_front = difference(nc.gpsimd, "z0_front", squares[0], crosses[0], front)
+        z0 = difference(nc.gpsimd, "z0", squares[0], crosses[0], whole)
 
         z_wd, z_sc = {}, {}
 
@@ -315,12 +321,13 @@ def tile_list_bell_discriminant_kernel(
                     h_half(s, u, numbers[u], nc.scalar.copy)
 
         finish_h((4, 5))
-        tierce = tierces_of((4, 5))
-        combine(4, tierce[4])
-        combine(5, tierce[5])
-        z0_back = difference(nc.gpsimd, "hum5", squares[0], crosses[0], back)
         finish_h((6, 7))
-        tierce = tierces_of((6, 7))
+        tierce = tierces_of(range(PACK, SLICES))
+        cast_wl(2, "wl_bf2", on_vector=True)
+        combine(4, tierce[4])
+        for k, part in enumerate(wl_parts):
+            quantize(wl_bf[k][:], wl_wd[:, part], wl_sc[:, part])
+        combine(5, tierce[5])
         prime = {s: pick("prime%d" % s, s, prime_list, whole) for s in (6, 7)}
         hum = {(s, cols.start): pick("hum%d_%d" % (s, cols.start), s, hum_list, cols) for cols in (front, back) for s in (6, 7)}
 
@@ -328,12 +335,12 @@ def tile_list_bell_discriminant_kernel(
             product(squares[1][:, s - PACK, cols], hum[s, cols.start][:], hum[s, cols.start][:], s)
 
         product(crosses[1][:, 2, :], prime[6][:], tierce[6][:], 6)
-        quantize_z(0, 0, z0_front[:], "z_wd00")
+        quantize_z(0, 0, z0[:, chunks[0], :], "z_wd00")
         second_product(0, 0)
         product(crosses[1][:, 3, :], prime[7][:], tierce[7][:], 7)
         square(6, front)
         square(7, front)
-        quantize_z(0, 1, z0_back[:, :P, :], "z_wd01")
+        quantize_z(0, 1, z0[:, chunks[1], :], "z_wd01")
         second_product(0, 1)
         z = difference(nc.vector, "z10", squares[1], crosses[1], front)
         square(6, back)
@@ -344,7 +351,7 @@ def tile_list_bell_discriminant_kernel(
             add_cut(0, c, c - c % 2, 2, False)
             if c % 2 == 1:
                 store(0, c - 1)
-        quantize_z(0, 2, z0_back[:, P:, :], "z_wd02")
+        quantize_z(0, 2, z0[:, chunks[2], :], "z_wd02")
         second_product(0, 2)
         z = difference(nc.vector, "z11", squares[1], crosses[1], chunks[1])
         last_z = difference(nc.vector, "z12", squares[1], crosses[1], chunks[2])
@@ -353,9 +360,9 @@ def tile_list_bell_discriminant_kernel(
         quantize_z(1, 2, last_z[:], "z_wd12")
         second_product(1, 2)
         for c in range(N_TILES):
-            add_cut(1, c, 0, N_TILES, False)
+            add_cut(1, c, 0, N_TILES, c == 3)
         store(1, 0)
         for c in range(N_TILES):
-            add_cut(2, c, c - c % 2, 2, True)
+            add_cut(2, c, c - c % 2, 2, c >= 2)
             if c % 2 == 1:
                 store(2, c - 1)

@@ -64,7 +64,6 @@ def tile_list_bell_discriminant_kernel(
         gain_sb = held([P, SLICES], F32, "gain_sb")
         cut_sb = held([P, N_TILES], F32, "cut_sb")
         wl_parts = (slice(0, N), slice(N, N + N // 2), slice(N + N // 2, 2 * N))
-        wl_wd = held([P, 2 * N], U32, "wl_wd")
         wl_sc = held([P, 2 * N], U8, "wl_sc")
         h_sb = [held([P, S], F32, "h_sb%d" % s) for s in range(SLICES)]
 
@@ -277,7 +276,7 @@ def tile_list_bell_discriminant_kernel(
             z_wd[b, j], z_sc[b, j] = held([P, width], U32, name), held([P, width], U8, "z_sc%d%d" % (b, j))
             quantize(z, z_wd[b, j][:], z_sc[b, j][:])
 
-        homes = (((1, (0, 1)), (2, (2, 3))), ((3, (0, 1, 2)), (4, (3,))), ((0, (0, 1)), (7, (2,)), (5, (3,))))
+        homes = (((1, (0, 1)), (2, (2, 3))), ((3, (0, 1, 2)), (4, (3,))), ((5, (0,)), (6, (1,)), (0, (2,)), (7, (3,))))
         sums = {}
 
         def second_product(b, j):
@@ -315,21 +314,19 @@ def tile_list_bell_discriminant_kernel(
             rows = out[P * c0 : P * (c0 + result.shape[1]), chunks[j]]
             nc.sync.dma_start(out=rows.rearrange("(c p) m -> p c m", p=P), in_=result[:])
 
-        def finish_h(pair):
-            for s, numbers in zip(pair, ((0, 7), (5, 6))):
-                for u in range(2):
-                    h_half(s, u, numbers[u], nc.scalar.copy)
-
-        finish_h((4, 5))
-        finish_h((6, 7))
-        tierce = tierces_of(range(PACK, SLICES))
-        cast_wl(2, "wl_bf2", on_vector=True)
+        for number, (s, u) in zip((1, 2, 3, 4, 5, 6, 0), ((s, u) for s in range(PACK, SLICES) for u in range(2))):
+            h_half(s, u, number, nc.scalar.copy)
+        tierce = tierces_of((4, 5))
+        h_half(7, 1, 7, nc.vector.tensor_copy)
+        tierce.update(tierces_of((6, 7)))
         combine(4, tierce[4])
+        cast_wl(2, "squares0", on_vector=True)
+        wl_wd = held([P, 2 * N], U32, "crosses0")
+        combine(5, tierce[5])
         for k, part in enumerate(wl_parts):
             quantize(wl_bf[k][:], wl_wd[:, part], wl_sc[:, part])
-        combine(5, tierce[5])
         prime = {s: pick("prime%d" % s, s, prime_list, whole) for s in (6, 7)}
-        hum = {(s, cols.start): pick("hum%d_%d" % (s, cols.start), s, hum_list, cols) for cols in (front, back) for s in (6, 7)}
+        hum = {(s, cols.start): pick("hum%d_%d" % (s, cols.start), s, hum_list, cols) for cols in chunks for s in (6, 7)}
 
         def square(s, cols):
             product(squares[1][:, s - PACK, cols], hum[s, cols.start][:], hum[s, cols.start][:], s)
@@ -343,26 +340,28 @@ def tile_list_bell_discriminant_kernel(
         quantize_z(0, 1, z0[:, chunks[1], :], "z_wd01")
         second_product(0, 1)
         z = difference(nc.vector, "z10", squares[1], crosses[1], front)
-        square(6, back)
+        square(6, chunks[1])
+        square(7, chunks[1])
         quantize_z(1, 0, z[:], "z_wd10")
         second_product(1, 0)
-        square(7, back)
         for c in range(N_TILES):
             add_cut(0, c, c - c % 2, 2, False)
             if c % 2 == 1:
                 store(0, c - 1)
-        quantize_z(0, 2, z0[:, chunks[2], :], "z_wd02")
-        second_product(0, 2)
         z = difference(nc.vector, "z11", squares[1], crosses[1], chunks[1])
-        last_z = difference(nc.vector, "z12", squares[1], crosses[1], chunks[2])
+        square(6, chunks[2])
+        square(7, chunks[2])
         quantize_z(1, 1, z[:], "z_wd11")
         second_product(1, 1)
-        quantize_z(1, 2, last_z[:], "z_wd12")
+        quantize_z(0, 2, z0[:, chunks[2], :], "hum7_256")
+        second_product(0, 2)
+        z = difference(nc.vector, "z12", squares[1], crosses[1], chunks[2])
+        for c in range(N_TILES):
+            add_cut(1, c, 0, N_TILES, False)
+        store(1, 0)
+        quantize_z(1, 2, z[:], "z_wd12")
         second_product(1, 2)
         for c in range(N_TILES):
-            add_cut(1, c, 0, N_TILES, c == 3)
-        store(1, 0)
-        for c in range(N_TILES):
-            add_cut(2, c, c - c % 2, 2, c >= 2)
+            add_cut(2, c, c - c % 2, 2, c % 2 == 1)
             if c % 2 == 1:
                 store(2, c - 1)

@@ -314,11 +314,9 @@ def tile_list_bell_discriminant_kernel(
             rows = out[P * c0 : P * (c0 + result.shape[1]), chunks[j]]
             nc.sync.dma_start(out=rows.rearrange("(c p) m -> p c m", p=P), in_=result[:])
 
-        for number, (s, u) in zip((1, 2, 3, 4, 5, 6, 0), ((s, u) for s in range(PACK, SLICES) for u in range(2))):
+        for number, (s, u) in zip((1, 2, 3, 4, 5, 6, 0, 7), ((s, u) for s in range(PACK, SLICES) for u in range(2))):
             h_half(s, u, number, nc.scalar.copy)
-        tierce = tierces_of((4, 5))
-        h_half(7, 1, 7, nc.vector.tensor_copy)
-        tierce.update(tierces_of((6, 7)))
+        tierce = tierces_of(range(PACK, SLICES))
         combine(4, tierce[4])
         cast_wl(2, "squares0", on_vector=True)
         wl_wd = held([P, 2 * N], U32, "crosses0")

@@ -245,8 +245,8 @@ def tile_list_bell_discriminant_kernel(
             else:
                 nc.gpsimd.tensor_scalar(wl_bf[k][:], in_turn(rows), 1.0, 0.0, ALU.mult, ALU.add)
 
-        def tierces_of(pair):
-            return {s: pick("tierce%d" % s, s, tierce_list, whole, on_vector=True) for s in pair}
+        def tierces_of(slices, names):
+            return {s: pick(name, s, tierce_list, whole, on_vector=True) for s, name in zip(slices, names)}
 
         def combine(s, tierce):
             b, t = divmod(s, PACK)
@@ -260,13 +260,10 @@ def tile_list_bell_discriminant_kernel(
         for a in range(2):
             order_w4(a, PACK, PACK, nc.gpsimd)
         cast_wl(0, "wl_bf0")
-        tierce = tierces_of((0, 1))
-        combine(0, tierce[0])
-        combine(1, tierce[1])
-        cast_wl(1, "hum1")
-        tierce = tierces_of((2, 3))
-        combine(2, tierce[2])
-        combine(3, tierce[3])
+        cast_wl(1, "wl_bf1")
+        tierce = tierces_of(range(PACK), ["tierce%d" % s for s in range(PACK)])
+        for s in range(PACK):
+            combine(s, tierce[s])
         z0 = difference(nc.gpsimd, "z0", squares[0], crosses[0], whole)
 
         z_wd, z_sc = {}, {}
@@ -316,32 +313,44 @@ def tile_list_bell_discriminant_kernel(
 
         for number, (s, u) in zip((1, 2, 3, 4, 5, 6, 0, 7), ((s, u) for s in range(PACK, SLICES) for u in range(2))):
             h_half(s, u, number, nc.scalar.copy)
-        tierce = tierces_of(range(PACK, SLICES))
+        tierce = tierces_of(range(PACK, SLICES), ("prime2", "prime3", "tierce2", "tierce3"))
         combine(4, tierce[4])
         cast_wl(2, "squares0", on_vector=True)
         wl_wd = held([P, 2 * N], U32, "crosses0")
         combine(5, tierce[5])
         for k, part in enumerate(wl_parts):
             quantize(wl_bf[k][:], wl_wd[:, part], wl_sc[:, part])
-        prime = {s: pick("prime%d" % s, s, prime_list, whole) for s in (6, 7)}
-        hum = {(s, cols.start): pick("hum%d_%d" % (s, cols.start), s, hum_list, cols) for cols in chunks for s in (6, 7)}
+        prime, hum = {}, {}
+        for s in (6, 7):
+            prime[s, 0] = pick("prime%d_0" % s, s, prime_list, front)
+            hum[s, 0] = pick("hum%d_0" % s, s, hum_list, front)
+        for s in (6, 7):
+            prime[s, HALF] = pick("prime%d_256" % s, s, prime_list, back)
+        for cols in chunks[1:]:
+            for s in (6, 7):
+                hum[s, cols.start] = pick("hum%d_%d" % (s, cols.start), s, hum_list, cols)
+
+        def cross(s, cols):
+            product(crosses[1][:, s - PACK, cols], prime[s, cols.start][:], tierce[s][:, cols], s)
 
         def square(s, cols):
             product(squares[1][:, s - PACK, cols], hum[s, cols.start][:], hum[s, cols.start][:], s)
 
-        product(crosses[1][:, 2, :], prime[6][:], tierce[6][:], 6)
+        cross(6, front)
+        square(6, front)
         quantize_z(0, 0, z0[:, chunks[0], :], "z_wd00")
         second_product(0, 0)
-        product(crosses[1][:, 3, :], prime[7][:], tierce[7][:], 7)
-        square(6, front)
+        cross(7, front)
         square(7, front)
         quantize_z(0, 1, z0[:, chunks[1], :], "z_wd01")
         second_product(0, 1)
         z = difference(nc.vector, "z10", squares[1], crosses[1], front)
-        square(6, chunks[1])
-        square(7, chunks[1])
+        cross(6, back)
         quantize_z(1, 0, z[:], "z_wd10")
         second_product(1, 0)
+        cross(7, back)
+        square(6, chunks[1])
+        square(7, chunks[1])
         for c in range(N_TILES):
             add_cut(0, c, c - c % 2, 2, False)
             if c % 2 == 1:

@@ -63,7 +63,7 @@ def tile_list_bell_discriminant_kernel(
         ident = held([P, P], F32, "ident")
         gain_sb = held([P, SLICES], F32, "gain_sb")
         cut_sb = held([P, N_TILES], F32, "cut_sb")
-        wl_parts = (slice(0, N), slice(N, N + N // 2), slice(N + N // 2, 2 * N))
+        wl_parts = (slice(0, N), slice(N, N + P), slice(N + P, 2 * N))
         wl_sc = held([P, 2 * N], U8, "wl_sc")
         h_sb = [held([P, S], F32, "h_sb%d" % s) for s in range(SLICES)]
 
@@ -311,9 +311,11 @@ def tile_list_bell_discriminant_kernel(
             rows = out[P * c0 : P * (c0 + result.shape[1]), chunks[j]]
             nc.sync.dma_start(out=rows.rearrange("(c p) m -> p c m", p=P), in_=result[:])
 
-        for number, (s, u) in zip((1, 2, 3, 4, 5, 6, 0, 7), ((s, u) for s in range(PACK, SLICES) for u in range(2))):
+        for number, (s, u) in zip((1, 2, 3, 4, 5, 6, 0), ((s, u) for s in range(PACK, SLICES) for u in range(2))):
             h_half(s, u, number, nc.scalar.copy)
-        tierce = tierces_of(range(PACK, SLICES), ("prime2", "prime3", "tierce2", "tierce3"))
+        tierce = tierces_of((4, 5), ("prime2", "prime3"))
+        h_half(7, 1, 7, nc.vector.tensor_copy)
+        tierce.update(tierces_of((6, 7), ("tierce2", "tierce3")))
         combine(4, tierce[4])
         cast_wl(2, "squares0", on_vector=True)
         wl_wd = held([P, 2 * N], U32, "crosses0")

@@ -108,12 +108,13 @@ def tile_list_bell_discriminant_kernel(
             for t in range(count):
                 w4_wd[a, s0 + t] = ordered[:, t, :]
 
-        def gather_words(a):
-            columns = BANK // PER_COLUMN
-            for u in range(2):
-                nc.vector.tensor_copy(
-                    v_wd[a][u][:], tab_wd[a][:].bitcast(U32).indirect(offs_sb[:, columns * u : columns * (u + 1)])
-                )
+        def gather_words(a, widths):
+            j0 = 0
+            for width in widths:
+                u, lo = divmod(j0, BANK)
+                entries = offs_sb[:, j0 // PER_COLUMN : (j0 + width) // PER_COLUMN]
+                nc.vector.tensor_copy(v_wd[a][u][:, lo : lo + width], tab_wd[a][:].bitcast(U32).indirect(entries))
+                j0 = j0 + width
 
         nc.vector.tensor_copy(
             out=staged[:, S // 4 :].rearrange("p (b t g w) -> p b t g w", b=2, t=PACK, w=2),
@@ -131,7 +132,7 @@ def tile_list_bell_discriminant_kernel(
                 queue.dma_start(out=planes[a][32 * q : 32 * q + 4, :].bitcast(I32), in_=staged[row : row + 4, :])
         for list_sb, src in zip(pos_sb, (pos1, pos2, pos3)):
             nc.sync.dma_start(list_sb[:], src)
-        gather_words(0)
+        gather_words(0, (BANK, BANK))
         wl_raw = [held([P, PACK, N], F32, "wl_raw%d" % b) for b in range(2)]
 
         def load_wl(b):
@@ -176,7 +177,7 @@ def tile_list_bell_discriminant_kernel(
         backs = [(0, BANK, HALF), (0, BANK + HALF, HALF), (1, BANK, BANK), (2, BANK, BANK), (3, 0, BANK)]
         for number, part in enumerate(fronts + backs):
             first_product(part, 0, number)
-        gather_words(1)
+        gather_words(1, (BANK, HALF, HALF))
         for part in fronts:
             first_product(part, 1)
             empty(part, nc.scalar.copy)
@@ -261,7 +262,7 @@ def tile_list_bell_discriminant_kernel(
             order_w4(a, PACK, PACK, nc.gpsimd)
         cast_wl(0, "wl_bf0")
         cast_wl(1, "wl_bf1")
-        tierce = tierces_of(range(PACK), ["tierce%d" % s for s in range(PACK)])
+        tierce = tierces_of(range(PACK), ("tierce0", "tierce1", "tierce2", "gain_rows"))
         for s in range(PACK):
             combine(s, tierce[s])
         z0 = difference(nc.gpsimd, "z0", squares[0], crosses[0], whole)
@@ -315,7 +316,7 @@ def tile_list_bell_discriminant_kernel(
             h_half(s, u, number, nc.scalar.copy)
         tierce = tierces_of((4, 5), ("prime2", "prime3"))
         h_half(7, 1, 7, nc.vector.tensor_copy)
-        tierce.update(tierces_of((6, 7), ("tierce2", "tierce3")))
+        tierce.update(tierces_of((6, 7), ("tierce2", "gain_rows")))
         combine(4, tierce[4])
         cast_wl(2, "squares0", on_vector=True)
         wl_wd = held([P, 2 * N], U32, "crosses0")

@@ -28,6 +28,7 @@ ROW0 = (48, 112)
 SLICES = H // P
 N_TILES = N // P
 HALF = M // 2
+PLACES = {"window0": 0, "wl_raw0": 0, "late_w4": 8192, "gain_rows": 12288}
 CUT0 = 32 - N_TILES
 
 
@@ -38,9 +39,12 @@ def tile_list_bell_discriminant_kernel(
     with ExitStack() as ctx:
         lists = ctx.enter_context(tc.tile_pool(name="lists", bufs=1))
         keep = ctx.enter_context(tc.tile_pool(name="keep", bufs=1))
+        reuse = ctx.enter_context(tc.tile_pool(name="reuse", bufs=1))
         psum = ctx.enter_context(tc.psum_pool(name="psum", bufs=1))
 
         def held(shape, dtype, name):
+            if name in PLACES:
+                return reuse.tile(shape, dtype, name=name, align_bytes=64, offset=PLACES[name])
             return keep.tile(shape, dtype, name=name, align_bytes=64)
 
         def bank(number, width):
@@ -54,12 +58,12 @@ def tile_list_bell_discriminant_kernel(
         picked_sc = held([P, S], U8, "picked_sc")
         w4_sc_raw = held([P, H // 4], I32, "w4_sc_raw")
         staged = held([P, (S + H) // 4], I32, "staged")
-        planes = [held([P, S + H], U8, "planes%d" % a) for a in range(2)]
+        planes = {0: held([P, S + H], U8, "planes0")}
         w4_raw = {}
         w4_wd = {}
         tab_wd = [held([P, T], I32, "window%d" % a) for a in range(2)]
         v_wd = [[held([P, BANK], U32, "v_wd%d%d" % (a, u)) for u in range(2)] for a in range(2)]
-        vec_rows = [held([P, P], F32, name) for name in ("gain_rows", "cut_rows")]
+        cut_rows = held([P, P], F32, "cut_rows")
         ident = held([P, P], F32, "ident")
         gain_sb = held([P, SLICES], F32, "gain_sb")
         cut_sb = held([P, N_TILES], F32, "cut_sb")
@@ -70,33 +74,39 @@ def tile_list_bell_discriminant_kernel(
         for a in range(2):
             nc.vector.memset(tab_sc[64 * a : ROW0[a], :].bitcast(I32), 0)
             nc.vector.memset(w4_sc_raw[64 * a : ROW0[a], :], 0)
-        for a in range(2):
-            nc.vector.memset(planes[a][:].bitcast(I32), 0)
-        nc.gpsimd.memset(vec_rows[0][:], 0.0)
+        nc.vector.memset(planes[0][:].bitcast(I32), 0)
         for rows in (slice(0, CUT0), slice(32, 64), slice(64, P)):
-            nc.gpsimd.memset(vec_rows[1][rows, :], 0.0)
+            nc.gpsimd.memset(cut_rows[rows, :], 0.0)
         make_identity(nc, ident[:])
 
-        def load_w4(a, b, name):
-            w4_raw[a, b] = held([P, PASS // 2], I32, name)[:]
-            nc.sync.dma_start(out=w4_raw[a, b], in_=w4_words[a, :, 2 * PASS * b : 2 * PASS * (b + 1)].bitcast(I32))
+        def load_w4(b, name):
+            both = held([P, 2, PASS // 2], I32, name)
+            cols = w4_words[:, :, 2 * PASS * b : 2 * PASS * (b + 1)]
+            nc.sync.dma_start(out=both[:], in_=cols.bitcast(I32).rearrange("a p w -> p a w"))
+            for a in range(2):
+                w4_raw[a, b] = both[:, a, :]
 
-        nc.scalar.dma_start(out=vec_rows[1][CUT0:32, :], in_=cut.rearrange("(c p) -> c p", p=P))
+        nc.scalar.dma_start(out=cut_rows[CUT0:32, :], in_=cut.rearrange("(c p) -> c p", p=P))
         nc.sync.dma_start(offs_sb[:], offs)
         for dst, src in ((tab_sc[:].bitcast(I32), tab_scales), (w4_sc_raw[:], w4_scales)):
             for a in range(2):
                 nc.sync.dma_start(out=dst[ROW0[a] : ROW0[a] + BLOCKS, :], in_=src[a].bitcast(I32))
-        load_w4(0, 0, "w4_raw00")
-        for a in range(2):
+        load_w4(0, "early_w4")
+
+        def load_table(a):
             nc.sync.dma_start(out=tab_wd[a][:], in_=tab_words[a].rearrange("p t i -> p (t i)").bitcast(I32))
-        load_w4(1, 0, "w4_raw10")
+
+        load_table(0)
+        load_table(1)
+        for list_sb, src in zip(pos_sb, (pos1, pos2, pos3)):
+            nc.sync.dma_start(list_sb[:], src)
 
         def turn(rows, row0, cols, copy):
             turned = bank(7, P)
             nc.tensor.transpose(turned[:], rows[:], ident[:])
             copy(out=cols[:], in_=turned[:, row0 : row0 + cols.shape[1]])
 
-        turn(vec_rows[1], CUT0, cut_sb, nc.scalar.copy)
+        turn(cut_rows, CUT0, cut_sb, nc.scalar.copy)
 
         def order_w4(a, s0, count, engine):
             b, t0 = divmod(s0, PACK)
@@ -122,35 +132,33 @@ def tile_list_bell_discriminant_kernel(
         )
         nc.vector.tensor_copy(picked_sc[:], tab_sc[:].indirect(offs_sb[:]))
         nc.vector.tensor_copy(out=staged[:, : S // 4], in_=picked_sc[:].bitcast(I32))
+        planes[1] = held([P, S + H], U8, "tab_sc")
+        nc.vector.memset(planes[1][:].bitcast(I32), 0)
         order_w4(0, 0, PACK, nc.gpsimd)
-        order_w4(1, 0, 1, nc.gpsimd)
-        order_w4(1, 1, PACK - 1, nc.gpsimd)
+        order_w4(1, 0, PACK, nc.gpsimd)
         for a in range(2):
-            for q in range(4):
-                row = ROW0[a] + 4 * q
-                queue = nc.sync if a == 1 and q % 2 == 1 else nc.scalar
-                queue.dma_start(out=planes[a][32 * q : 32 * q + 4, :].bitcast(I32), in_=staged[row : row + 4, :])
-        for list_sb, src in zip(pos_sb, (pos1, pos2, pos3)):
-            nc.sync.dma_start(list_sb[:], src)
+            for y in range(4):
+                queue = (nc.scalar, nc.sync)[a]
+                queue.dma_start(
+                    out=planes[a][y:P:32, :].bitcast(I32), in_=staged[ROW0[a] + y : ROW0[a] + BLOCKS : 4, :]
+                )
         gather_words(0, (BANK, BANK))
-        wl_raw = [held([P, PACK, N], F32, "wl_raw%d" % b) for b in range(2)]
+        wl_raw = {0: held([P, PACK, N], F32, "wl_raw0")}
 
         def load_wl(b):
             rows = wl[PASS * b : PASS * (b + 1), :].rearrange("(g t i) n -> t g i n", t=PACK, i=RUN)
             for t in range(PACK):
                 nc.sync.dma_start(out=wl_raw[b][:, t, :], in_=rows[t])
 
-        late_w4 = held([P, 2, PASS // 2], I32, "late_w4")
-        nc.sync.dma_start(out=late_w4[:], in_=w4_words[:, :, 2 * PASS :].bitcast(I32).rearrange("a p w -> p a w"))
-        for a in range(2):
-            w4_raw[a, 1] = late_w4[:, a, :]
+        load_w4(1, "late_w4")
         load_wl(0)
+        gain_rows = held([P, P], F32, "gain_rows")
+        nc.gpsimd.memset(gain_rows[:], 0.0)
         for b in range(2):
             nc.sync.dma_start(
-                out=vec_rows[0][PACK * b : PACK * (b + 1), :],
+                out=gain_rows[PACK * b : PACK * (b + 1), :],
                 in_=gain[PASS * b : PASS * (b + 1)].rearrange("(g t i) -> t g i", t=PACK, i=RUN),
             )
-        load_wl(1)
 
         acc = {}
 
@@ -178,6 +186,8 @@ def tile_list_bell_discriminant_kernel(
         for number, part in enumerate(fronts + backs):
             first_product(part, 0, number)
         gather_words(1, (BANK, HALF, HALF))
+        wl_raw[1] = held([P, PACK, N], F32, "window1")
+        load_wl(1)
         for part in fronts:
             first_product(part, 1)
             empty(part, nc.scalar.copy)
@@ -192,7 +202,7 @@ def tile_list_bell_discriminant_kernel(
             empty(part, copy)
 
         h_half(3, 1, 0, nc.vector.tensor_copy)
-        turn(vec_rows[0], 0, gain_sb, nc.vector.tensor_copy)
+        turn(gain_rows, 0, gain_sb, nc.vector.tensor_copy)
 
         def rows_view(ap):
             return ap.rearrange("p t (c i) -> p c t i", i=2)

@@ -24,7 +24,7 @@ BANK = 512
 RUN = 8
 PER_COLUMN = 16
 BLOCKS = 16
-ROW0 = (48, 112)
+ROW0 = (96, 112)
 SLICES = H // P
 N_TILES = N // P
 HALF = M // 2
@@ -55,13 +55,13 @@ def tile_list_bell_discriminant_kernel(
         hum_list, prime_list, tierce_list = pos_sb
 
         tab_sc = held([P, T], U8, "tab_sc")
-        picked_sc = held([P, S], U8, "picked_sc")
+        picked_sc = held([P, S], U8, "window1")
         w4_sc_raw = held([P, H // 4], I32, "w4_sc_raw")
         staged = held([P, (S + H) // 4], I32, "staged")
         planes = {0: held([P, S + H], U8, "planes0")}
         w4_raw = {}
         w4_wd = {}
-        tab_wd = [held([P, T], I32, "window%d" % a) for a in range(2)]
+        tab_wd = {0: held([P, T], I32, "window0")}
         v_wd = [[held([P, BANK], U32, "v_wd%d%d" % (a, u)) for u in range(2)] for a in range(2)]
         cut_rows = held([P, P], F32, "cut_rows")
         ident = held([P, P], F32, "ident")
@@ -71,10 +71,9 @@ def tile_list_bell_discriminant_kernel(
         wl_sc = held([P, 2 * N], U8, "wl_sc")
         h_sb = [held([P, S], F32, "h_sb%d" % s) for s in range(SLICES)]
 
-        for a in range(2):
-            nc.vector.memset(tab_sc[64 * a : ROW0[a], :].bitcast(I32), 0)
-            nc.vector.memset(w4_sc_raw[64 * a : ROW0[a], :], 0)
-        nc.vector.memset(planes[0][:].bitcast(I32), 0)
+        nc.vector.memset(tab_sc[: ROW0[0], :].bitcast(I32), 0)
+        nc.vector.memset(w4_sc_raw[: ROW0[0], :], 0)
+        nc.gpsimd.memset(planes[0][:].bitcast(I32), 0)
         for rows in (slice(0, CUT0), slice(32, 64), slice(64, P)):
             nc.gpsimd.memset(cut_rows[rows, :], 0.0)
         make_identity(nc, ident[:])
@@ -89,17 +88,15 @@ def tile_list_bell_discriminant_kernel(
         nc.scalar.dma_start(out=cut_rows[CUT0:32, :], in_=cut.rearrange("(c p) -> c p", p=P))
         nc.sync.dma_start(offs_sb[:], offs)
         for dst, src in ((tab_sc[:].bitcast(I32), tab_scales), (w4_sc_raw[:], w4_scales)):
-            for a in range(2):
-                nc.sync.dma_start(out=dst[ROW0[a] : ROW0[a] + BLOCKS, :], in_=src[a].bitcast(I32))
-        load_w4(0, "early_w4")
+            nc.sync.dma_start(out=dst[ROW0[0] :, :], in_=src.rearrange("a q c -> (a q) c").bitcast(I32))
 
         def load_table(a):
             nc.sync.dma_start(out=tab_wd[a][:], in_=tab_words[a].rearrange("p t i -> p (t i)").bitcast(I32))
 
-        load_table(0)
-        load_table(1)
         for list_sb, src in zip(pos_sb, (pos1, pos2, pos3)):
             nc.sync.dma_start(list_sb[:], src)
+        load_table(0)
+        load_w4(0, "early_w4")
 
         def turn(rows, row0, cols, copy):
             turned = bank(7, P)
@@ -137,9 +134,11 @@ def tile_list_bell_discriminant_kernel(
         order_w4(0, 0, PACK, nc.gpsimd)
         order_w4(1, 0, PACK, nc.gpsimd)
         for a in range(2):
+            if a == 1:
+                tab_wd[1] = held([P, T], I32, "window1")
+                load_table(1)
             for y in range(4):
-                queue = (nc.scalar, nc.sync)[a]
-                queue.dma_start(
+                nc.sync.dma_start(
                     out=planes[a][y:P:32, :].bitcast(I32), in_=staged[ROW0[a] + y : ROW0[a] + BLOCKS : 4, :]
                 )
         gather_words(0, (BANK, BANK))

@@ -28,7 +28,15 @@ ROW0 = (96, 112)
 SLICES = H // P
 N_TILES = N // P
 HALF = M // 2
-PLACES = {"window0": 0, "wl_raw0": 0, "late_w4": 8192, "gain_rows": 12288}
+PLACES = {
+    "window0": 0,
+    "wl_raw0": 0,
+    "gain_rows": 8192,
+    "wl_raw1": 10240,
+    "late_w4": 18432,
+    "picked_sc": 19968,
+    "window1": 20480,
+}
 CUT0 = 32 - N_TILES
 
 
@@ -55,10 +63,10 @@ def tile_list_bell_discriminant_kernel(
         hum_list, prime_list, tierce_list = pos_sb
 
         tab_sc = held([P, T], U8, "tab_sc")
-        picked_sc = held([P, S], U8, "window1")
+        picked_sc = held([P, S], U8, "picked_sc")
         w4_sc_raw = held([P, H // 4], I32, "w4_sc_raw")
         staged = held([P, (S + H) // 4], I32, "staged")
-        planes = {0: held([P, S + H], U8, "planes0")}
+        planes = [held([P, S + H], U8, "planes%d" % a) for a in range(2)]
         w4_raw = {}
         w4_wd = {}
         tab_wd = {0: held([P, T], I32, "window0")}
@@ -67,13 +75,14 @@ def tile_list_bell_discriminant_kernel(
         ident = held([P, P], F32, "ident")
         gain_sb = held([P, SLICES], F32, "gain_sb")
         cut_sb = held([P, N_TILES], F32, "cut_sb")
-        wl_parts = (slice(0, N), slice(N, N + P), slice(N + P, 2 * N))
+        wl_parts = (slice(0, N), slice(N, 2 * N))
         wl_sc = held([P, 2 * N], U8, "wl_sc")
         h_sb = [held([P, S], F32, "h_sb%d" % s) for s in range(SLICES)]
 
         nc.vector.memset(tab_sc[: ROW0[0], :].bitcast(I32), 0)
         nc.vector.memset(w4_sc_raw[: ROW0[0], :], 0)
-        nc.gpsimd.memset(planes[0][:].bitcast(I32), 0)
+        for a in range(2):
+            nc.gpsimd.memset(planes[a][:].bitcast(I32), 0)
         for rows in (slice(0, CUT0), slice(32, 64), slice(64, P)):
             nc.gpsimd.memset(cut_rows[rows, :], 0.0)
         make_identity(nc, ident[:])
@@ -129,8 +138,6 @@ def tile_list_bell_discriminant_kernel(
         )
         nc.vector.tensor_copy(picked_sc[:], tab_sc[:].indirect(offs_sb[:]))
         nc.vector.tensor_copy(out=staged[:, : S // 4], in_=picked_sc[:].bitcast(I32))
-        planes[1] = held([P, S + H], U8, "tab_sc")
-        nc.vector.memset(planes[1][:].bitcast(I32), 0)
         order_w4(0, 0, PACK, nc.gpsimd)
         order_w4(1, 0, PACK, nc.gpsimd)
         for a in range(2):
@@ -142,7 +149,7 @@ def tile_list_bell_discriminant_kernel(
                     out=planes[a][y:P:32, :].bitcast(I32), in_=staged[ROW0[a] + y : ROW0[a] + BLOCKS : 4, :]
                 )
         gather_words(0, (BANK, BANK))
-        wl_raw = {0: held([P, PACK, N], F32, "wl_raw0")}
+        wl_raw = [held([P, PACK, N], F32, "wl_raw%d" % b) for b in range(2)]
 
         def load_wl(b):
             rows = wl[PASS * b : PASS * (b + 1), :].rearrange("(g t i) n -> t g i n", t=PACK, i=RUN)
@@ -158,22 +165,25 @@ def tile_list_bell_discriminant_kernel(
                 out=gain_rows[PACK * b : PACK * (b + 1), :],
                 in_=gain[PASS * b : PASS * (b + 1)].rearrange("(g t i) -> t g i", t=PACK, i=RUN),
             )
+        load_wl(1)
 
         acc = {}
 
-        def first_product(part, a, number=None):
-            s, j0, width = part
+        def first_product(part, a, number=None, piece=None):
+            s, part0, whole_width = part
+            first, width = piece or (0, whole_width)
+            j0 = part0 + first
             u, lo = divmod(j0, BANK)
             if a == 0:
                 acc[part] = bank(number, width)
             nc.tensor.matmul_mx(
-                out=acc[part][:],
+                out=acc[part][:, first : first + width],
                 lhsT=w4_wd[a, s].bitcast(FP4X4),
                 lhsT_scale=planes[a][:, S + P * s : S + P * (s + 1)],
                 rhs=v_wd[a][u][:, lo : lo + width].bitcast(FP8X4),
                 rhs_scale=planes[a][:, j0 : j0 + width],
                 start=(a == 0),
-                stop=(a == 1),
+                stop=(a == 1 and first + width == whole_width),
             )
 
         def empty(part, copy):
@@ -184,11 +194,11 @@ def tile_list_bell_discriminant_kernel(
         backs = [(0, BANK, HALF), (0, BANK + HALF, HALF), (1, BANK, BANK), (2, BANK, BANK), (3, 0, BANK)]
         for number, part in enumerate(fronts + backs):
             first_product(part, 0, number)
-        gather_words(1, (BANK, HALF, HALF))
-        wl_raw[1] = held([P, PACK, N], F32, "window1")
-        load_wl(1)
+        gather_words(1, (HALF, HALF, HALF, HALF))
         for part in fronts:
-            first_product(part, 1)
+            first_product(part, 1, piece=(0, HALF))
+        for part in fronts:
+            first_product(part, 1, piece=(HALF, HALF))
             empty(part, nc.scalar.copy)
         for part in backs:
             first_product(part, 1)
@@ -245,15 +255,12 @@ def tile_list_bell_discriminant_kernel(
 
         wl_bf = {}
 
-        def cast_wl(k, name, on_vector=False):
+        def cast_wl(k, name):
             b, n0 = divmod(wl_parts[k].start, N)
             width = width_of(wl_parts[k])
             wl_bf[k] = held([P, width, PACK], BF16, name)
             rows = wl_raw[b][:, :, n0 : n0 + width]
-            if on_vector:
-                nc.vector.tensor_copy(out=words_view(wl_bf[k][:]), in_=rows_view(rows))
-            else:
-                nc.gpsimd.tensor_scalar(wl_bf[k][:], in_turn(rows), 1.0, 0.0, ALU.mult, ALU.add)
+            nc.gpsimd.tensor_scalar(wl_bf[k][:], in_turn(rows), 1.0, 0.0, ALU.mult, ALU.add)
 
         def tierces_of(slices, names):
             return {s: pick(name, s, tierce_list, whole, on_vector=True) for s, name in zip(slices, names)}
@@ -327,7 +334,6 @@ def tile_list_bell_discriminant_kernel(
         h_half(7, 1, 7, nc.vector.tensor_copy)
         tierce.update(tierces_of((6, 7), ("tierce2", "gain_rows")))
         combine(4, tierce[4])
-        cast_wl(2, "squares0", on_vector=True)
         wl_wd = held([P, 2 * N], U32, "crosses0")
         combine(5, tierce[5])
         for k, part in enumerate(wl_parts):

@@ -328,9 +328,10 @@ def tile_list_bell_discriminant_kernel(
             rows = out[P * c0 : P * (c0 + result.shape[1]), chunks[j]]
             nc.sync.dma_start(out=rows.rearrange("(c p) m -> p c m", p=P), in_=result[:])
 
-        for number, (s, u) in zip((1, 2, 3, 4, 5, 6, 0), ((s, u) for s in range(PACK, SLICES) for u in range(2))):
+        for number, (s, u) in zip((1, 2, 3, 4, 5, 6), ((s, u) for s in range(PACK, SLICES) for u in range(2))):
             h_half(s, u, number, nc.scalar.copy)
         tierce = tierces_of((4, 5), ("prime2", "prime3"))
+        h_half(7, 0, 0, nc.vector.tensor_copy)
         h_half(7, 1, 7, nc.vector.tensor_copy)
         tierce.update(tierces_of((6, 7), ("tierce2", "gain_rows")))
         combine(4, tierce[4])

@@ -34,7 +34,8 @@ PLACES = {
     "gain_rows": 8192,
     "wl_raw1": 10240,
     "late_w4": 18432,
-    "picked_sc": 19968,
+    "w4_sc_raw": 19968,
+    "picked_sc": 20992,
     "window1": 20480,
 }
 CUT0 = 32 - N_TILES
@@ -95,9 +96,13 @@ def tile_list_bell_discriminant_kernel(
                 w4_raw[a, b] = both[:, a, :]
 
         nc.scalar.dma_start(out=cut_rows[CUT0:32, :], in_=cut.rearrange("(c p) -> c p", p=P))
-        nc.sync.dma_start(offs_sb[:], offs)
-        for dst, src in ((tab_sc[:].bitcast(I32), tab_scales), (w4_sc_raw[:], w4_scales)):
+
+        def load_scale_rows(dst, src):
             nc.sync.dma_start(out=dst[ROW0[0] :, :], in_=src.rearrange("a q c -> (a q) c").bitcast(I32))
+
+        load_scale_rows(tab_sc[:].bitcast(I32), tab_scales)
+        nc.sync.dma_start(offs_sb[:], offs)
+        load_scale_rows(w4_sc_raw[:], w4_scales)
 
         def load_table(a):
             nc.sync.dma_start(out=tab_wd[a][:], in_=tab_words[a].rearrange("p t i -> p (t i)").bitcast(I32))
@@ -132,7 +137,7 @@ def tile_list_bell_discriminant_kernel(
                 nc.vector.tensor_copy(v_wd[a][u][:, lo : lo + width], tab_wd[a][:].bitcast(U32).indirect(entries))
                 j0 = j0 + width
 
-        nc.vector.tensor_copy(
+        nc.gpsimd.tensor_copy(
             out=staged[:, S // 4 :].rearrange("p (b t g w) -> p b t g w", b=2, t=PACK, w=2),
             in_=w4_sc_raw[:].rearrange("p (b g t w) -> p b t g w", b=2, t=PACK, w=2),
         )
@@ -195,9 +200,10 @@ def tile_list_bell_discriminant_kernel(
         for number, part in enumerate(fronts + backs):
             first_product(part, 0, number)
         gather_words(1, (HALF, HALF, HALF, HALF))
-        for part in fronts:
-            first_product(part, 1, piece=(0, HALF))
-        for part in fronts:
+        first_product(fronts[0], 1, piece=(0, HALF))
+        for part, ahead in zip(fronts, fronts[1:] + [None]):
+            if ahead:
+                first_product(ahead, 1, piece=(0, HALF))
             first_product(part, 1, piece=(HALF, HALF))
             empty(part, nc.scalar.copy)
         for part in backs:
@@ -350,7 +356,9 @@ def tile_list_bell_discriminant_kernel(
                 hum[s, cols.start] = pick("hum%d_%d" % (s, cols.start), s, hum_list, cols)
 
         def cross(s, cols):
-            product(crosses[1][:, s - PACK, cols], prime[s, cols.start][:], tierce[s][:, cols], s)
+            first = cols.start - cols.start % HALF
+            picked = prime[s, first][:, cols.start - first : cols.stop - first]
+            product(crosses[1][:, s - PACK, cols], picked, tierce[s][:, cols], s)
 
         def square(s, cols):
             product(squares[1][:, s - PACK, cols], hum[s, cols.start][:], hum[s, cols.start][:], s)
@@ -364,26 +372,28 @@ def tile_list_bell_discriminant_kernel(
         quantize_z(0, 1, z0[:, chunks[1], :], "z_wd01")
         second_product(0, 1)
         z = difference(nc.vector, "z10", squares[1], crosses[1], front)
-        cross(6, back)
+        cross(6, chunks[1])
+        cross(7, chunks[1])
         quantize_z(1, 0, z[:], "z_wd10")
         second_product(1, 0)
-        cross(7, back)
         square(6, chunks[1])
         square(7, chunks[1])
+        cross(6, chunks[2])
         for c in range(N_TILES):
             add_cut(0, c, c - c % 2, 2, False)
             if c % 2 == 1:
                 store(0, c - 1)
         z = difference(nc.vector, "z11", squares[1], crosses[1], chunks[1])
-        square(6, chunks[2])
-        square(7, chunks[2])
+        cross(7, chunks[2])
         quantize_z(1, 1, z[:], "z_wd11")
         second_product(1, 1)
+        square(6, chunks[2])
+        square(7, chunks[2])
         quantize_z(0, 2, z0[:, chunks[2], :], "hum7_256")
         second_product(0, 2)
         z = difference(nc.vector, "z12", squares[1], crosses[1], chunks[2])
         for c in range(N_TILES):
-            add_cut(1, c, 0, N_TILES, False)
+            add_cut(1, c, 0, N_TILES, c == N_TILES - 1)
         store(1, 0)
         quantize_z(1, 2, z[:], "z_wd12")
         second_product(1, 2)

@@ -29,14 +29,15 @@ SLICES = H // P
 N_TILES = N // P
 HALF = M // 2
 PLACES = {
-    "window0": 0,
-    "wl_raw0": 0,
-    "gain_rows": 8192,
-    "wl_raw1": 10240,
-    "late_w4": 18432,
-    "w4_sc_raw": 19968,
-    "picked_sc": 20992,
-    "window1": 20480,
+    "window0": 8192,
+    "wl_raw0": 8192,
+    "crosses0": 4096,
+    "squares0": 12288,
+    "wl_raw1": 20480,
+    "late_w4": 28672,
+    "w4_sc_raw": 30208,
+    "window1": 30720,
+    "picked_sc": 31232,
 }
 CUT0 = 32 - N_TILES
 
@@ -111,6 +112,8 @@ def tile_list_bell_discriminant_kernel(
             nc.sync.dma_start(list_sb[:], src)
         load_table(0)
         load_w4(0, "early_w4")
+        gain_raw = held([2, PASS], F32, "gain_raw")
+        nc.sync.dma_start(out=gain_raw[:], in_=gain.rearrange("(b r) -> b r", b=2))
 
         def turn(rows, row0, cols, copy):
             turned = bank(7, P)
@@ -118,6 +121,18 @@ def tile_list_bell_discriminant_kernel(
             copy(out=cols[:], in_=turned[:, row0 : row0 + cols.shape[1]])
 
         turn(cut_rows, CUT0, cut_sb, nc.scalar.copy)
+        gain_rows = held([P, PACK, P], F32, "gain_rows")
+        nc.gpsimd.memset(gain_rows[:], 0.0)
+        nc.gpsimd.tensor_copy(
+            out=gain_rows[:2].rearrange("b t (g i) -> b t g i", i=RUN),
+            in_=gain_raw[:2, :].rearrange("b (g t i) -> b t g i", t=PACK, i=RUN),
+        )
+        turned_gain = psum.tile([P, PACK, P], F32, name="bank6")
+        for t in range(PACK):
+            nc.tensor.transpose(turned_gain[:, t, :], gain_rows[:, t, :], ident[:])
+        nc.scalar.copy(
+            out=gain_sb[:].rearrange("p (b t) -> p b t", b=2), in_=turned_gain[:, :, :2].rearrange("p t b -> p b t")
+        )
 
         def order_w4(a, s0, count, engine):
             b, t0 = divmod(s0, PACK)
@@ -163,13 +178,6 @@ def tile_list_bell_discriminant_kernel(
 
         load_w4(1, "late_w4")
         load_wl(0)
-        gain_rows = held([P, P], F32, "gain_rows")
-        nc.gpsimd.memset(gain_rows[:], 0.0)
-        for b in range(2):
-            nc.sync.dma_start(
-                out=gain_rows[PACK * b : PACK * (b + 1), :],
-                in_=gain[PASS * b : PASS * (b + 1)].rearrange("(g t i) -> t g i", t=PACK, i=RUN),
-            )
         load_wl(1)
 
         acc = {}
@@ -217,7 +225,6 @@ def tile_list_bell_discriminant_kernel(
             empty(part, copy)
 
         h_half(3, 1, 0, nc.vector.tensor_copy)
-        turn(gain_rows, 0, gain_sb, nc.vector.tensor_copy)
 
         def rows_view(ap):
             return ap.rearrange("p t (c i) -> p c t i", i=2)
@@ -284,7 +291,8 @@ def tile_list_bell_discriminant_kernel(
             order_w4(a, PACK, PACK, nc.gpsimd)
         cast_wl(0, "wl_bf0")
         cast_wl(1, "wl_bf1")
-        tierce = tierces_of(range(PACK), ("tierce0", "tierce1", "tierce2", "gain_rows"))
+        h_half(4, 0, 1, nc.vector.tensor_copy)
+        tierce = tierces_of(range(PACK), ("tierce0", "tierce1", "tierce2", "tierce3"))
         for s in range(PACK):
             combine(s, tierce[s])
         z0 = difference(nc.gpsimd, "z0", squares[0], crosses[0], whole)
@@ -334,12 +342,11 @@ def tile_list_bell_discriminant_kernel(
             rows = out[P * c0 : P * (c0 + result.shape[1]), chunks[j]]
             nc.sync.dma_start(out=rows.rearrange("(c p) m -> p c m", p=P), in_=result[:])
 
-        for number, (s, u) in zip((1, 2, 3, 4, 5, 6), ((s, u) for s in range(PACK, SLICES) for u in range(2))):
+        for number, (s, u) in zip((2, 3, 4, 5, 6, 0), ((4, 1), (5, 0), (5, 1), (6, 0), (6, 1), (7, 0))):
             h_half(s, u, number, nc.scalar.copy)
         tierce = tierces_of((4, 5), ("prime2", "prime3"))
-        h_half(7, 0, 0, nc.vector.tensor_copy)
         h_half(7, 1, 7, nc.vector.tensor_copy)
-        tierce.update(tierces_of((6, 7), ("tierce2", "gain_rows")))
+        tierce.update(tierces_of((6, 7), ("tierce2", "tierce3")))
         combine(4, tierce[4])
         wl_wd = held([P, 2 * N], U32, "crosses0")
         combine(5, tierce[5])

@@ -30,10 +30,11 @@ N_TILES = N // P
 HALF = M // 2
 PLACES = {
     "window0": 8192,
-    "wl_raw0": 8192,
+    "wl_raw0": 16384,
+    "wl_raw1": 10240,
     "crosses0": 4096,
     "squares0": 12288,
-    "wl_raw1": 20480,
+    "wl_raw2": 20480,
     "late_w4": 28672,
     "w4_sc_raw": 30208,
     "window1": 30720,
@@ -77,7 +78,7 @@ def tile_list_bell_discriminant_kernel(
         ident = held([P, P], F32, "ident")
         gain_sb = held([P, SLICES], F32, "gain_sb")
         cut_sb = held([P, N_TILES], F32, "cut_sb")
-        wl_parts = (slice(0, N), slice(N, 2 * N))
+        wl_parts = (slice(0, N // 2), slice(N // 2, N), slice(N, 2 * N))
         wl_sc = held([P, 2 * N], U8, "wl_sc")
         h_sb = [held([P, S], F32, "h_sb%d" % s) for s in range(SLICES)]
 
@@ -169,16 +170,18 @@ def tile_list_bell_discriminant_kernel(
                     out=planes[a][y:P:32, :].bitcast(I32), in_=staged[ROW0[a] + y : ROW0[a] + BLOCKS : 4, :]
                 )
         gather_words(0, (BANK, BANK))
-        wl_raw = [held([P, PACK, N], F32, "wl_raw%d" % b) for b in range(2)]
+        wl_raw = [held([P, PACK, part.stop - part.start], F32, "wl_raw%d" % k) for k, part in enumerate(wl_parts)]
 
-        def load_wl(b):
-            rows = wl[PASS * b : PASS * (b + 1), :].rearrange("(g t i) n -> t g i n", t=PACK, i=RUN)
+        def load_wl(k):
+            b, n0 = divmod(wl_parts[k].start, N)
+            block = wl[PASS * b : PASS * (b + 1), n0 : n0 + wl_raw[k].shape[2]]
+            rows = block.rearrange("(g t i) n -> t g i n", t=PACK, i=RUN)
             for t in range(PACK):
-                nc.sync.dma_start(out=wl_raw[b][:, t, :], in_=rows[t])
+                nc.sync.dma_start(out=wl_raw[k][:, t, :], in_=rows[t])
 
         load_w4(1, "late_w4")
-        load_wl(0)
-        load_wl(1)
+        for k in range(len(wl_parts)):
+            load_wl(k)
 
         acc = {}
 
@@ -266,14 +269,7 @@ def tile_list_bell_discriminant_kernel(
         front, back = slice(0, HALF), slice(HALF, M)
         chunks = (front, slice(HALF, HALF + P), slice(HALF + P, M))
 
-        wl_bf = {}
-
-        def cast_wl(k, name):
-            b, n0 = divmod(wl_parts[k].start, N)
-            width = width_of(wl_parts[k])
-            wl_bf[k] = held([P, width, PACK], BF16, name)
-            rows = wl_raw[b][:, :, n0 : n0 + width]
-            nc.gpsimd.tensor_scalar(wl_bf[k][:], in_turn(rows), 1.0, 0.0, ALU.mult, ALU.add)
+        wl_bf = held([P, 2 * N, PACK], BF16, "wl_bf")
 
         def tierces_of(slices, names):
             return {s: pick(name, s, tierce_list, whole, on_vector=True) for s, name in zip(slices, names)}
@@ -289,8 +285,8 @@ def tile_list_bell_discriminant_kernel(
         crosses = [held([P, PACK, M], F32, "crosses%d" % b) for b in range(2)]
         for a in range(2):
             order_w4(a, PACK, PACK, nc.gpsimd)
-        cast_wl(0, "wl_bf0")
-        cast_wl(1, "wl_bf1")
+        for part, rows in zip(wl_parts, wl_raw):
+            nc.gpsimd.tensor_scalar(wl_bf[:, part, :], in_turn(rows[:]), 1.0, 0.0, ALU.mult, ALU.add)
         h_half(4, 0, 1, nc.vector.tensor_copy)
         tierce = tierces_of(range(PACK), ("tierce0", "tierce1", "tierce2", "tierce3"))
         for s in range(PACK):
@@ -350,8 +346,7 @@ def tile_list_bell_discriminant_kernel(
         combine(4, tierce[4])
         wl_wd = held([P, 2 * N], U32, "crosses0")
         combine(5, tierce[5])
-        for k, part in enumerate(wl_parts):
-            quantize(wl_bf[k][:], wl_wd[:, part], wl_sc[:, part])
+        quantize(wl_bf[:], wl_wd[:], wl_sc[:])
         prime, hum = {}, {}
         for s in (6, 7):
             prime[s, 0] = pick("prime%d_0" % s, s, prime_list, front)

from contextlib import ExitStack

import concourse.mybir as mybir
from concourse.masks import make_identity

K, H, N, T, S, M = 1024, 1024, 512, 4096, 1024, 512
FLOPS = 2 * K * H * S + 2 * H * N * M

F32 = mybir.dt.float32
BF16 = mybir.dt.bfloat16
I32 = mybir.dt.int32
U32 = mybir.dt.uint32
U16 = mybir.dt.uint16
U8 = mybir.dt.uint8
FP8X4 = mybir.dt.float8_e4m3fn_x4
FP4X4 = mybir.dt.float4_e2m1fn_x4
ACT = mybir.ActivationFunctionType
ALU = mybir.AluOpType

P = 128
PACK = 4
PASS = P * PACK
BANK = 512
RUN = 8
PER_COLUMN = 16
BLOCKS = 16
ROW0 = (96, 112)
SLICES = H // P
N_TILES = N // P
HALF = M // 2
PLACES = {
    "window0": 8192,
    "wl_raw0": 16384,
    "wl_raw1": 10240,
    "crosses0": 4096,
    "squares0": 12288,
    "wl_raw2": 20480,
    "late_w4": 28672,
    "w4_sc_raw": 30208,
    "window1": 30720,
    "picked_sc": 31232,
}
CUT0 = 32 - N_TILES


def tile_list_bell_discriminant_kernel(
    tc, tab_words, tab_scales, offs, w4_words, w4_scales, pos1, pos2, pos3, gain, wl, cut, out
):
    nc = tc.nc
    with ExitStack() as ctx:
        lists = ctx.enter_context(tc.tile_pool(name="lists", bufs=1))
        keep = ctx.enter_context(tc.tile_pool(name="keep", bufs=1))
        reuse = ctx.enter_context(tc.tile_pool(name="reuse", bufs=1))
        psum = ctx.enter_context(tc.psum_pool(name="psum", bufs=1))

        def held(shape, dtype, name):
            if name in PLACES:
                return reuse.tile(shape, dtype, name=name, align_bytes=64, offset=PLACES[name])
            return keep.tile(shape, dtype, name=name, align_bytes=64)

        def bank(number, width):
            return psum.tile([P, width], F32, name="bank%d" % number)

        offs_sb = lists.tile([P, S // PER_COLUMN], U16, name="offs_sb")
        pos_sb = [lists.tile([P, M // PER_COLUMN], U16, name="pos_sb%d" % i) for i in range(3)]
        hum_list, prime_list, tierce_list = pos_sb

        tab_sc = held([P, T], U8, "tab_sc")
        picked_sc = held([P, S], U8, "picked_sc")
        w4_sc_raw = held([P, H // 4], I32, "w4_sc_raw")
        staged = held([P, (S + H) // 4], I32, "staged")
        planes = [held([P, S + H], U8, "planes%d" % a) for a in range(2)]
        w4_raw = {}
        w4_wd = {}
        tab_wd = {0: held([P, T], I32, "window0")}
        v_wd = [[held([P, BANK], U32, "v_wd%d%d" % (a, u)) for u in range(2)] for a in range(2)]
        cut_rows = held([P, P], F32, "cut_rows")
        ident = held([P, P], F32, "ident")
        gain_sb = held([P, SLICES], F32, "gain_sb")
        cut_sb = held([P, N_TILES], F32, "cut_sb")
        wl_parts = (slice(0, N // 2), slice(N // 2, N), slice(N, 2 * N))
        wl_sc = held([P, 2 * N], U8, "wl_sc")
        h_sb = [held([P, S], F32, "h_sb%d" % s) for s in range(SLICES)]

        nc.vector.memset(tab_sc[: ROW0[0], :].bitcast(I32), 0)
        nc.vector.memset(w4_sc_raw[: ROW0[0], :], 0)
        for a in range(2):
            nc.gpsimd.memset(planes[a][:].bitcast(I32), 0)
        for rows in (slice(0, CUT0), slice(32, 64), slice(64, P)):
            nc.gpsimd.memset(cut_rows[rows, :], 0.0)
        make_identity(nc, ident[:])

        def load_w4(b, name):
            both = held([P, 2, PASS // 2], I32, name)
            cols = w4_words[:, :, 2 * PASS * b : 2 * PASS * (b + 1)]
            nc.sync.dma_start(out=both[:], in_=cols.bitcast(I32).rearrange("a p w -> p a w"))
            for a in range(2):
                w4_raw[a, b] = both[:, a, :]

        nc.scalar.dma_start(out=cut_rows[CUT0:32, :], in_=cut.rearrange("(c p) -> c p", p=P))

        def load_scale_rows(dst, src):
            nc.sync.dma_start(out=dst[ROW0[0] :, :], in_=src.rearrange("a q c -> (a q) c").bitcast(I32))

        load_scale_rows(tab_sc[:].bitcast(I32), tab_scales)
        nc.sync.dma_start(offs_sb[:], offs)
        load_scale_rows(w4_sc_raw[:], w4_scales)

        def load_table(a):
            nc.sync.dma_start(out=tab_wd[a][:], in_=tab_words[a].rearrange("p t i -> p (t i)").bitcast(I32))

        for list_sb, src in zip(pos_sb, (pos1, pos2, pos3)):
            nc.sync.dma_start(list_sb[:], src)
        load_table(0)
        load_w4(0, "early_w4")
        gain_raw = held([2, PASS], F32, "gain_raw")
        nc.sync.dma_start(out=gain_raw[:], in_=gain.rearrange("(b r) -> b r", b=2))

        def turn(rows, row0, cols, copy):
            turned = bank(7, P)
            nc.tensor.transpose(turned[:], rows[:], ident[:])
            copy(out=cols[:], in_=turned[:, row0 : row0 + cols.shape[1]])

        turn(cut_rows, CUT0, cut_sb, nc.scalar.copy)
        gain_rows = held([P, PACK, P], F32, "gain_rows")
        nc.gpsimd.memset(gain_rows[:], 0.0)
        nc.gpsimd.tensor_copy(
            out=gain_rows[:2].rearrange("b t (g i) -> b t g i", i=RUN),
            in_=gain_raw[:2, :].rearrange("b (g t i) -> b t g i", t=PACK, i=RUN),
        )
        turned_gain = psum.tile([P, PACK, P], F32, name="bank6")
        for t in range(PACK):
            nc.tensor.transpose(turned_gain[:, t, :], gain_rows[:, t, :], ident[:])
        nc.scalar.copy(
            out=gain_sb[:].rearrange("p (b t) -> p b t", b=2), in_=turned_gain[:, :, :2].rearrange("p t b -> p b t")
        )

        def order_w4(a, s0, count, engine):
            b, t0 = divmod(s0, PACK)
            ordered = held([P, count, 2 * P], U8, "w4_wd%d%d" % (a, s0))
            engine.tensor_copy(
                out=ordered[:].bitcast(I32).rearrange("p t (g w) -> p t g w", w=4),
                in_=w4_raw[a, b].rearrange("p (g t w) -> p t g w", t=PACK, w=4)[:, t0 : t0 + count],
            )
            for t in range(count):
                w4_wd[a, s0 + t] = ordered[:, t, :]

        def gather_words(a, widths):
            j0 = 0
            for width in widths:
                u, lo = divmod(j0, BANK)
                entries = offs_sb[:, j0 // PER_COLUMN : (j0 + width) // PER_COLUMN]
                nc.vector.tensor_copy(v_wd[a][u][:, lo : lo + width], tab_wd[a][:].bitcast(U32).indirect(entries))
                j0 = j0 + width

        nc.gpsimd.tensor_copy(
            out=staged[:, S // 4 :].rearrange("p (b t g w) -> p b t g w", b=2, t=PACK, w=2),
            in_=w4_sc_raw[:].rearrange("p (b g t w) -> p b t g w", b=2, t=PACK, w=2),
        )
        nc.vector.tensor_copy(picked_sc[:], tab_sc[:].indirect(offs_sb[:]))
        nc.vector.tensor_copy(out=staged[:, : S // 4], in_=picked_sc[:].bitcast(I32))
        order_w4(0, 0, PACK, nc.gpsimd)
        order_w4(1, 0, PACK, nc.gpsimd)
        for a in range(2):
            if a == 1:
                tab_wd[1] = held([P, T], I32, "window1")
                load_table(1)
            for y in range(4):
                nc.sync.dma_start(
                    out=planes[a][y:P:32, :].bitcast(I32), in_=staged[ROW0[a] + y : ROW0[a] + BLOCKS : 4, :]
                )
        gather_words(0, (BANK, BANK))
        wl_raw = [held([P, PACK, part.stop - part.start], F32, "wl_raw%d" % k) for k, part in enumerate(wl_parts)]

        def load_wl(k):
            b, n0 = divmod(wl_parts[k].start, N)
            block = wl[PASS * b : PASS * (b + 1), n0 : n0 + wl_raw[k].shape[2]]
            rows = block.rearrange("(g t i) n -> t g i n", t=PACK, i=RUN)
            for t in range(PACK):
                nc.sync.dma_start(out=wl_raw[k][:, t, :], in_=rows[t])

        load_w4(1, "late_w4")
        for k in range(len(wl_parts)):
            load_wl(k)

        acc = {}

        def first_product(part, a, number=None, piece=None):
            s, part0, whole_width = part
            first, width = piece or (0, whole_width)
            j0 = part0 + first
            u, lo = divmod(j0, BANK)
            if a == 0:
                acc[part] = bank(number, width)
            nc.tensor.matmul_mx(
                out=acc[part][:, first : first + width],
                lhsT=w4_wd[a, s].bitcast(FP4X4),
                lhsT_scale=planes[a][:, S + P * s : S + P * (s + 1)],
                rhs=v_wd[a][u][:, lo : lo + width].bitcast(FP8X4),
                rhs_scale=planes[a][:, j0 : j0 + width],
                start=(a == 0),
                stop=(a == 1 and first + width == whole_width),
            )

        def empty(part, copy):
            s, j0, width = part
            copy(out=h_sb[s][:, j0 : j0 + width], in_=acc[part][:])

        fronts = [(s, 0, BANK) for s in range(3)]
        backs = [(0, BANK, HALF), (0, BANK + HALF, HALF), (1, BANK, BANK), (2, BANK, BANK), (3, 0, BANK)]
        for number, part in enumerate(fronts + backs):
            first_product(part, 0, number)
        gather_words(1, (HALF, HALF, HALF, HALF))
        first_product(fronts[0], 1, piece=(0, HALF))
        for part, ahead in zip(fronts, fronts[1:] + [None]):
            if ahead:
                first_product(ahead, 1, piece=(0, HALF))
            first_product(part, 1, piece=(HALF, HALF))
            empty(part, nc.scalar.copy)
        for part in backs:
            first_product(part, 1)
            empty(part, nc.vector.tensor_copy)

        def h_half(s, u, number, copy):
            part = (s, BANK * u, BANK)
            first_product(part, 0, number)
            first_product(part, 1)
            empty(part, copy)

        h_half(3, 1, 0, nc.vector.tensor_copy)

        def rows_view(ap):
            return ap.rearrange("p t (c i) -> p c t i", i=2)

        def words_view(ap):
            return ap.rearrange("p (c i) t -> p c t i", i=2)

        def in_turn(ap):
            return ap.rearrange("p t m -> p m t")

        def quantize(grouped, codes, scales):
            nc.vector.quantize_mx(out=codes.bitcast(FP8X4), scales=scales, in_=grouped.rearrange("p m t -> p (m t)"))

        def width_of(cols):
            return cols.stop - cols.start

        def window(s, picks, cols):
            return h_sb[s][:].indirect(picks[:, cols.start // PER_COLUMN : cols.stop // PER_COLUMN])

        def pick(name, s, picks, cols, on_vector=False):
            picked = held([P, width_of(cols)], F32, name)
            if on_vector:
                nc.vector.tensor_copy(picked[:], window(s, picks, cols))
            else:
                nc.scalar.activation(picked[:], window(s, picks, cols), ACT.Copy)
            return picked

        def product(dst, left, right, s):
            nc.vector.scalar_tensor_tensor(dst, left, gain_sb[:, s : s + 1], right, ALU.mult, ALU.mult)

        def difference(engine, name, squares, crosses, cols):
            z = held([P, width_of(cols), PACK], BF16, name)
            engine.tensor_tensor(
                words_view(z[:]), rows_view(squares[:, :, cols]), rows_view(crosses[:, :, cols]), ALU.subtract
            )
            return z

        whole = slice(0, M)
        front, back = slice(0, HALF), slice(HALF, M)
        chunks = (front, slice(HALF, HALF + P), slice(HALF + P, M))

        wl_bf = held([P, 2 * N, PACK], BF16, "wl_bf")

        def tierces_of(slices, names):
            return {s: pick(name, s, tierce_list, whole, on_vector=True) for s, name in zip(slices, names)}

        def combine(s, tierce):
            b, t = divmod(s, PACK)
            prime = pick("prime%d" % s, s, prime_list, whole)
            hum = pick("hum%d" % s, s, hum_list, whole)
            product(crosses[b][:, t, :], prime[:], tierce[:], s)
            product(squares[b][:, t, :], hum[:], hum[:], s)

        squares = [held([P, PACK, M], F32, "squares%d" % b) for b in range(2)]
        crosses = [held([P, PACK, M], F32, "crosses%d" % b) for b in range(2)]
        for a in range(2):
            order_w4(a, PACK, PACK, nc.gpsimd)
        for part, rows in zip(wl_parts, wl_raw):
            nc.gpsimd.tensor_scalar(wl_bf[:, part, :], in_turn(rows[:]), 1.0, 0.0, ALU.mult, ALU.add)
        h_half(4, 0, 1, nc.vector.tensor_copy)
        tierce = tierces_of(range(PACK), ("tierce0", "tierce1", "tierce2", "tierce3"))
        for s in range(PACK):
            combine(s, tierce[s])
        z0 = difference(nc.gpsimd, "z0", squares[0], crosses[0], whole)

        z_wd, z_sc = {}, {}

        def quantize_z(b, j, z, name):
            width = width_of(chunks[j])
            z_wd[b, j], z_sc[b, j] = held([P, width], U32, name), held([P, width], U8, "z_sc%d%d" % (b, j))
            quantize(z, z_wd[b, j][:], z_sc[b, j][:])

        homes = (((1, (0, 1)), (2, (2, 3))), ((3, (0, 1, 2)), (4, (3,))), ((5, (0,)), (6, (1,)), (0, (2,)), (7, (3,))))
        sums = {}

        def second_product(b, j):
            width = width_of(chunks[j])
            for number, tiles in homes[j]:
                if b == 0:
                    group = bank(number, len(tiles) * width)
                    for lo, c in enumerate(tiles):
                        sums[j, c] = group[:, width * lo : width * (lo + 1)]
                for c in tiles:
                    cols = slice(N * b + P * c, N * b + P * (c + 1))
                    nc.tensor.matmul_mx(
                        out=sums[j, c],
                        lhsT=wl_wd[:, cols].bitcast(FP8X4),
                        lhsT_scale=wl_sc[:, cols],
                        rhs=z_wd[b, j][:].bitcast(FP8X4),
                        rhs_scale=z_sc[b, j][:],
                        start=(b == 0 and c == tiles[0]),
                        stop=(b == 1 and c == tiles[-1]),
                    )

        results = {}

        def add_cut(j, c, c0, count, on_vector):
            if (j, c0) not in results:
                results[j, c0] = held([P, count, width_of(chunks[j])], F32, "result%d%d" % (j, c0))
            dst, bias = results[j, c0][:, c - c0, :], cut_sb[:, c : c + 1]
            if on_vector:
                nc.vector.tensor_scalar(dst, sums[j, c], bias, None, ALU.add)
            else:
                nc.scalar.activation(out=dst, in_=sums[j, c], func=ACT.Identity, bias=bias)

        def store(j, c0):
            result = results[j, c0]
            rows = out[P * c0 : P * (c0 + result.shape[1]), chunks[j]]
            nc.sync.dma_start(out=rows.rearrange("(c p) m -> p c m", p=P), in_=result[:])

        for number, (s, u) in zip((2, 3, 4, 5, 6, 0), ((4, 1), (5, 0), (5, 1), (6, 0), (6, 1), (7, 0))):
            h_half(s, u, number, nc.scalar.copy)
        tierce = tierces_of((4, 5), ("prime2", "prime3"))
        h_half(7, 1, 7, nc.vector.tensor_copy)
        tierce.update(tierces_of((6, 7), ("tierce2", "tierce3")))
        combine(4, tierce[4])
        wl_wd = held([P, 2 * N], U32, "crosses0")
        combine(5, tierce[5])
        quantize(wl_bf[:], wl_wd[:], wl_sc[:])
        prime, hum = {}, {}
        for s in (6, 7):
            prime[s, 0] = pick("prime%d_0" % s, s, prime_list, front)
            hum[s, 0] = pick("hum%d_0" % s, s, hum_list, front)
        for s in (6, 7):
            prime[s, HALF] = pick("prime%d_256" % s, s, prime_list, back)
        for cols in chunks[1:]:
            for s in (6, 7):
                hum[s, cols.start] = pick("hum%d_%d" % (s, cols.start), s, hum_list, cols)

        def cross(s, cols):
            first = cols.start - cols.start % HALF
            picked = prime[s, first][:, cols.start - first : cols.stop - first]
            product(crosses[1][:, s - PACK, cols], picked, tierce[s][:, cols], s)

        def square(s, cols):
            product(squares[1][:, s - PACK, cols], hum[s, cols.start][:], hum[s, cols.start][:], s)

        cross(6, front)
        square(6, front)
        quantize_z(0, 0, z0[:, chunks[0], :], "z_wd00")
        second_product(0, 0)
        cross(7, front)
        square(7, front)
        quantize_z(0, 1, z0[:, chunks[1], :], "z_wd01")
        second_product(0, 1)
        z = difference(nc.vector, "z10", squares[1], crosses[1], front)
        cross(6, chunks[1])
        cross(7, chunks[1])
        quantize_z(1, 0, z[:], "z_wd10")
        second_product(1, 0)
        square(6, chunks[1])
        square(7, chunks[1])
        cross(6, chunks[2])
        for c in range(N_TILES):
            add_cut(0, c, c - c % 2, 2, False)
            if c % 2 == 1:
                store(0, c - 1)
        z = difference(nc.vector, "z11", squares[1], crosses[1], chunks[1])
        cross(7, chunks[2])
        quantize_z(1, 1, z[:], "z_wd11")
        second_product(1, 1)
        square(6, chunks[2])
        square(7, chunks[2])
        quantize_z(0, 2, z0[:, chunks[2], :], "hum7_256")
        second_product(0, 2)
        z = difference(nc.vector, "z12", squares[1], crosses[1], chunks[2])
        for c in range(N_TILES):
            add_cut(1, c, 0, N_TILES, c == N_TILES - 1)
        store(1, 0)
        quantize_z(1, 2, z[:], "z_wd12")
        second_product(1, 2)
        for c in range(N_TILES):
            add_cut(2, c, c - c % 2, 2, c % 2 == 1)
            if c % 2 == 1:
                store(2, c - 1)
